import numpy as np
import ml_dtypes


def mxq(x, axis, fmt="e4m3"):
    dtype, down = {"e4m3": (ml_dtypes.float8_e4m3fn, 7), "e5m2": (ml_dtypes.float8_e5m2, 14)}[fmt]
    v = np.moveaxis(np.asarray(x, np.float32).astype(ml_dtypes.bfloat16).astype(np.float64), axis, -1)
    blocks = v.reshape(v.shape[:-1] + (-1, 32))
    amax = np.abs(blocks).max(-1, keepdims=True)
    byte = np.maximum(np.where(amax > 0, np.frexp(amax)[1] - 1 + 127, 0) - down, 1)
    scale = np.exp2(byte - 127.0)
    codes = (blocks / scale).astype(np.float32).astype(dtype).astype(np.float64)
    return np.moveaxis((codes * scale).reshape(v.shape), -1, axis)


WIDE = False


def mx_kscale(k):
    if not WIDE:
        return np.ones(k)
    levels = np.array([30, -30])
    if k % 512:
        return np.exp2(np.random.permutation(np.resize(levels, k // 32))).repeat(32)
    a = np.empty((k // 512, 16))
    for p in range(k // 512):
        a[p, :8] = np.random.permutation(np.resize(levels, 8))
        for g in range(8):
            far = levels[np.abs(levels - a[p, g]) >= 10]
            a[p, g + 8] = far[np.random.randint(len(far))]
    return np.exp2(a.ravel()).repeat(32)


def f64(x):
    return np.asarray(x).astype(np.float64)


def striped(idx):
    return np.tile(idx.reshape(-1, 16).T, (8, 1)).astype(np.uint16)


def unstriped(offs):
    return offs[:16].T.reshape(-1).astype(np.int64)


E2M1 = np.array([0.0, 0.5, 1.0, 1.5, 2.0, 3.0, 4.0, 6.0, -0.0, -0.5, -1.0, -1.5, -2.0, -3.0, -4.0, -6.0])


def pack_weight(w, fmt):
    k, n = w.shape
    w = f64(np.asarray(w, np.float32).astype(ml_dtypes.bfloat16)).reshape(k // 32, 32, n)
    amax = np.abs(w).max(1)
    if fmt == "e4m3":
        byte = np.frexp(amax)[1] - 1 + 127 - 7
    else:
        mant, ex = np.frexp(amax / 6.0)
        byte = np.where(mant > 0.5, ex, ex - 1) + 127
    byte = np.clip(np.where(amax > 0, byte, 1), 1, 254)
    scaled = (w * np.exp2(127.0 - byte)[:, None, :]).reshape(k, n).astype(np.float32)
    by_word = np.ascontiguousarray(scaled.reshape(k // 512, 128, 4, n).transpose(0, 1, 3, 2))
    if fmt == "e4m3":
        words = by_word.astype(ml_dtypes.float8_e4m3fn).view(np.uint8)
    else:
        c = by_word.astype(ml_dtypes.float4_e2m1fn).view(np.uint8) & 0xF
        words = (c[..., 0::2] | (c[..., 1::2] << 4)).reshape(k // 512, 128, 2 * n)
    return np.ascontiguousarray(words), np.ascontiguousarray(byte.astype(np.uint8).reshape(k // 512, 16, n))


def unpack_weight(words, scales, fmt):
    g, _, n = scales.shape
    words = np.ascontiguousarray(words).reshape(g, 128, n, -1)
    if fmt == "e4m3":
        vals = words.view(ml_dtypes.float8_e4m3fn).astype(np.float64)
    else:
        nib = np.empty((g, 128, n, 4), np.uint8)
        nib[..., 0::2] = words & 0xF
        nib[..., 1::2] = words >> 4
        vals = E2M1[nib]
    vals = vals * np.repeat(np.exp2(scales.astype(np.float64) - 127.0), 8, axis=1)[..., None]
    return vals.transpose(0, 1, 3, 2).reshape(g * 512, n)


K, N, T, J = 512, 512, 2048, 1024


def setup_inputs():
    n = np.random.standard_normal
    s = mx_kscale(K)[:, None]
    m = np.exp(0.5 * n((1, J)))
    p_w = pack_weight(n((K, N)) / np.sqrt(K) / s, "e4m3")
    return {
        "dy": (m * n((K, J)) * s).astype(np.float32),
        "w_words": p_w[0],
        "w_scales": p_w[1],
        "wgo": np.tile(np.random.uniform(0.5, 2.0, J), (128, 1)).astype(np.float32),
        "offs": striped(np.random.permutation(T)[:J]),
    }


def reference(dy, w_words, w_scales, wgo, offs):
    idx = unstriped(offs)
    dy_q_ = mxq(f64(dy), 0, "e5m2")
    dy_r_ = mxq(f64(dy) - dy_q_, 0, "e4m3")
    w_ = unpack_weight(w_words, w_scales, "e4m3")
    dx = w_.T @ dy_q_ + w_.T @ dy_r_
    out = np.zeros((N, T))
    out[:, idx] = f64(wgo)[0] * (dx)
    return out

@@ -1,0 +1,243 @@
+from contextlib import ExitStack
+
+import concourse.mybir as mybir
+from concourse.masks import make_identity
+
+K, N, T, J = 512, 512, 2048, 1024
+FLOPS = 1610612736
+
+F32 = mybir.dt.float32
+BF16 = mybir.dt.bfloat16
+I32 = mybir.dt.int32
+U32 = mybir.dt.uint32
+U16 = mybir.dt.uint16
+U8 = mybir.dt.uint8
+E4M3X4 = mybir.dt.float8_e4m3fn_x4
+E5M2X4 = mybir.dt.float8_e5m2_x4
+MULT = mybir.AluOpType.mult
+SUB = mybir.AluOpType.subtract
+COPY = mybir.ActivationFunctionType.Copy
+
+P = 128
+PACK = 4
+CHUNK = 512
+PIECE = 256
+BLOCKS = N // P
+CHUNKS = J // CHUNK
+
+
+def interleave(copy, dst, src, lo, hi):
+    copy(
+        out=dst[:, lo:hi, :].rearrange("p (c j) i -> p c i j", j=4),
+        in_=src[:, :, lo:hi].rearrange("p i (c j) -> p c i j", j=4),
+    )
+
+
+def tile_list_embg_tgq8_none_kernel(tc, dy, w_words, w_scales, wgo, offs, out):
+    nc = tc.nc
+    with ExitStack() as ctx:
+        keep = ctx.enter_context(tc.tile_pool(name="keep", bufs=1))
+        psum = ctx.enter_context(tc.psum_pool(name="psum", bufs=1))
+
+        offsets = keep.tile([P, J // 16], U16, name="offsets")
+        w_codes = keep.tile([P, N], U32, name="w_codes", align_bytes=64)
+        w_plane = keep.tile([P, N], U8, name="w_plane", align_bytes=64)
+        wgo_sb = keep.tile([P, J], F32, name="wgo_sb")
+        dy_rows = dy.rearrange("(p i) j -> p i j", i=PACK)
+        raw_chunk = [keep.tile([P, CHUNK // PIECE, PACK, PIECE], F32, name=f"raw{c}") for c in range(CHUNKS)]
+        raw = [raw_chunk[h // 2][:, h % 2, :, :] for h in range(J // PIECE)]
+
+        nc.vector.memset(w_plane[:].bitcast(I32), 0)
+        for h in (0, 1):
+            nc.sync.dma_start(out=raw[h], in_=dy_rows[:, :, h * PIECE : (h + 1) * PIECE])
+        for q in range(4):
+            nc.sync.dma_start(
+                out=w_plane[32 * q : 32 * q + 4, :].bitcast(I32), in_=w_scales[0, 4 * q : 4 * q + 4, :].bitcast(I32)
+            )
+        nc.sync.dma_start(out=w_codes[:].bitcast(I32), in_=w_words[0].rearrange("p n i -> p (n i)").bitcast(I32))
+        for h in (2, 3):
+            nc.sync.dma_start(out=raw[h], in_=dy_rows[:, :, h * PIECE : (h + 1) * PIECE])
+        nc.sync.dma_start(offsets[:], offs)
+        nc.sync.dma_start(out=wgo_sb[:], in_=wgo)
+
+        eye = keep.tile([P, P], F32, name="eye")
+        make_identity(nc, eye[:])
+        eye_bf = keep.tile([P, PACK, P, PACK], BF16, name="eye_bf", align_bytes=64)
+        nc.vector.memset(eye_bf[:].rearrange("p t m i -> p (t m i)"), 0.0)
+        for t in range(PACK - 1):
+            nc.vector.tensor_copy(out=eye_bf[:, t, :, t], in_=eye[:])
+        nc.scalar.copy(out=eye_bf[:, PACK - 1, :, PACK - 1], in_=eye[:])
+        eye_codes = keep.tile([P, K], U32, name="eye_codes", align_bytes=64)
+        eye_plane = keep.tile([P, K], U8, name="eye_plane", align_bytes=64)
+        nc.vector.quantize_mx(
+            out=eye_codes[:].bitcast(E4M3X4), scales=eye_plane[:], in_=eye_bf[:].rearrange("p t m i -> p (t m i)")
+        )
+
+        q_codes = [keep.tile([P, CHUNK], U32, name="q_codes0", align_bytes=64), None]
+        q_plane = [keep.tile([P, CHUNK], U8, name=f"q_plane{c}", align_bytes=64) for c in range(CHUNKS)]
+        r_codes = [keep.tile([P, CHUNK], U32, name=f"r_codes{c}", align_bytes=64) for c in range(CHUNKS)]
+        r_plane = [keep.tile([P, CHUNK], U8, name=f"r_plane{c}", align_bytes=64) for c in range(CHUNKS)]
+        pages = [None] * BLOCKS
+        acc = {}
+        dx = {}
+
+        def first_tier(h, vector_share, tag):
+            c, lo = divmod(h * PIECE, CHUNK)
+            dy_bf = keep.tile([P, PIECE, PACK], BF16, name=f"dy_bf{h}", tag=tag, align_bytes=64)
+            if vector_share > 0:
+                interleave(nc.vector.tensor_copy, dy_bf, raw[h], 0, vector_share)
+            if vector_share < PIECE:
+                interleave(nc.scalar.copy, dy_bf, raw[h], vector_share, PIECE)
+            nc.vector.quantize_mx(
+                out=q_codes[c][:, lo : lo + PIECE].bitcast(E5M2X4),
+                scales=q_plane[c][:, lo : lo + PIECE],
+                in_=dy_bf[:].rearrange("p j i -> p (j i)"),
+            )
+
+        def clear_page(b, tag):
+            pages[b] = keep.tile([P, T], F32, name=f"page{b}", tag=tag, align_bytes=64)
+            nc.gpsimd.memset(pages[b][:], 0.0)
+
+        def dequantise(c):
+            back = [psum.tile([P, CHUNK], F32, name=f"back{c}_{t}", tag=f"bank{4 * c + t}") for t in range(PACK)]
+            for t in range(PACK):
+                nc.tensor.matmul_mx(
+                    out=back[t][:],
+                    lhsT=eye_codes[:, t * P : (t + 1) * P].bitcast(E4M3X4),
+                    lhsT_scale=eye_plane[:, t * P : (t + 1) * P],
+                    rhs=q_codes[c][:].bitcast(E5M2X4),
+                    rhs_scale=q_plane[c][:],
+                    start=True,
+                    stop=True,
+                )
+            return back
+
+        def first_product(c):
+            for b in range(BLOCKS):
+                acc[c, b] = psum.tile([P, CHUNK], F32, name=f"acc{c}_{b}", tag=f"bank{b}")
+                nc.tensor.matmul_mx(
+                    out=acc[c, b][:],
+                    lhsT=w_codes[:, b * P : (b + 1) * P].bitcast(E4M3X4),
+                    lhsT_scale=w_plane[:, b * P : (b + 1) * P],
+                    rhs=q_codes[c][:].bitcast(E5M2X4),
+                    rhs_scale=q_plane[c][:],
+                    start=True,
+                    stop=False,
+                )
+
+        def first_tier_late(c, tag_in, tag_out):
+            dy_bf = keep.tile([P, CHUNK, PACK], BF16, name=f"dy_bf_late{c}", tag=tag_in, align_bytes=64)
+            for u in range(CHUNK // PIECE):
+                interleave(nc.scalar.copy, dy_bf[:, u * PIECE : (u + 1) * PIECE, :], raw[2 * c + u], 0, PIECE)
+            q_codes[c] = keep.tile([P, CHUNK], U32, name=f"q_codes{c}", tag=tag_out, align_bytes=64)
+            nc.vector.quantize_mx(
+                out=q_codes[c][:].bitcast(E5M2X4), scales=q_plane[c][:], in_=dy_bf[:].rearrange("p j i -> p (j i)")
+            )
+
+        def residual(c, back, tag):
+            left_bf = keep.tile([P, CHUNK, PACK], BF16, name=f"left_bf{c}", tag=tag, align_bytes=64)
+            left = keep.tile([P, PACK, CHUNK], BF16, name=f"left{c}")
+            for t in range(PACK):
+                nc.vector.tensor_tensor(
+                    out=left[:, t, :].rearrange("p (u j) -> p u j", j=PIECE),
+                    in0=raw_chunk[c][:, :, t, :],
+                    in1=back[t][:].rearrange("p (u j) -> p u j", j=PIECE),
+                    op=SUB,
+                )
+            for lo in range(0, CHUNK, PIECE):
+                interleave(nc.vector.tensor_copy, left_bf, left, lo, lo + PIECE)
+            for lo in range(0, CHUNK, PIECE):
+                nc.vector.quantize_mx(
+                    out=r_codes[c][:, lo : lo + PIECE].bitcast(E4M3X4),
+                    scales=r_plane[c][:, lo : lo + PIECE],
+                    in_=left_bf[:, lo : lo + PIECE, :].rearrange("p j i -> p (j i)"),
+                )
+
+        def residual_on_tensor(c, back, tag):
+            left_bf = keep.tile([P, CHUNK, PACK], BF16, name=f"left_bf{c}", tag=tag, align_bytes=64)
+            left_words = left_bf[:].rearrange("p j i -> p (j i)").bitcast(F32).rearrange("p (j u) -> p j u", u=2)
+            minus = [keep.tile([P, CHUNK], F32, name=f"minus{t}") for t in range(PACK)]
+            for t in range(PACK):
+                nc.scalar.activation(out=minus[t][:], in_=back[t][:], func=COPY, scale=-1.0)
+            for g in range(CHUNK // P):
+                h, lo = divmod(c * CHUNK + g * P, PIECE)
+                diff = psum.tile([P, PACK, P], F32, name=f"diff{g}", tag=f"bank{4 + g % 2}")
+                for t in range(PACK):
+                    nc.tensor.matmul(
+                        diff[:, t, :], raw[h][:, t, lo : lo + P], eye[:], start=(t == 0), stop=False, is_transpose=True
+                    )
+                for t in range(PACK):
+                    nc.tensor.matmul(
+                        diff[:, t, :],
+                        minus[t][:, g * P : (g + 1) * P],
+                        eye[:],
+                        start=False,
+                        stop=(t == PACK - 1),
+                        is_transpose=True,
+                    )
+                pairs = keep.tile([P, 2, P, 2], BF16, name=f"pairs{g}", align_bytes=64)
+                nc.scalar.copy(out=pairs[:], in_=diff[:].rearrange("j (u e) p -> j u p e", e=2))
+                pair_words = pairs[:].rearrange("j u p e -> j (u p e)").bitcast(F32)
+                turned = psum.tile([P, 2, P], F32, name=f"turned{g}", tag=f"bank{6 + g % 2}")
+                for u in range(2):
+                    nc.tensor.transpose(turned[:, u, :], pair_words[:, u * P : (u + 1) * P], eye[:])
+                nc.scalar.copy(out=left_words[:, g * P : (g + 1) * P, :], in_=turned[:].rearrange("p u j -> p j u"))
+            nc.vector.quantize_mx(
+                out=r_codes[c][:].bitcast(E4M3X4), scales=r_plane[c][:], in_=left_bf[:].rearrange("p j i -> p (j i)")
+            )
+
+        def second_product(c, b, width):
+            for lo in range(0, CHUNK, width):
+                nc.tensor.matmul_mx(
+                    out=acc[c, b][:, lo : lo + width],
+                    lhsT=w_codes[:, b * P : (b + 1) * P].bitcast(E4M3X4),
+                    lhsT_scale=w_plane[:, b * P : (b + 1) * P],
+                    rhs=r_codes[c][:, lo : lo + width].bitcast(E4M3X4),
+                    rhs_scale=r_plane[c][:, lo : lo + width],
+                    start=False,
+                    stop=(lo + width == CHUNK),
+                )
+
+        def evacuate(c, b, tag, width=CHUNK):
+            dx[c, b] = keep.tile([P, CHUNK], F32, name=f"dx{c}_{b}", tag=tag, align_bytes=64)
+            for lo in range(0, CHUNK, width):
+                nc.scalar.copy(out=dx[c, b][:, lo : lo + width], in_=acc[c, b][:, lo : lo + width])
+
+        def scatter(c, b, width=CHUNK):
+            for lo in range(0, CHUNK, width):
+                j = c * CHUNK + lo
+                nc.vector.tensor_tensor(
+                    out=pages[b][:].indirect(offsets[:, j // 16 : (j + width) // 16]),
+                    in0=dx[c, b][:, lo : lo + width],
+                    in1=wgo_sb[:, j : j + width],
+                    op=MULT,
+                )
+
+        first_tier(0, PIECE, "eye_bf")
+        first_tier(1, 176, "page0")
+        back = dequantise(0)
+        first_product(0)
+        clear_page(0, "page0")
+        residual(0, back, "left_bf0")
+        for b in range(BLOCKS):
+            second_product(0, b, PIECE if b == 0 else CHUNK)
+        evacuate(0, 0, "page2")
+        first_tier_late(1, "page1", "left_bf0")
+        scatter(0, 0)
+        evacuate(0, 1, "page3")
+        evacuate(0, 2, "dx0_2")
+        back = dequantise(1)
+        clear_page(1, "page1")
+        clear_page(2, "page2")
+        scatter(0, 1)
+        residual_on_tensor(1, back, "left_bf1")
+        clear_page(3, "page3")
+        scatter(0, 2)
+        evacuate(0, 3, "pairs3")
+        first_product(1)
+        scatter(0, 3)
+        for b in range(BLOCKS):
+            second_product(1, b, CHUNK)
+            evacuate(1, b, f"dx1_{b}")
+            scatter(1, b)
+            nc.sync.dma_start(out=out[b * P : (b + 1) * P, :], in_=pages[b][:])

@@ -1,7 +1,6 @@
 from contextlib import ExitStack
 
 import concourse.mybir as mybir
-from concourse.masks import make_identity
 
 K, N, T, J = 512, 512, 2048, 1024
 FLOPS = 1610612736
@@ -15,7 +14,9 @@ U8 = mybir.dt.uint8
 E4M3X4 = mybir.dt.float8_e4m3fn_x4
 E5M2X4 = mybir.dt.float8_e5m2_x4
 MULT = mybir.AluOpType.mult
+ADD = mybir.AluOpType.add
 SUB = mybir.AluOpType.subtract
+IS_EQUAL = mybir.AluOpType.is_equal
 COPY = mybir.ActivationFunctionType.Copy
 
 P = 128
@@ -37,6 +38,7 @@ def tile_list_embg_tgq8_none_kernel(tc, dy, w_words, w_scales, wgo, offs, out):
     nc = tc.nc
     with ExitStack() as ctx:
         keep = ctx.enter_context(tc.tile_pool(name="keep", bufs=1))
+        shared = ctx.enter_context(tc.tile_pool(name="shared", bufs=1))
         psum = ctx.enter_context(tc.psum_pool(name="psum", bufs=1))
 
         offsets = keep.tile([P, J // 16], U16, name="offsets")
@@ -60,18 +62,31 @@ def tile_list_embg_tgq8_none_kernel(tc, dy, w_words, w_scales, wgo, offs, out):
         nc.sync.dma_start(offsets[:], offs)
         nc.sync.dma_start(out=wgo_sb[:], in_=wgo)
 
+        ones = keep.tile([P, P], F32, name="ones")
+        nc.vector.memset(ones[:], 1.0)
+        ramp = keep.tile([P, P], F32, name="ramp", align_bytes=64)
+        nc.vector.tensor_tensor_scan(out=ramp[:], data0=ones[:], data1=ones[:], initial=-1.0, op0=MULT, op1=ADD)
+        lane = keep.tile([P, 32], F32, name="lane", align_bytes=64)
+        nc.vector.transpose(out=lane[:], in_=ramp[:, 0:32])
+        quadrant = keep.tile([P, 1], F32, name="quadrant")
+        for q in range(4):
+            nc.vector.memset(quadrant[32 * q : 32 * (q + 1), :], 32.0 * q)
+        marks = keep.tile([P, K + PACK], BF16, name="marks")
+        nc.vector.memset(marks[:].bitcast(I32), 0)
+        diagonal = marks[:, PACK - 1 : K + PACK - 1 : PACK]
+        nc.vector.tensor_scalar(
+            out=diagonal, in0=ramp[:], scalar1=lane[:, 0:1], scalar2=quadrant[:], op0=SUB, op1=IS_EQUAL
+        )
+        eye_first = shared.tile([P, K], BF16, name="eye_first", align_bytes=64, offset=4 * T + 1024)
+        eye_rest = keep.tile([P, PACK - 1, K], BF16, name="eye_rest", align_bytes=64)
+        eye_bf = [eye_first[:]] + [eye_rest[:, t, :] for t in range(PACK - 1)]
+        for t in range(PACK):
+            nc.vector.tensor_copy(out=eye_bf[t], in_=marks[:, PACK - 1 - t : K + PACK - 1 - t])
         eye = keep.tile([P, P], F32, name="eye")
-        make_identity(nc, eye[:])
-        eye_bf = keep.tile([P, PACK, P, PACK], BF16, name="eye_bf", align_bytes=64)
-        nc.vector.memset(eye_bf[:].rearrange("p t m i -> p (t m i)"), 0.0)
-        for t in range(PACK - 1):
-            nc.vector.tensor_copy(out=eye_bf[:, t, :, t], in_=eye[:])
-        nc.scalar.copy(out=eye_bf[:, PACK - 1, :, PACK - 1], in_=eye[:])
+        nc.scalar.copy(out=eye[:], in_=diagonal)
         eye_codes = keep.tile([P, K], U32, name="eye_codes", align_bytes=64)
         eye_plane = keep.tile([P, K], U8, name="eye_plane", align_bytes=64)
-        nc.vector.quantize_mx(
-            out=eye_codes[:].bitcast(E4M3X4), scales=eye_plane[:], in_=eye_bf[:].rearrange("p t m i -> p (t m i)")
-        )
+        nc.vector.quantize_mx(out=eye_codes[:, :P].bitcast(E4M3X4), scales=eye_plane[:, :P], in_=eye_bf[0])
 
         q_codes = [keep.tile([P, CHUNK], U32, name="q_codes0", align_bytes=64), None]
         q_plane = [keep.tile([P, CHUNK], U8, name=f"q_plane{c}", align_bytes=64) for c in range(CHUNKS)]
@@ -81,9 +96,8 @@ def tile_list_embg_tgq8_none_kernel(tc, dy, w_words, w_scales, wgo, offs, out):
         acc = {}
         dx = {}
 
-        def first_tier(h, vector_share, tag):
+        def first_tier(h, vector_share, dy_bf):
             c, lo = divmod(h * PIECE, CHUNK)
-            dy_bf = keep.tile([P, PIECE, PACK], BF16, name=f"dy_bf{h}", tag=tag, align_bytes=64)
             if vector_share > 0:
                 interleave(nc.vector.tensor_copy, dy_bf, raw[h], 0, vector_share)
             if vector_share < PIECE:
@@ -93,10 +107,6 @@ def tile_list_embg_tgq8_none_kernel(tc, dy, w_words, w_scales, wgo, offs, out):
                 scales=q_plane[c][:, lo : lo + PIECE],
                 in_=dy_bf[:].rearrange("p j i -> p (j i)"),
             )
-
-        def clear_page(b, tag):
-            pages[b] = keep.tile([P, T], F32, name=f"page{b}", tag=tag, align_bytes=64)
-            nc.gpsimd.memset(pages[b][:], 0.0)
 
         def dequantise(c):
             back = [psum.tile([P, CHUNK], F32, name=f"back{c}_{t}", tag=f"bank{4 * c + t}") for t in range(PACK)]
@@ -112,18 +122,17 @@ def tile_list_embg_tgq8_none_kernel(tc, dy, w_words, w_scales, wgo, offs, out):
                 )
             return back
 
-        def first_product(c):
-            for b in range(BLOCKS):
-                acc[c, b] = psum.tile([P, CHUNK], F32, name=f"acc{c}_{b}", tag=f"bank{b}")
-                nc.tensor.matmul_mx(
-                    out=acc[c, b][:],
-                    lhsT=w_codes[:, b * P : (b + 1) * P].bitcast(E4M3X4),
-                    lhsT_scale=w_plane[:, b * P : (b + 1) * P],
-                    rhs=q_codes[c][:].bitcast(E5M2X4),
-                    rhs_scale=q_plane[c][:],
-                    start=True,
-                    stop=False,
-                )
+        def first_product(c, b, bank):
+            acc[c, b] = psum.tile([P, CHUNK], F32, name=f"acc{c}_{b}", tag=f"bank{bank}")
+            nc.tensor.matmul_mx(
+                out=acc[c, b][:],
+                lhsT=w_codes[:, b * P : (b + 1) * P].bitcast(E4M3X4),
+                lhsT_scale=w_plane[:, b * P : (b + 1) * P],
+                rhs=q_codes[c][:].bitcast(E5M2X4),
+                rhs_scale=q_plane[c][:],
+                start=True,
+                stop=False,
+            )
 
         def first_tier_late(c, tag_in, tag_out):
             dy_bf = keep.tile([P, CHUNK, PACK], BF16, name=f"dy_bf_late{c}", tag=tag_in, align_bytes=64)
@@ -161,7 +170,7 @@ def tile_list_embg_tgq8_none_kernel(tc, dy, w_words, w_scales, wgo, offs, out):
                 nc.scalar.activation(out=minus[t][:], in_=back[t][:], func=COPY, scale=-1.0)
             for g in range(CHUNK // P):
                 h, lo = divmod(c * CHUNK + g * P, PIECE)
-                diff = psum.tile([P, PACK, P], F32, name=f"diff{g}", tag=f"bank{4 + g % 2}")
+                diff = psum.tile([P, PACK, P], F32, name=f"diff{g}", tag=f"bank{(0, 1, 2, 4)[g]}")
                 for t in range(PACK):
                     nc.tensor.matmul(
                         diff[:, t, :], raw[h][:, t, lo : lo + P], eye[:], start=(t == 0), stop=False, is_transpose=True
@@ -175,10 +184,10 @@ def tile_list_embg_tgq8_none_kernel(tc, dy, w_words, w_scales, wgo, offs, out):
                         stop=(t == PACK - 1),
                         is_transpose=True,
                     )
-                pairs = keep.tile([P, 2, P, 2], BF16, name=f"pairs{g}", align_bytes=64)
+                pairs = keep.tile([P, 2, P, 2], BF16, name=f"pairs{g}", tag=f"pairs{g}", align_bytes=64)
                 nc.scalar.copy(out=pairs[:], in_=diff[:].rearrange("j (u e) p -> j u p e", e=2))
                 pair_words = pairs[:].rearrange("j u p e -> j (u p e)").bitcast(F32)
-                turned = psum.tile([P, 2, P], F32, name=f"turned{g}", tag=f"bank{6 + g % 2}")
+                turned = psum.tile([P, 2, P], F32, name=f"turned{g}", tag=f"bank{5 + g % 3}")
                 for u in range(2):
                     nc.tensor.transpose(turned[:, u, :], pair_words[:, u * P : (u + 1) * P], eye[:])
                 nc.scalar.copy(out=left_words[:, g * P : (g + 1) * P, :], in_=turned[:].rearrange("p u j -> p j u"))
@@ -198,46 +207,64 @@ def tile_list_embg_tgq8_none_kernel(tc, dy, w_words, w_scales, wgo, offs, out):
                     stop=(lo + width == CHUNK),
                 )
 
-        def evacuate(c, b, tag, width=CHUNK):
-            dx[c, b] = keep.tile([P, CHUNK], F32, name=f"dx{c}_{b}", tag=tag, align_bytes=64)
-            for lo in range(0, CHUNK, width):
-                nc.scalar.copy(out=dx[c, b][:, lo : lo + width], in_=acc[c, b][:, lo : lo + width])
+        def evacuate(c, b, dst, lo=0, hi=CHUNK):
+            nc.scalar.copy(out=dst, in_=acc[c, b][:, lo:hi])
 
-        def scatter(c, b, width=CHUNK):
-            for lo in range(0, CHUNK, width):
-                j = c * CHUNK + lo
-                nc.vector.tensor_tensor(
-                    out=pages[b][:].indirect(offsets[:, j // 16 : (j + width) // 16]),
-                    in0=dx[c, b][:, lo : lo + width],
-                    in1=wgo_sb[:, j : j + width],
-                    op=MULT,
-                )
+        def scatter(page, values, j, width):
+            nc.vector.tensor_tensor(
+                out=page[:].indirect(offsets[:, j // 16 : (j + width) // 16]),
+                in0=values,
+                in1=wgo_sb[:, j : j + width],
+                op=MULT,
+            )
 
-        first_tier(0, PIECE, "eye_bf")
-        first_tier(1, 176, "page0")
+        dy_bf0 = shared.tile([P, PIECE, PACK], BF16, name="dy_bf0", align_bytes=64, offset=4 * T + 1024)
+        first_tier(0, PIECE, dy_bf0)
+        dy_bf1 = shared.tile([P, PIECE, PACK], BF16, name="dy_bf1", align_bytes=64, offset=4 * T - 1024)
+        first_tier(1, 176, dy_bf1)
+        nc.vector.quantize_mx(out=eye_codes[:, P : 2 * P].bitcast(E4M3X4), scales=eye_plane[:, P : 2 * P], in_=eye_bf[1])
+        nc.vector.quantize_mx(
+            out=eye_codes[:, 2 * P :].bitcast(E4M3X4),
+            scales=eye_plane[:, 2 * P :],
+            in_=eye_rest[:, 1:, :].rearrange("p t m -> p (t m)"),
+        )
         back = dequantise(0)
-        first_product(0)
-        clear_page(0, "page0")
+        pages[0] = shared.tile([P, T], F32, name="page0", align_bytes=64, offset=0)
+        nc.vector.memset(pages[0][:, : T // 4 + 8], 0.0)
+        nc.gpsimd.memset(pages[0][:, T // 4 :], 0.0)
         residual(0, back, "left_bf0")
         for b in range(BLOCKS):
+            first_product(0, b, b)
+        for b in range(BLOCKS):
             second_product(0, b, PIECE if b == 0 else CHUNK)
-        evacuate(0, 0, "page2")
+
+        def clear_page(b):
+            pages[b] = keep.tile([P, T], F32, name=f"page{b}", tag=f"page{b}", align_bytes=64)
+            nc.gpsimd.memset(pages[b][:], 0.0)
+
+        dx00 = keep.tile([P, CHUNK], F32, name="dx00", tag="page2", align_bytes=64)
+        evacuate(0, 0, dx00[:])
         first_tier_late(1, "page1", "left_bf0")
-        scatter(0, 0)
-        evacuate(0, 1, "page3")
-        evacuate(0, 2, "dx0_2")
+        clear_page(1)
+        scatter(pages[0], dx00[:], 0, CHUNK)
+        clear_page(2)
+        dx01 = keep.tile([P, CHUNK], F32, name="dx01", tag="page3", align_bytes=64)
+        evacuate(0, 1, dx01[:])
         back = dequantise(1)
-        clear_page(1, "page1")
-        clear_page(2, "page2")
-        scatter(0, 1)
+        scatter(pages[1], dx01[:], 0, CHUNK)
+        clear_page(3)
+        dx02 = keep.tile([P, CHUNK], F32, name="dx02")
+        evacuate(0, 2, dx02[:])
+        scatter(pages[2], dx02[:], 0, CHUNK)
         residual_on_tensor(1, back, "left_bf1")
-        clear_page(3, "page3")
-        scatter(0, 2)
-        evacuate(0, 3, "pairs3")
-        first_product(1)
-        scatter(0, 3)
+        dx03 = keep.tile([P, CHUNK], F32, name="dx03", tag="pairs3", align_bytes=64)
+        evacuate(0, 3, dx03[:])
+        scatter(pages[3], dx03[:], 0, CHUNK)
+        for b in range(BLOCKS):
+            first_product(1, b, (0, 1, 2, 4)[b])
         for b in range(BLOCKS):
             second_product(1, b, CHUNK)
-            evacuate(1, b, f"dx1_{b}")
-            scatter(1, b)
+            dx1 = keep.tile([P, CHUNK], F32, name=f"dx1{b}")
+            evacuate(1, b, dx1[:])
+            scatter(pages[b], dx1[:], CHUNK, CHUNK)
             nc.sync.dma_start(out=out[b * P : (b + 1) * P, :], in_=pages[b][:])

@@ -25,6 +25,7 @@ CHUNK = 512
 PIECE = 256
 BLOCKS = N // P
 CHUNKS = J // CHUNK
+EYE_ORDER = (3, 0, 1, 2)
 
 
 def interleave(copy, dst, src, lo, hi):
@@ -50,17 +51,19 @@ def tile_list_embg_tgq8_none_kernel(tc, dy, w_words, w_scales, wgo, offs, out):
         raw = [raw_chunk[h // 2][:, h % 2, :, :] for h in range(J // PIECE)]
 
         nc.vector.memset(w_plane[:].bitcast(I32), 0)
-        for h in (0, 1):
+        nc.sync.dma_start(out=raw[0], in_=dy_rows[:, :, :PIECE])
+        for lo in (0, P):
+            nc.sync.dma_start(out=raw[1][:, :, lo : lo + P], in_=dy_rows[:, :, PIECE + lo : PIECE + lo + P])
+        for h in (2, 3):
             nc.sync.dma_start(out=raw[h], in_=dy_rows[:, :, h * PIECE : (h + 1) * PIECE])
+        nc.sync.dma_start(out=w_codes[:].bitcast(I32), in_=w_words[0].rearrange("p n i -> p (n i)").bitcast(I32))
         for q in range(4):
             nc.sync.dma_start(
                 out=w_plane[32 * q : 32 * q + 4, :].bitcast(I32), in_=w_scales[0, 4 * q : 4 * q + 4, :].bitcast(I32)
             )
-        nc.sync.dma_start(out=w_codes[:].bitcast(I32), in_=w_words[0].rearrange("p n i -> p (n i)").bitcast(I32))
-        for h in (2, 3):
-            nc.sync.dma_start(out=raw[h], in_=dy_rows[:, :, h * PIECE : (h + 1) * PIECE])
         nc.sync.dma_start(offsets[:], offs)
-        nc.sync.dma_start(out=wgo_sb[:], in_=wgo)
+        for lo in range(0, J, CHUNK):
+            nc.sync.dma_start(out=wgo_sb[:, lo : lo + CHUNK], in_=wgo[:, lo : lo + CHUNK])
 
         ones = keep.tile([P, P], F32, name="ones")
         nc.vector.memset(ones[:], 1.0)
@@ -71,22 +74,21 @@ def tile_list_embg_tgq8_none_kernel(tc, dy, w_words, w_scales, wgo, offs, out):
         quadrant = keep.tile([P, 1], F32, name="quadrant")
         for q in range(4):
             nc.vector.memset(quadrant[32 * q : 32 * (q + 1), :], 32.0 * q)
-        marks = keep.tile([P, K + PACK], BF16, name="marks")
+        marks = keep.tile([P, K + PACK], BF16, name="marks", align_bytes=64)
         nc.vector.memset(marks[:].bitcast(I32), 0)
         diagonal = marks[:, PACK - 1 : K + PACK - 1 : PACK]
         nc.vector.tensor_scalar(
             out=diagonal, in0=ramp[:], scalar1=lane[:, 0:1], scalar2=quadrant[:], op0=SUB, op1=IS_EQUAL
         )
-        eye_first = shared.tile([P, K], BF16, name="eye_first", align_bytes=64, offset=4 * T + 1024)
-        eye_rest = keep.tile([P, PACK - 1, K], BF16, name="eye_rest", align_bytes=64)
-        eye_bf = [eye_first[:]] + [eye_rest[:, t, :] for t in range(PACK - 1)]
-        for t in range(PACK):
-            nc.vector.tensor_copy(out=eye_bf[t], in_=marks[:, PACK - 1 - t : K + PACK - 1 - t])
+        eye_last = keep.tile([P, P], U32, name="eye_last", align_bytes=64)
+        eye_plane = keep.tile([P, K], U8, name="eye_plane", align_bytes=64)
+        nc.vector.quantize_mx(out=eye_last[:].bitcast(E4M3X4), scales=eye_plane[:, 3 * P :], in_=marks[:, :K])
+        eye_rest = shared.tile([P, PACK - 1, K], BF16, name="eye_rest", align_bytes=64, offset=2048)
+        for t in range(PACK - 1):
+            copy = nc.vector.tensor_copy if t == 0 else nc.scalar.copy
+            copy(out=eye_rest[:, t, :], in_=marks[:, PACK - 1 - t : K + PACK - 1 - t])
         eye = keep.tile([P, P], F32, name="eye")
         nc.scalar.copy(out=eye[:], in_=diagonal)
-        eye_codes = keep.tile([P, K], U32, name="eye_codes", align_bytes=64)
-        eye_plane = keep.tile([P, K], U8, name="eye_plane", align_bytes=64)
-        nc.vector.quantize_mx(out=eye_codes[:, :P].bitcast(E4M3X4), scales=eye_plane[:, :P], in_=eye_bf[0])
 
         q_codes = [keep.tile([P, CHUNK], U32, name="q_codes0", align_bytes=64), None]
         q_plane = [keep.tile([P, CHUNK], U8, name=f"q_plane{c}", align_bytes=64) for c in range(CHUNKS)]
@@ -96,24 +98,21 @@ def tile_list_embg_tgq8_none_kernel(tc, dy, w_words, w_scales, wgo, offs, out):
         acc = {}
         dx = {}
 
-        def first_tier(h, vector_share, dy_bf):
-            c, lo = divmod(h * PIECE, CHUNK)
-            if vector_share > 0:
-                interleave(nc.vector.tensor_copy, dy_bf, raw[h], 0, vector_share)
-            if vector_share < PIECE:
-                interleave(nc.scalar.copy, dy_bf, raw[h], vector_share, PIECE)
+        def first_tier(copy, j, width, dy_bf):
+            h, lo = divmod(j, PIECE)
+            interleave(copy, dy_bf, raw[h][:, :, lo : lo + width], 0, width)
             nc.vector.quantize_mx(
-                out=q_codes[c][:, lo : lo + PIECE].bitcast(E5M2X4),
-                scales=q_plane[c][:, lo : lo + PIECE],
+                out=q_codes[0][:, j : j + width].bitcast(E5M2X4),
+                scales=q_plane[0][:, j : j + width],
                 in_=dy_bf[:].rearrange("p j i -> p (j i)"),
             )
 
         def dequantise(c):
             back = [psum.tile([P, CHUNK], F32, name=f"back{c}_{t}", tag=f"bank{4 * c + t}") for t in range(PACK)]
-            for t in range(PACK):
+            for t in EYE_ORDER:
                 nc.tensor.matmul_mx(
                     out=back[t][:],
-                    lhsT=eye_codes[:, t * P : (t + 1) * P].bitcast(E4M3X4),
+                    lhsT=eye_codes[t].bitcast(E4M3X4),
                     lhsT_scale=eye_plane[:, t * P : (t + 1) * P],
                     rhs=q_codes[c][:].bitcast(E5M2X4),
                     rhs_scale=q_plane[c][:],
@@ -134,43 +133,22 @@ def tile_list_embg_tgq8_none_kernel(tc, dy, w_words, w_scales, wgo, offs, out):
                 stop=False,
             )
 
-        def first_tier_late(c, tag_in, tag_out):
-            dy_bf = keep.tile([P, CHUNK, PACK], BF16, name=f"dy_bf_late{c}", tag=tag_in, align_bytes=64)
-            for u in range(CHUNK // PIECE):
-                interleave(nc.scalar.copy, dy_bf[:, u * PIECE : (u + 1) * PIECE, :], raw[2 * c + u], 0, PIECE)
-            q_codes[c] = keep.tile([P, CHUNK], U32, name=f"q_codes{c}", tag=tag_out, align_bytes=64)
+        def second_tier(c, lo, left_bf):
             nc.vector.quantize_mx(
-                out=q_codes[c][:].bitcast(E5M2X4), scales=q_plane[c][:], in_=dy_bf[:].rearrange("p j i -> p (j i)")
+                out=r_codes[c][:, lo : lo + PIECE].bitcast(E4M3X4),
+                scales=r_plane[c][:, lo : lo + PIECE],
+                in_=left_bf.rearrange("p j i -> p (j i)"),
             )
-
-        def residual(c, back, tag):
-            left_bf = keep.tile([P, CHUNK, PACK], BF16, name=f"left_bf{c}", tag=tag, align_bytes=64)
-            left = keep.tile([P, PACK, CHUNK], BF16, name=f"left{c}")
-            for t in range(PACK):
-                nc.vector.tensor_tensor(
-                    out=left[:, t, :].rearrange("p (u j) -> p u j", j=PIECE),
-                    in0=raw_chunk[c][:, :, t, :],
-                    in1=back[t][:].rearrange("p (u j) -> p u j", j=PIECE),
-                    op=SUB,
-                )
-            for lo in range(0, CHUNK, PIECE):
-                interleave(nc.vector.tensor_copy, left_bf, left, lo, lo + PIECE)
-            for lo in range(0, CHUNK, PIECE):
-                nc.vector.quantize_mx(
-                    out=r_codes[c][:, lo : lo + PIECE].bitcast(E4M3X4),
-                    scales=r_plane[c][:, lo : lo + PIECE],
-                    in_=left_bf[:, lo : lo + PIECE, :].rearrange("p j i -> p (j i)"),
-                )
 
         def residual_on_tensor(c, back, tag):
             left_bf = keep.tile([P, CHUNK, PACK], BF16, name=f"left_bf{c}", tag=tag, align_bytes=64)
             left_words = left_bf[:].rearrange("p j i -> p (j i)").bitcast(F32).rearrange("p (j u) -> p j u", u=2)
             minus = [keep.tile([P, CHUNK], F32, name=f"minus{t}") for t in range(PACK)]
-            for t in range(PACK):
+            for t in EYE_ORDER:
                 nc.scalar.activation(out=minus[t][:], in_=back[t][:], func=COPY, scale=-1.0)
             for g in range(CHUNK // P):
                 h, lo = divmod(c * CHUNK + g * P, PIECE)
-                diff = psum.tile([P, PACK, P], F32, name=f"diff{g}", tag=f"bank{(0, 1, 2, 4)[g]}")
+                diff = psum.tile([P, PACK, P], F32, name=f"diff{g}", tag=f"bank{g}")
                 for t in range(PACK):
                     nc.tensor.matmul(
                         diff[:, t, :], raw[h][:, t, lo : lo + P], eye[:], start=(t == 0), stop=False, is_transpose=True
@@ -191,12 +169,15 @@ def tile_list_embg_tgq8_none_kernel(tc, dy, w_words, w_scales, wgo, offs, out):
                 for u in range(2):
                     nc.tensor.transpose(turned[:, u, :], pair_words[:, u * P : (u + 1) * P], eye[:])
                 nc.scalar.copy(out=left_words[:, g * P : (g + 1) * P, :], in_=turned[:].rearrange("p u j -> p j u"))
-            nc.vector.quantize_mx(
-                out=r_codes[c][:].bitcast(E4M3X4), scales=r_plane[c][:], in_=left_bf[:].rearrange("p j i -> p (j i)")
-            )
+            for lo in range(0, CHUNK, PIECE):
+                nc.vector.quantize_mx(
+                    out=r_codes[c][:, lo : lo + PIECE].bitcast(E4M3X4),
+                    scales=r_plane[c][:, lo : lo + PIECE],
+                    in_=left_bf[:, lo : lo + PIECE, :].rearrange("p j i -> p (j i)"),
+                )
 
-        def second_product(c, b, width):
-            for lo in range(0, CHUNK, width):
+        def second_product(c, b, width, first=0, last=CHUNK):
+            for lo in range(first, last, width):
                 nc.tensor.matmul_mx(
                     out=acc[c, b][:, lo : lo + width],
                     lhsT=w_codes[:, b * P : (b + 1) * P].bitcast(E4M3X4),
@@ -204,7 +185,7 @@ def tile_list_embg_tgq8_none_kernel(tc, dy, w_words, w_scales, wgo, offs, out):
                     rhs=r_codes[c][:, lo : lo + width].bitcast(E4M3X4),
                     rhs_scale=r_plane[c][:, lo : lo + width],
                     start=False,
-                    stop=(lo + width == CHUNK),
+                    stop=(lo + width == last),
                 )
 
         def evacuate(c, b, dst, lo=0, hi=CHUNK):
@@ -218,52 +199,74 @@ def tile_list_embg_tgq8_none_kernel(tc, dy, w_words, w_scales, wgo, offs, out):
                 op=MULT,
             )
 
-        dy_bf0 = shared.tile([P, PIECE, PACK], BF16, name="dy_bf0", align_bytes=64, offset=4 * T + 1024)
-        first_tier(0, PIECE, dy_bf0)
-        dy_bf1 = shared.tile([P, PIECE, PACK], BF16, name="dy_bf1", align_bytes=64, offset=4 * T - 1024)
-        first_tier(1, 176, dy_bf1)
-        nc.vector.quantize_mx(out=eye_codes[:, P : 2 * P].bitcast(E4M3X4), scales=eye_plane[:, P : 2 * P], in_=eye_bf[1])
+        dy_bf0 = keep.tile([P, PIECE, PACK], BF16, name="dy_bf0", align_bytes=64)
+        first_tier(nc.vector.tensor_copy, 0, PIECE, dy_bf0)
+        dy_bf1 = keep.tile([P, P, PACK], BF16, name="dy_bf1", align_bytes=64)
+        first_tier(nc.scalar.copy, PIECE, P, dy_bf1)
+        dy_bf2 = keep.tile([P, P, PACK], BF16, name="dy_bf2", tag="eye_first", align_bytes=64)
+        first_tier(nc.vector.tensor_copy, PIECE + P, P, dy_bf2)
+        pages[1] = keep.tile([P, T], F32, name="page1", align_bytes=64)
+        for lo in range(0, T, PIECE):
+            nc.vector.memset(pages[1][:, lo : lo + PIECE], 0.0)
+        eye_first = keep.tile([P, 3 * P], U32, name="eye_first", tag="eye_first", align_bytes=64)
+        eye_codes = [eye_first[:, t * P : (t + 1) * P] for t in range(PACK - 1)] + [eye_last[:]]
+        nc.vector.quantize_mx(out=eye_codes[0].bitcast(E4M3X4), scales=eye_plane[:, :P], in_=eye_rest[:, 0, :])
         nc.vector.quantize_mx(
-            out=eye_codes[:, 2 * P :].bitcast(E4M3X4),
-            scales=eye_plane[:, 2 * P :],
+            out=eye_first[:, P:].bitcast(E4M3X4),
+            scales=eye_plane[:, P : 3 * P],
             in_=eye_rest[:, 1:, :].rearrange("p t m -> p (t m)"),
         )
         back = dequantise(0)
         pages[0] = shared.tile([P, T], F32, name="page0", align_bytes=64, offset=0)
-        nc.vector.memset(pages[0][:, : T // 4 + 8], 0.0)
-        nc.gpsimd.memset(pages[0][:, T // 4 :], 0.0)
-        residual(0, back, "left_bf0")
+        nc.gpsimd.memset(pages[0][:], 0.0)
+        dy_bf_late = shared.tile([P, CHUNK, PACK], BF16, name="dy_bf_late", align_bytes=64, offset=4 * T + 2048)
+        for u in range(CHUNK // PIECE):
+            interleave(nc.scalar.copy, dy_bf_late[:, u * PIECE : (u + 1) * PIECE, :], raw[2 + u], 0, PIECE)
+        left = keep.tile([P, PACK, CHUNK], BF16, name="left")
+        for t in EYE_ORDER:
+            nc.vector.tensor_tensor(
+                out=left[:, t, :].rearrange("p (u j) -> p u j", j=PIECE),
+                in0=raw_chunk[0][:, :, t, :],
+                in1=back[t][:].rearrange("p (u j) -> p u j", j=PIECE),
+                op=SUB,
+            )
+        left_bf0 = keep.tile([P, PIECE, PACK], BF16, name="left_bf0", tag="left_bf0", align_bytes=64)
+        interleave(nc.vector.tensor_copy, left_bf0, left[:, :, :PIECE], 0, PIECE)
+        left_bf1 = shared.tile([P, PIECE, PACK], BF16, name="left_bf1", align_bytes=64, offset=4 * T)
+        interleave(nc.scalar.copy, left_bf1, left[:, :, PIECE:], 0, PIECE)
+        second_tier(0, 0, left_bf0[:])
+        second_tier(0, PIECE, left_bf1[:])
+        q_codes[1] = keep.tile([P, CHUNK], U32, name="q_codes1", tag="left_bf0", align_bytes=64)
+        nc.vector.quantize_mx(
+            out=q_codes[1][:].bitcast(E5M2X4), scales=q_plane[1][:], in_=dy_bf_late[:].rearrange("p j i -> p (j i)")
+        )
+        pages[2] = shared.tile([P, T], F32, name="page2", align_bytes=64, offset=4 * T)
+        nc.gpsimd.memset(pages[2][:], 0.0)
         for b in range(BLOCKS):
             first_product(0, b, b)
-        for b in range(BLOCKS):
-            second_product(0, b, PIECE if b == 0 else CHUNK)
-
-        def clear_page(b):
-            pages[b] = keep.tile([P, T], F32, name=f"page{b}", tag=f"page{b}", align_bytes=64)
-            nc.gpsimd.memset(pages[b][:], 0.0)
-
-        dx00 = keep.tile([P, CHUNK], F32, name="dx00", tag="page2", align_bytes=64)
-        evacuate(0, 0, dx00[:])
-        first_tier_late(1, "page1", "left_bf0")
-        clear_page(1)
-        scatter(pages[0], dx00[:], 0, CHUNK)
-        clear_page(2)
-        dx01 = keep.tile([P, CHUNK], F32, name="dx01", tag="page3", align_bytes=64)
-        evacuate(0, 1, dx01[:])
+        second_product(0, 0, PIECE, 0, PIECE)
+        dx00 = keep.tile([P, PIECE], F32, name="dx00", tag="page3", align_bytes=64)
+        evacuate(0, 0, dx00[:], 0, PIECE)
+        scatter(pages[0], dx00[:], 0, PIECE)
+        pages[3] = keep.tile([P, T], F32, name="page3", tag="page3", align_bytes=64)
+        nc.gpsimd.memset(pages[3][:], 0.0)
+        for b in range(1, BLOCKS):
+            second_product(0, b, CHUNK)
+            dx0 = keep.tile([P, CHUNK], F32, name=f"dx0{b}")
+            evacuate(0, b, dx0[:])
+            scatter(pages[b], dx0[:], 0, CHUNK)
         back = dequantise(1)
-        scatter(pages[1], dx01[:], 0, CHUNK)
-        clear_page(3)
-        dx02 = keep.tile([P, CHUNK], F32, name="dx02")
-        evacuate(0, 2, dx02[:])
-        scatter(pages[2], dx02[:], 0, CHUNK)
-        residual_on_tensor(1, back, "left_bf1")
-        dx03 = keep.tile([P, CHUNK], F32, name="dx03", tag="pairs3", align_bytes=64)
-        evacuate(0, 3, dx03[:])
-        scatter(pages[3], dx03[:], 0, CHUNK)
-        for b in range(BLOCKS):
-            first_product(1, b, (0, 1, 2, 4)[b])
-        for b in range(BLOCKS):
-            second_product(1, b, CHUNK)
+        residual_on_tensor(1, back, "left_bf_late")
+        first_product(0, 0, 3)
+        second_product(0, 0, PIECE, PIECE, CHUNK)
+        dx00b = keep.tile([P, PIECE], F32, name="dx00b", align_bytes=64)
+        evacuate(0, 0, dx00b[:], PIECE, CHUNK)
+        scatter(pages[0], dx00b[:], PIECE, PIECE)
+        last = (1, 2, 3, 0)
+        for b in last:
+            first_product(1, b, (4, 0, 1, 2)[b])
+        for b in last:
+            second_product(1, b, PIECE if b == last[0] else CHUNK)
             dx1 = keep.tile([P, CHUNK], F32, name=f"dx1{b}")
             evacuate(1, b, dx1[:])
             scatter(pages[b], dx1[:], CHUNK, CHUNK)

@@ -58,7 +58,8 @@ def tile_list_embg_tgq8_none_kernel(tc, dy, w_words, w_scales, wgo, offs, out):
             nc.sync.dma_start(out=raw[h], in_=dy_rows[:, :, h * PIECE : (h + 1) * PIECE])
         nc.sync.dma_start(out=w_codes[:].bitcast(I32), in_=w_words[0].rearrange("p n i -> p (n i)").bitcast(I32))
         for q in range(4):
-            nc.sync.dma_start(
+            queue = nc.scalar if q < 2 else nc.sync
+            queue.dma_start(
                 out=w_plane[32 * q : 32 * q + 4, :].bitcast(I32), in_=w_scales[0, 4 * q : 4 * q + 4, :].bitcast(I32)
             )
         nc.sync.dma_start(offsets[:], offs)
@@ -133,19 +134,22 @@ def tile_list_embg_tgq8_none_kernel(tc, dy, w_words, w_scales, wgo, offs, out):
                 stop=False,
             )
 
-        def second_tier(c, lo, left_bf):
+        def second_tier(c, lo, left_bf, width=PIECE):
             nc.vector.quantize_mx(
-                out=r_codes[c][:, lo : lo + PIECE].bitcast(E4M3X4),
-                scales=r_plane[c][:, lo : lo + PIECE],
+                out=r_codes[c][:, lo : lo + width].bitcast(E4M3X4),
+                scales=r_plane[c][:, lo : lo + width],
                 in_=left_bf.rearrange("p j i -> p (j i)"),
             )
 
-        def residual_on_tensor(c, back, tag):
-            left_bf = keep.tile([P, CHUNK, PACK], BF16, name=f"left_bf{c}", tag=tag, align_bytes=64)
-            left_words = left_bf[:].rearrange("p j i -> p (j i)").bitcast(F32).rearrange("p (j u) -> p j u", u=2)
+        def negated(back):
             minus = [keep.tile([P, CHUNK], F32, name=f"minus{t}") for t in range(PACK)]
             for t in EYE_ORDER:
                 nc.scalar.activation(out=minus[t][:], in_=back[t][:], func=COPY, scale=-1.0)
+            return minus
+
+        def residual_on_tensor(c, minus, tag):
+            left_bf = keep.tile([P, CHUNK, PACK], BF16, name=f"left_bf{c}", tag=tag, align_bytes=64)
+            left_words = left_bf[:].rearrange("p j i -> p (j i)").bitcast(F32).rearrange("p (j u) -> p j u", u=2)
             for g in range(CHUNK // P):
                 h, lo = divmod(c * CHUNK + g * P, PIECE)
                 diff = psum.tile([P, PACK, P], F32, name=f"diff{g}", tag=f"bank{g}")
@@ -223,18 +227,24 @@ def tile_list_embg_tgq8_none_kernel(tc, dy, w_words, w_scales, wgo, offs, out):
         for u in range(CHUNK // PIECE):
             interleave(nc.scalar.copy, dy_bf_late[:, u * PIECE : (u + 1) * PIECE, :], raw[2 + u], 0, PIECE)
         left = keep.tile([P, PACK, CHUNK], BF16, name="left")
-        for t in EYE_ORDER:
+        for t in EYE_ORDER[:-1]:
             nc.vector.tensor_tensor(
                 out=left[:, t, :].rearrange("p (u j) -> p u j", j=PIECE),
                 in0=raw_chunk[0][:, :, t, :],
                 in1=back[t][:].rearrange("p (u j) -> p u j", j=PIECE),
                 op=SUB,
             )
+        t = EYE_ORDER[-1]
+        for h in (0, 1):
+            cols = slice(h * PIECE, (h + 1) * PIECE)
+            nc.vector.tensor_tensor(out=left[:, t, cols], in0=raw[h][:, t, :], in1=back[t][:, cols], op=SUB)
         left_bf0 = keep.tile([P, PIECE, PACK], BF16, name="left_bf0", tag="left_bf0", align_bytes=64)
-        interleave(nc.vector.tensor_copy, left_bf0, left[:, :, :PIECE], 0, PIECE)
+        for lo in (0, P):
+            interleave(nc.vector.tensor_copy, left_bf0, left[:, :, :PIECE], lo, lo + P)
         left_bf1 = shared.tile([P, PIECE, PACK], BF16, name="left_bf1", align_bytes=64, offset=4 * T)
         interleave(nc.scalar.copy, left_bf1, left[:, :, PIECE:], 0, PIECE)
-        second_tier(0, 0, left_bf0[:])
+        for lo in (0, P):
+            second_tier(0, lo, left_bf0[:, lo : lo + P, :], P)
         second_tier(0, PIECE, left_bf1[:])
         q_codes[1] = keep.tile([P, CHUNK], U32, name="q_codes1", tag="left_bf0", align_bytes=64)
         nc.vector.quantize_mx(
@@ -244,7 +254,7 @@ def tile_list_embg_tgq8_none_kernel(tc, dy, w_words, w_scales, wgo, offs, out):
         nc.gpsimd.memset(pages[2][:], 0.0)
         for b in range(BLOCKS):
             first_product(0, b, b)
-        second_product(0, 0, PIECE, 0, PIECE)
+        second_product(0, 0, P, 0, PIECE)
         dx00 = keep.tile([P, PIECE], F32, name="dx00", tag="page3", align_bytes=64)
         evacuate(0, 0, dx00[:], 0, PIECE)
         scatter(pages[0], dx00[:], 0, PIECE)
@@ -255,8 +265,9 @@ def tile_list_embg_tgq8_none_kernel(tc, dy, w_words, w_scales, wgo, offs, out):
             dx0 = keep.tile([P, CHUNK], F32, name=f"dx0{b}")
             evacuate(0, b, dx0[:])
             scatter(pages[b], dx0[:], 0, CHUNK)
-        back = dequantise(1)
-        residual_on_tensor(1, back, "left_bf_late")
+            if b == 1:
+                minus = negated(dequantise(1))
+        residual_on_tensor(1, minus, "left_bf_late")
         first_product(0, 0, 3)
         second_product(0, 0, PIECE, PIECE, CHUNK)
         dx00b = keep.tile([P, PIECE], F32, name="dx00b", align_bytes=64)

@@ -47,13 +47,13 @@ def tile_list_embg_tgq8_none_kernel(tc, dy, w_words, w_scales, wgo, offs, out):
         w_plane = keep.tile([P, N], U8, name="w_plane", align_bytes=64)
         wgo_sb = keep.tile([P, J], F32, name="wgo_sb")
         dy_rows = dy.rearrange("(p i) j -> p i j", i=PACK)
-        raw_chunk = [keep.tile([P, CHUNK // PIECE, PACK, PIECE], F32, name=f"raw{c}") for c in range(CHUNKS)]
-        raw = [raw_chunk[h // 2][:, h % 2, :, :] for h in range(J // PIECE)]
+        raw_first = keep.tile([P, PACK, CHUNK], F32, name="raw_first")
+        raw_late = keep.tile([P, CHUNK // PIECE, PACK, PIECE], F32, name="raw_late")
+        raw = [None, None, raw_late[:, 0, :, :], raw_late[:, 1, :, :]]
 
         nc.vector.memset(w_plane[:].bitcast(I32), 0)
-        nc.sync.dma_start(out=raw[0], in_=dy_rows[:, :, :PIECE])
-        for lo in (0, P):
-            nc.sync.dma_start(out=raw[1][:, :, lo : lo + P], in_=dy_rows[:, :, PIECE + lo : PIECE + lo + P])
+        for lo, hi in ((0, 3 * P), (3 * P, CHUNK)):
+            nc.sync.dma_start(out=raw_first[:, :, lo:hi], in_=dy_rows[:, :, lo:hi])
         for h in (2, 3):
             nc.sync.dma_start(out=raw[h], in_=dy_rows[:, :, h * PIECE : (h + 1) * PIECE])
         nc.sync.dma_start(out=w_codes[:].bitcast(I32), in_=w_words[0].rearrange("p n i -> p (n i)").bitcast(I32))
@@ -86,7 +86,7 @@ def tile_list_embg_tgq8_none_kernel(tc, dy, w_words, w_scales, wgo, offs, out):
         nc.vector.quantize_mx(out=eye_last[:].bitcast(E4M3X4), scales=eye_plane[:, 3 * P :], in_=marks[:, :K])
         eye_rest = shared.tile([P, PACK - 1, K], BF16, name="eye_rest", align_bytes=64, offset=2048)
         for t in range(PACK - 1):
-            copy = nc.vector.tensor_copy if t == 0 else nc.scalar.copy
+            copy = nc.vector.tensor_copy if t < 2 else nc.scalar.copy
             copy(out=eye_rest[:, t, :], in_=marks[:, PACK - 1 - t : K + PACK - 1 - t])
         eye = keep.tile([P, P], F32, name="eye")
         nc.scalar.copy(out=eye[:], in_=diagonal)
@@ -99,13 +99,11 @@ def tile_list_embg_tgq8_none_kernel(tc, dy, w_words, w_scales, wgo, offs, out):
         acc = {}
         dx = {}
 
-        def first_tier(copy, j, width, dy_bf):
-            h, lo = divmod(j, PIECE)
-            interleave(copy, dy_bf, raw[h][:, :, lo : lo + width], 0, width)
+        def first_tier(lo, hi, dy_bf):
             nc.vector.quantize_mx(
-                out=q_codes[0][:, j : j + width].bitcast(E5M2X4),
-                scales=q_plane[0][:, j : j + width],
-                in_=dy_bf[:].rearrange("p j i -> p (j i)"),
+                out=q_codes[0][:, lo:hi].bitcast(E5M2X4),
+                scales=q_plane[0][:, lo:hi],
+                in_=dy_bf.rearrange("p j i -> p (j i)"),
             )
 
         def dequantise(c):
@@ -203,16 +201,18 @@ def tile_list_embg_tgq8_none_kernel(tc, dy, w_words, w_scales, wgo, offs, out):
                 op=MULT,
             )
 
-        dy_bf0 = keep.tile([P, PIECE, PACK], BF16, name="dy_bf0", align_bytes=64)
-        first_tier(nc.vector.tensor_copy, 0, PIECE, dy_bf0)
-        dy_bf1 = keep.tile([P, P, PACK], BF16, name="dy_bf1", align_bytes=64)
-        first_tier(nc.scalar.copy, PIECE, P, dy_bf1)
-        dy_bf2 = keep.tile([P, P, PACK], BF16, name="dy_bf2", tag="eye_first", align_bytes=64)
-        first_tier(nc.vector.tensor_copy, PIECE + P, P, dy_bf2)
+        dy_bf0 = shared.tile([P, 3 * P, PACK], BF16, name="dy_bf0", align_bytes=64, offset=8 * T + 1024)
+        interleave(nc.vector.tensor_copy, dy_bf0, raw_first, 0, 192)
+        interleave(nc.scalar.copy, dy_bf0, raw_first, 192, 3 * P)
+        first_tier(0, P, dy_bf0[:, :P, :])
+        dy_bf2 = shared.tile([P, P, PACK], BF16, name="dy_bf2", align_bytes=64, offset=8 * T)
+        interleave(nc.vector.tensor_copy, dy_bf2, raw_first[:, :, 3 * P :], 0, P)
+        first_tier(P, 3 * P, dy_bf0[:, P:, :])
+        first_tier(3 * P, CHUNK, dy_bf2[:])
         pages[1] = keep.tile([P, T], F32, name="page1", align_bytes=64)
         for lo in range(0, T, PIECE):
             nc.vector.memset(pages[1][:, lo : lo + PIECE], 0.0)
-        eye_first = keep.tile([P, 3 * P], U32, name="eye_first", tag="eye_first", align_bytes=64)
+        eye_first = shared.tile([P, 3 * P], U32, name="eye_first", align_bytes=64, offset=8 * T)
         eye_codes = [eye_first[:, t * P : (t + 1) * P] for t in range(PACK - 1)] + [eye_last[:]]
         nc.vector.quantize_mx(out=eye_codes[0].bitcast(E4M3X4), scales=eye_plane[:, :P], in_=eye_rest[:, 0, :])
         nc.vector.quantize_mx(
@@ -228,16 +228,11 @@ def tile_list_embg_tgq8_none_kernel(tc, dy, w_words, w_scales, wgo, offs, out):
             interleave(nc.scalar.copy, dy_bf_late[:, u * PIECE : (u + 1) * PIECE, :], raw[2 + u], 0, PIECE)
         left = keep.tile([P, PACK, CHUNK], BF16, name="left")
         for t in EYE_ORDER[:-1]:
-            nc.vector.tensor_tensor(
-                out=left[:, t, :].rearrange("p (u j) -> p u j", j=PIECE),
-                in0=raw_chunk[0][:, :, t, :],
-                in1=back[t][:].rearrange("p (u j) -> p u j", j=PIECE),
-                op=SUB,
-            )
+            nc.vector.tensor_tensor(out=left[:, t, :], in0=raw_first[:, t, :], in1=back[t][:], op=SUB)
         t = EYE_ORDER[-1]
         for h in (0, 1):
             cols = slice(h * PIECE, (h + 1) * PIECE)
-            nc.vector.tensor_tensor(out=left[:, t, cols], in0=raw[h][:, t, :], in1=back[t][:, cols], op=SUB)
+            nc.vector.tensor_tensor(out=left[:, t, cols], in0=raw_first[:, t, cols], in1=back[t][:, cols], op=SUB)
         left_bf0 = keep.tile([P, PIECE, PACK], BF16, name="left_bf0", tag="left_bf0", align_bytes=64)
         for lo in (0, P):
             interleave(nc.vector.tensor_copy, left_bf0, left[:, :, :PIECE], lo, lo + P)

@@ -74,7 +74,7 @@ def tile_list_embg_tgq8_none_kernel(tc, dy, w_words, w_scales, wgo, offs, out):
         nc.vector.transpose(out=lane[:], in_=ramp[:, 0:32])
         quadrant = keep.tile([P, 1], F32, name="quadrant")
         for q in range(4):
-            nc.vector.memset(quadrant[32 * q : 32 * (q + 1), :], 32.0 * q)
+            nc.gpsimd.memset(quadrant[32 * q : 32 * (q + 1), :], 32.0 * q)
         marks = keep.tile([P, K + PACK], BF16, name="marks", align_bytes=64)
         nc.vector.memset(marks[:].bitcast(I32), 0)
         diagonal = marks[:, PACK - 1 : K + PACK - 1 : PACK]
@@ -120,16 +120,17 @@ def tile_list_embg_tgq8_none_kernel(tc, dy, w_words, w_scales, wgo, offs, out):
                 )
             return back
 
-        def first_product(c, b, bank):
-            acc[c, b] = psum.tile([P, CHUNK], F32, name=f"acc{c}_{b}", tag=f"bank{bank}")
+        def first_product(c, b, bank=None):
+            if bank is not None:
+                acc[c, b] = psum.tile([P, CHUNK], F32, name=f"acc{c}_{b}", tag=f"bank{bank}")
             nc.tensor.matmul_mx(
                 out=acc[c, b][:],
                 lhsT=w_codes[:, b * P : (b + 1) * P].bitcast(E4M3X4),
                 lhsT_scale=w_plane[:, b * P : (b + 1) * P],
                 rhs=q_codes[c][:].bitcast(E5M2X4),
                 rhs_scale=q_plane[c][:],
-                start=True,
-                stop=False,
+                start=bank is not None,
+                stop=bank is None,
             )
 
         def second_tier(c, lo, left_bf, width=PIECE):
@@ -150,7 +151,7 @@ def tile_list_embg_tgq8_none_kernel(tc, dy, w_words, w_scales, wgo, offs, out):
             left_words = left_bf[:].rearrange("p j i -> p (j i)").bitcast(F32).rearrange("p (j u) -> p j u", u=2)
             for g in range(CHUNK // P):
                 h, lo = divmod(c * CHUNK + g * P, PIECE)
-                diff = psum.tile([P, PACK, P], F32, name=f"diff{g}", tag=f"bank{g}")
+                diff = psum.tile([P, PACK, P], F32, name=f"diff{g}", tag=f"bank{(0, 1, 7, 4)[g]}")
                 for t in range(PACK):
                     nc.tensor.matmul(
                         diff[:, t, :], raw[h][:, t, lo : lo + P], eye[:], start=(t == 0), stop=False, is_transpose=True
@@ -167,7 +168,7 @@ def tile_list_embg_tgq8_none_kernel(tc, dy, w_words, w_scales, wgo, offs, out):
                 pairs = keep.tile([P, 2, P, 2], BF16, name=f"pairs{g}", tag=f"pairs{g}", align_bytes=64)
                 nc.scalar.copy(out=pairs[:], in_=diff[:].rearrange("j (u e) p -> j u p e", e=2))
                 pair_words = pairs[:].rearrange("j u p e -> j (u p e)").bitcast(F32)
-                turned = psum.tile([P, 2, P], F32, name=f"turned{g}", tag=f"bank{5 + g % 3}")
+                turned = psum.tile([P, 2, P], F32, name=f"turned{g}", tag=f"bank{5 + g % 2}")
                 for u in range(2):
                     nc.tensor.transpose(turned[:, u, :], pair_words[:, u * P : (u + 1) * P], eye[:])
                 nc.scalar.copy(out=left_words[:, g * P : (g + 1) * P, :], in_=turned[:].rearrange("p u j -> p j u"))
@@ -256,23 +257,34 @@ def tile_list_embg_tgq8_none_kernel(tc, dy, w_words, w_scales, wgo, offs, out):
         pages[3] = keep.tile([P, T], F32, name="page3", tag="page3", align_bytes=64)
         nc.gpsimd.memset(pages[3][:], 0.0)
         for b in range(1, BLOCKS):
-            second_product(0, b, CHUNK)
+            second_product(0, b, PIECE if b == 1 else CHUNK)
             dx0 = keep.tile([P, CHUNK], F32, name=f"dx0{b}")
             evacuate(0, b, dx0[:])
             scatter(pages[b], dx0[:], 0, CHUNK)
             if b == 1:
                 minus = negated(dequantise(1))
         residual_on_tensor(1, minus, "left_bf_late")
-        first_product(0, 0, 3)
+        first_product(0, 0, 4)
         second_product(0, 0, PIECE, PIECE, CHUNK)
         dx00b = keep.tile([P, PIECE], F32, name="dx00b", align_bytes=64)
         evacuate(0, 0, dx00b[:], PIECE, CHUNK)
         scatter(pages[0], dx00b[:], PIECE, PIECE)
-        last = (1, 2, 3, 0)
-        for b in last:
-            first_product(1, b, (4, 0, 1, 2)[b])
-        for b in last:
-            second_product(1, b, PIECE if b == last[0] else CHUNK)
+        for b, bank in ((1, 6), (2, 0), (3, 1), (0, 2)):
+            if b == 1:
+                first_product(1, b, bank)
+                second_product(1, b, PIECE)
+            else:
+                acc[1, b] = psum.tile([P, CHUNK], F32, name=f"acc1_{b}", tag=f"bank{bank}")
+                nc.tensor.matmul_mx(
+                    out=acc[1, b][:],
+                    lhsT=w_codes[:, b * P : (b + 1) * P].bitcast(E4M3X4),
+                    lhsT_scale=w_plane[:, b * P : (b + 1) * P],
+                    rhs=r_codes[1][:].bitcast(E4M3X4),
+                    rhs_scale=r_plane[1][:],
+                    start=True,
+                    stop=False,
+                )
+                first_product(1, b)
             dx1 = keep.tile([P, CHUNK], F32, name=f"dx1{b}")
             evacuate(1, b, dx1[:])
             scatter(pages[b], dx1[:], CHUNK, CHUNK)

@@ -21,18 +21,14 @@ COPY = mybir.ActivationFunctionType.Copy
 
 P = 128
 PACK = 4
-CHUNK = 512
 PIECE = 256
+HALF = 128
 BLOCKS = N // P
-CHUNKS = J // CHUNK
-EYE_ORDER = (3, 0, 1, 2)
+PIECES = J // PIECE
 
 
-def interleave(copy, dst, src, lo, hi):
-    copy(
-        out=dst[:, lo:hi, :].rearrange("p (c j) i -> p c i j", j=4),
-        in_=src[:, :, lo:hi].rearrange("p i (c j) -> p c i j", j=4),
-    )
+def by_fours(ap, order):
+    return ap.rearrange(order + " -> p c i j", j=4)
 
 
 def tile_list_embg_tgq8_none_kernel(tc, dy, w_words, w_scales, wgo, offs, out):
@@ -47,245 +43,218 @@ def tile_list_embg_tgq8_none_kernel(tc, dy, w_words, w_scales, wgo, offs, out):
         w_plane = keep.tile([P, N], U8, name="w_plane", align_bytes=64)
         wgo_sb = keep.tile([P, J], F32, name="wgo_sb")
         dy_rows = dy.rearrange("(p i) j -> p i j", i=PACK)
-        raw_first = keep.tile([P, PACK, CHUNK], F32, name="raw_first")
-        raw_late = keep.tile([P, CHUNK // PIECE, PACK, PIECE], F32, name="raw_late")
-        raw = [None, None, raw_late[:, 0, :, :], raw_late[:, 1, :, :]]
+        loads = [(0, 1), (1, 2), (2, 4), (4, 6), (6, 8)]
+        loaded = [keep.tile([P, PACK, (hi - lo) * HALF], F32, name=f"raw{lo}") for lo, hi in loads]
+        raw = []
+        for (lo, hi), tile in zip(loads, loaded):
+            raw.extend(tile[:, :, g * HALF : (g + 1) * HALF] for g in range(hi - lo))
 
-        nc.vector.memset(w_plane[:].bitcast(I32), 0)
-        for lo, hi in ((0, 3 * P), (3 * P, CHUNK)):
-            nc.sync.dma_start(out=raw_first[:, :, lo:hi], in_=dy_rows[:, :, lo:hi])
-        for h in (2, 3):
-            nc.sync.dma_start(out=raw[h], in_=dy_rows[:, :, h * PIECE : (h + 1) * PIECE])
+        def load_dy(n):
+            lo, hi = loads[n]
+            nc.sync.dma_start(out=loaded[n][:], in_=dy_rows[:, :, lo * HALF : hi * HALF])
+
+        nc.gpsimd.memset(w_plane[:].bitcast(I32), 0)
+        for n in range(3):
+            load_dy(n)
         nc.sync.dma_start(out=w_codes[:].bitcast(I32), in_=w_words[0].rearrange("p n i -> p (n i)").bitcast(I32))
         for q in range(4):
-            queue = nc.scalar if q < 2 else nc.sync
-            queue.dma_start(
+            nc.scalar.dma_start(
                 out=w_plane[32 * q : 32 * q + 4, :].bitcast(I32), in_=w_scales[0, 4 * q : 4 * q + 4, :].bitcast(I32)
             )
         nc.sync.dma_start(offsets[:], offs)
-        for lo in range(0, J, CHUNK):
-            nc.sync.dma_start(out=wgo_sb[:, lo : lo + CHUNK], in_=wgo[:, lo : lo + CHUNK])
+        nc.sync.dma_start(out=wgo_sb[:, :PIECE], in_=wgo[:, :PIECE])
+        load_dy(3)
+        load_dy(4)
+        nc.sync.dma_start(out=wgo_sb[:, PIECE:], in_=wgo[:, PIECE:])
 
-        ones = keep.tile([P, P], F32, name="ones")
-        nc.vector.memset(ones[:], 1.0)
-        ramp = keep.tile([P, P], F32, name="ramp", align_bytes=64)
-        nc.vector.tensor_tensor_scan(out=ramp[:], data0=ones[:], data1=ones[:], initial=-1.0, op0=MULT, op1=ADD)
-        lane = keep.tile([P, 32], F32, name="lane", align_bytes=64)
-        nc.vector.transpose(out=lane[:], in_=ramp[:, 0:32])
-        quadrant = keep.tile([P, 1], F32, name="quadrant")
-        for q in range(4):
-            nc.gpsimd.memset(quadrant[32 * q : 32 * (q + 1), :], 32.0 * q)
-        marks = keep.tile([P, K + PACK], BF16, name="marks", align_bytes=64)
-        nc.vector.memset(marks[:].bitcast(I32), 0)
-        diagonal = marks[:, PACK - 1 : K + PACK - 1 : PACK]
-        nc.vector.tensor_scalar(
-            out=diagonal, in0=ramp[:], scalar1=lane[:, 0:1], scalar2=quadrant[:], op0=SUB, op1=IS_EQUAL
-        )
-        eye_last = keep.tile([P, P], U32, name="eye_last", align_bytes=64)
-        eye_plane = keep.tile([P, K], U8, name="eye_plane", align_bytes=64)
-        nc.vector.quantize_mx(out=eye_last[:].bitcast(E4M3X4), scales=eye_plane[:, 3 * P :], in_=marks[:, :K])
-        eye_rest = shared.tile([P, PACK - 1, K], BF16, name="eye_rest", align_bytes=64, offset=2048)
-        for t in range(PACK - 1):
-            copy = nc.vector.tensor_copy if t < 2 else nc.scalar.copy
-            copy(out=eye_rest[:, t, :], in_=marks[:, PACK - 1 - t : K + PACK - 1 - t])
+        ramp = keep.tile([P, P], F32, name="ramp")
+        nc.gpsimd.iota(ramp[:], [[1, P]], base=0, channel_multiplier=-1, allow_small_or_imprecise_dtypes=True)
+        marks = shared.tile([P, K], BF16, name="marks", align_bytes=64, offset=8 * T)
+        nc.gpsimd.memset(marks[:].bitcast(I32), 0)
+        diagonal = marks[:, 0:K:PACK]
+        nc.vector.tensor_scalar(out=diagonal, in0=ramp[:], scalar1=0.0, scalar2=None, op0=IS_EQUAL)
+        eye_first = keep.tile([P, P], U32, name="eye_first", align_bytes=64)
+        eye_rest = keep.tile([P, (PACK - 1) * P], U32, name="eye_rest", align_bytes=64)
+        eye_plane = keep.tile([P, P], U8, name="eye_plane", align_bytes=64)
+        nc.vector.memset(eye_rest[:], 0)
+        nc.vector.quantize_mx(out=eye_first[:].bitcast(E4M3X4), scales=eye_plane[:], in_=marks[:])
+        eye_codes = [eye_first[:]] + [eye_rest[:, t * P : (t + 1) * P] for t in range(PACK - 1)]
+        for t in range(1, PACK):
+            nc.vector.tensor_copy(out=eye_codes[t].bitcast(U8)[:, t:K:PACK], in_=eye_first[:].bitcast(U8)[:, 0:K:PACK])
         eye = keep.tile([P, P], F32, name="eye")
-        nc.scalar.copy(out=eye[:], in_=diagonal)
+        nc.gpsimd.tensor_scalar(out=eye[:], in0=ramp[:], scalar1=0.0, scalar2=None, op0=IS_EQUAL)
+        zeros = keep.tile([P, HALF], F32, name="zeros")
+        nc.gpsimd.memset(zeros[:], 0.0)
+        pages = [keep.tile([P, T], F32, name="page0", align_bytes=64), None, None, None]
 
-        q_codes = [keep.tile([P, CHUNK], U32, name="q_codes0", align_bytes=64), None]
-        q_plane = [keep.tile([P, CHUNK], U8, name=f"q_plane{c}", align_bytes=64) for c in range(CHUNKS)]
-        r_codes = [keep.tile([P, CHUNK], U32, name=f"r_codes{c}", align_bytes=64) for c in range(CHUNKS)]
-        r_plane = [keep.tile([P, CHUNK], U8, name=f"r_plane{c}", align_bytes=64) for c in range(CHUNKS)]
-        pages = [None] * BLOCKS
-        acc = {}
-        dx = {}
+        q_codes = [keep.tile([P, HALF], U32, name="q_first", align_bytes=64), None, None, None]
+        q_plane = keep.tile([P, J], U8, name="q_plane", align_bytes=64)
+        r_codes = [keep.tile([P, n * HALF], U32, name=f"r_codes{h}", align_bytes=64) for h, n in enumerate((1, 1, 2, 4))]
+        r_plane = keep.tile([P, J], U8, name="r_plane", align_bytes=64)
 
-        def first_tier(lo, hi, dy_bf):
+        first = (q_codes, q_plane, E5M2X4)
+        second = (r_codes, r_plane, E4M3X4)
+
+        def words(codes, j, width):
+            starts = (0, HALF, PIECE, 2 * PIECE)
+            h = max(n for n, start in enumerate(starts) if start <= j)
+            lo = j - starts[h]
+            return codes[h][:, lo : lo + width]
+
+        def bank(number, shape, name):
+            return psum.tile(shape, F32, name=name, tag=f"bank{number}")
+
+        def cast(copy, dst, src):
+            copy(out=by_fours(dst, "p (c j) i"), in_=by_fours(src, "p i (c j)"))
+
+        def quantise(codes, plane, fmt, j, values):
+            width = values.shape[1]
             nc.vector.quantize_mx(
-                out=q_codes[0][:, lo:hi].bitcast(E5M2X4),
-                scales=q_plane[0][:, lo:hi],
-                in_=dy_bf.rearrange("p j i -> p (j i)"),
+                out=words(codes, j, width).bitcast(fmt),
+                scales=plane[:, j : j + width],
+                in_=values.rearrange("p j i -> p (j i)"),
             )
 
-        def dequantise(c):
-            back = [psum.tile([P, CHUNK], F32, name=f"back{c}_{t}", tag=f"bank{4 * c + t}") for t in range(PACK)]
-            for t in EYE_ORDER:
+        def dequantise(j, number):
+            back = bank(number, [P, PACK, HALF], f"back{j}")
+            for t in range(PACK):
                 nc.tensor.matmul_mx(
-                    out=back[t][:],
+                    out=back[:, t, :],
                     lhsT=eye_codes[t].bitcast(E4M3X4),
-                    lhsT_scale=eye_plane[:, t * P : (t + 1) * P],
-                    rhs=q_codes[c][:].bitcast(E5M2X4),
-                    rhs_scale=q_plane[c][:],
+                    lhsT_scale=eye_plane[:],
+                    rhs=words(q_codes, j, HALF).bitcast(E5M2X4),
+                    rhs_scale=q_plane[:, j : j + HALF],
                     start=True,
                     stop=True,
                 )
             return back
 
-        def first_product(c, b, bank=None):
-            if bank is not None:
-                acc[c, b] = psum.tile([P, CHUNK], F32, name=f"acc{c}_{b}", tag=f"bank{bank}")
-            nc.tensor.matmul_mx(
-                out=acc[c, b][:],
-                lhsT=w_codes[:, b * P : (b + 1) * P].bitcast(E4M3X4),
-                lhsT_scale=w_plane[:, b * P : (b + 1) * P],
-                rhs=q_codes[c][:].bitcast(E5M2X4),
-                rhs_scale=q_plane[c][:],
-                start=bank is not None,
-                stop=bank is None,
-            )
+        def product(b, j, widths, number, tiers):
+            acc = bank(number, [P, sum(widths)], f"acc{b}_{j}")
+            passes = []
+            for codes, plane, fmt in tiers:
+                for n, cols in enumerate(widths):
+                    passes.append((codes, plane, fmt, sum(widths[:n]), cols))
+            for n, (codes, plane, fmt, lo, cols) in enumerate(passes):
+                nc.tensor.matmul_mx(
+                    out=acc[:, lo : lo + cols],
+                    lhsT=w_codes[:, b * P : (b + 1) * P].bitcast(E4M3X4),
+                    lhsT_scale=w_plane[:, b * P : (b + 1) * P],
+                    rhs=words(codes, j + lo, cols).bitcast(fmt),
+                    rhs_scale=plane[:, j + lo : j + lo + cols],
+                    start=(n == 0),
+                    stop=(n == len(passes) - 1),
+                )
+            return acc
 
-        def second_tier(c, lo, left_bf, width=PIECE):
-            nc.vector.quantize_mx(
-                out=r_codes[c][:, lo : lo + width].bitcast(E4M3X4),
-                scales=r_plane[c][:, lo : lo + width],
-                in_=left_bf.rearrange("p j i -> p (j i)"),
-            )
+        def window(b, j, width):
+            return pages[b][:].indirect(offsets[:, j // 16 : (j + width) // 16])
 
-        def negated(back):
-            minus = [keep.tile([P, CHUNK], F32, name=f"minus{t}") for t in range(PACK)]
-            for t in EYE_ORDER:
-                nc.scalar.activation(out=minus[t][:], in_=back[t][:], func=COPY, scale=-1.0)
-            return minus
+        def weigh(b, j, number):
+            acc = product(b, j, [HALF], number, [first, second])
+            weighted = keep.tile([P, HALF], F32, name=f"weighted{b}_{j}")
+            nc.vector.tensor_tensor(out=weighted[:], in0=acc[:], in1=wgo_sb[:, j : j + HALF], op=MULT)
+            return weighted
 
-        def residual_on_tensor(c, minus, tag):
-            left_bf = keep.tile([P, CHUNK, PACK], BF16, name=f"left_bf{c}", tag=tag, align_bytes=64)
-            left_words = left_bf[:].rearrange("p j i -> p (j i)").bitcast(F32).rearrange("p (j u) -> p j u", u=2)
-            for g in range(CHUNK // P):
-                h, lo = divmod(c * CHUNK + g * P, PIECE)
-                diff = psum.tile([P, PACK, P], F32, name=f"diff{g}", tag=f"bank{(0, 1, 7, 4)[g]}")
-                for t in range(PACK):
+        def place_weighted(b, j, weighted):
+            nc.vector.tensor_tensor(out=window(b, j, HALF), in0=weighted[:], in1=zeros[:], op=ADD)
+
+        def clear(b):
+            for lo in range(0, T, 2 * PIECE):
+                nc.vector.memset(pages[b][:, lo : lo + 2 * PIECE].bitcast(I32), 0)
+
+        def place(b, j, widths, number):
+            width = sum(widths)
+            acc = product(b, j, widths, number, [second, first])
+            dx = keep.tile([P, width], F32, name=f"dx{b}_{j}")
+            nc.scalar.copy(out=dx[:], in_=acc[:])
+            nc.vector.tensor_tensor(out=window(b, j, width), in0=dx[:], in1=wgo_sb[:, j : j + width], op=MULT)
+            if j + width == J:
+                nc.sync.dma_start(out=out[b * P : (b + 1) * P, :], in_=pages[b][:])
+
+        def residual_on_tensor(units, back_banks, diff_banks, turn_banks, left=None):
+            if left is None:
+                left = keep.tile([P, PIECE, PACK], BF16, name=f"left{units[0]}", align_bytes=64)
+            left_words = left[:].rearrange("p j i -> p (j i)").bitcast(F32).rearrange("p (j u) -> p j u", u=2)
+            minus = [keep.tile([P, PACK, HALF], F32, name=f"minus{x}") for x in units]
+            pairs = [keep.tile([P, 2, P, 2], BF16, name=f"pairs{x}", align_bytes=64) for x in units]
+            for g, x in enumerate(units):
+                back = dequantise(x * HALF, back_banks[g])
+                nc.scalar.activation(out=minus[g][:], in_=back[:], func=COPY, scale=-1.0)
+            for g, x in enumerate(units):
+                diff = bank(diff_banks[g], [P, PACK, P], f"diff{x}")
+                terms = [raw[x][:, t, :] for t in range(PACK)] + [minus[g][:, t, :] for t in range(PACK)]
+                for n, term in enumerate(terms):
                     nc.tensor.matmul(
-                        diff[:, t, :], raw[h][:, t, lo : lo + P], eye[:], start=(t == 0), stop=False, is_transpose=True
+                        diff[:, n % PACK, :], term, eye[:], start=(n == 0), stop=(n == len(terms) - 1), is_transpose=True
                     )
-                for t in range(PACK):
-                    nc.tensor.matmul(
-                        diff[:, t, :],
-                        minus[t][:, g * P : (g + 1) * P],
-                        eye[:],
-                        start=False,
-                        stop=(t == PACK - 1),
-                        is_transpose=True,
-                    )
-                pairs = keep.tile([P, 2, P, 2], BF16, name=f"pairs{g}", tag=f"pairs{g}", align_bytes=64)
-                nc.scalar.copy(out=pairs[:], in_=diff[:].rearrange("j (u e) p -> j u p e", e=2))
-                pair_words = pairs[:].rearrange("j u p e -> j (u p e)").bitcast(F32)
-                turned = psum.tile([P, 2, P], F32, name=f"turned{g}", tag=f"bank{5 + g % 2}")
+                nc.scalar.copy(out=pairs[g][:], in_=diff[:].rearrange("j (u e) p -> j u p e", e=2))
+            for g, x in enumerate(units):
+                pair_words = pairs[g][:].rearrange("j u p e -> j (u p e)").bitcast(F32)
+                turned = bank(turn_banks[g], [P, 2, P], f"turned{x}")
                 for u in range(2):
                     nc.tensor.transpose(turned[:, u, :], pair_words[:, u * P : (u + 1) * P], eye[:])
-                nc.scalar.copy(out=left_words[:, g * P : (g + 1) * P, :], in_=turned[:].rearrange("p u j -> p j u"))
-            for lo in range(0, CHUNK, PIECE):
-                nc.vector.quantize_mx(
-                    out=r_codes[c][:, lo : lo + PIECE].bitcast(E4M3X4),
-                    scales=r_plane[c][:, lo : lo + PIECE],
-                    in_=left_bf[:, lo : lo + PIECE, :].rearrange("p j i -> p (j i)"),
+                nc.scalar.copy(
+                    out=left_words[:, g * HALF : (g + 1) * HALF, :], in_=turned[:].rearrange("p u j -> p j u")
                 )
+            quantise(r_codes, r_plane, E4M3X4, units[0] * HALF, left[:])
 
-        def second_product(c, b, width, first=0, last=CHUNK):
-            for lo in range(first, last, width):
-                nc.tensor.matmul_mx(
-                    out=acc[c, b][:, lo : lo + width],
-                    lhsT=w_codes[:, b * P : (b + 1) * P].bitcast(E4M3X4),
-                    lhsT_scale=w_plane[:, b * P : (b + 1) * P],
-                    rhs=r_codes[c][:, lo : lo + width].bitcast(E4M3X4),
-                    rhs_scale=r_plane[c][:, lo : lo + width],
-                    start=False,
-                    stop=(lo + width == last),
-                )
+        def first_tier(copy, units, rounded=None):
+            if rounded is None:
+                rounded = keep.tile([P, len(units) * HALF, PACK], BF16, name=f"rounded{units[0]}", align_bytes=64)
+            for g, x in enumerate(units):
+                cast(copy, rounded[:, g * HALF : (g + 1) * HALF, :], raw[x])
+            quantise(q_codes, q_plane, E5M2X4, units[0] * HALF, rounded[:])
 
-        def evacuate(c, b, dst, lo=0, hi=CHUNK):
-            nc.scalar.copy(out=dst, in_=acc[c, b][:, lo:hi])
-
-        def scatter(page, values, j, width):
+        def residual_on_vector(x, back, left):
             nc.vector.tensor_tensor(
-                out=page[:].indirect(offsets[:, j // 16 : (j + width) // 16]),
-                in0=values,
-                in1=wgo_sb[:, j : j + width],
-                op=MULT,
+                out=by_fours(left[:], "p (c j) i"),
+                in0=by_fours(raw[x], "p i (c j)"),
+                in1=by_fours(back[:], "p i (c j)"),
+                op=SUB,
             )
+            quantise(r_codes, r_plane, E4M3X4, x * HALF, left[:])
 
-        dy_bf0 = shared.tile([P, 3 * P, PACK], BF16, name="dy_bf0", align_bytes=64, offset=8 * T + 1024)
-        interleave(nc.vector.tensor_copy, dy_bf0, raw_first, 0, 192)
-        interleave(nc.scalar.copy, dy_bf0, raw_first, 192, 3 * P)
-        first_tier(0, P, dy_bf0[:, :P, :])
-        dy_bf2 = shared.tile([P, P, PACK], BF16, name="dy_bf2", align_bytes=64, offset=8 * T)
-        interleave(nc.vector.tensor_copy, dy_bf2, raw_first[:, :, 3 * P :], 0, P)
-        first_tier(P, 3 * P, dy_bf0[:, P:, :])
-        first_tier(3 * P, CHUNK, dy_bf2[:])
-        pages[1] = keep.tile([P, T], F32, name="page1", align_bytes=64)
-        for lo in range(0, T, PIECE):
-            nc.vector.memset(pages[1][:, lo : lo + PIECE], 0.0)
-        eye_first = shared.tile([P, 3 * P], U32, name="eye_first", align_bytes=64, offset=8 * T)
-        eye_codes = [eye_first[:, t * P : (t + 1) * P] for t in range(PACK - 1)] + [eye_last[:]]
-        nc.vector.quantize_mx(out=eye_codes[0].bitcast(E4M3X4), scales=eye_plane[:, :P], in_=eye_rest[:, 0, :])
-        nc.vector.quantize_mx(
-            out=eye_first[:, P:].bitcast(E4M3X4),
-            scales=eye_plane[:, P : 3 * P],
-            in_=eye_rest[:, 1:, :].rearrange("p t m -> p (t m)"),
-        )
-        back = dequantise(0)
-        pages[0] = shared.tile([P, T], F32, name="page0", align_bytes=64, offset=0)
-        nc.gpsimd.memset(pages[0][:], 0.0)
-        dy_bf_late = shared.tile([P, CHUNK, PACK], BF16, name="dy_bf_late", align_bytes=64, offset=4 * T + 2048)
-        for u in range(CHUNK // PIECE):
-            interleave(nc.scalar.copy, dy_bf_late[:, u * PIECE : (u + 1) * PIECE, :], raw[2 + u], 0, PIECE)
-        left = keep.tile([P, PACK, CHUNK], BF16, name="left")
-        for t in EYE_ORDER[:-1]:
-            nc.vector.tensor_tensor(out=left[:, t, :], in0=raw_first[:, t, :], in1=back[t][:], op=SUB)
-        t = EYE_ORDER[-1]
-        for h in (0, 1):
-            cols = slice(h * PIECE, (h + 1) * PIECE)
-            nc.vector.tensor_tensor(out=left[:, t, cols], in0=raw_first[:, t, cols], in1=back[t][:, cols], op=SUB)
-        left_bf0 = keep.tile([P, PIECE, PACK], BF16, name="left_bf0", tag="left_bf0", align_bytes=64)
-        for lo in (0, P):
-            interleave(nc.vector.tensor_copy, left_bf0, left[:, :, :PIECE], lo, lo + P)
-        left_bf1 = shared.tile([P, PIECE, PACK], BF16, name="left_bf1", align_bytes=64, offset=4 * T)
-        interleave(nc.scalar.copy, left_bf1, left[:, :, PIECE:], 0, PIECE)
-        for lo in (0, P):
-            second_tier(0, lo, left_bf0[:, lo : lo + P, :], P)
-        second_tier(0, PIECE, left_bf1[:])
-        q_codes[1] = keep.tile([P, CHUNK], U32, name="q_codes1", tag="left_bf0", align_bytes=64)
-        nc.vector.quantize_mx(
-            out=q_codes[1][:].bitcast(E5M2X4), scales=q_plane[1][:], in_=dy_bf_late[:].rearrange("p j i -> p (j i)")
-        )
-        pages[2] = shared.tile([P, T], F32, name="page2", align_bytes=64, offset=4 * T)
-        nc.gpsimd.memset(pages[2][:], 0.0)
-        for b in range(BLOCKS):
-            first_product(0, b, b)
-        second_product(0, 0, P, 0, PIECE)
-        dx00 = keep.tile([P, PIECE], F32, name="dx00", tag="page3", align_bytes=64)
-        evacuate(0, 0, dx00[:], 0, PIECE)
-        scatter(pages[0], dx00[:], 0, PIECE)
-        pages[3] = keep.tile([P, T], F32, name="page3", tag="page3", align_bytes=64)
-        nc.gpsimd.memset(pages[3][:], 0.0)
-        for b in range(1, BLOCKS):
-            second_product(0, b, PIECE if b == 1 else CHUNK)
-            dx0 = keep.tile([P, CHUNK], F32, name=f"dx0{b}")
-            evacuate(0, b, dx0[:])
-            scatter(pages[b], dx0[:], 0, CHUNK)
-            if b == 1:
-                minus = negated(dequantise(1))
-        residual_on_tensor(1, minus, "left_bf_late")
-        first_product(0, 0, 4)
-        second_product(0, 0, PIECE, PIECE, CHUNK)
-        dx00b = keep.tile([P, PIECE], F32, name="dx00b", align_bytes=64)
-        evacuate(0, 0, dx00b[:], PIECE, CHUNK)
-        scatter(pages[0], dx00b[:], PIECE, PIECE)
-        for b, bank in ((1, 6), (2, 0), (3, 1), (0, 2)):
-            if b == 1:
-                first_product(1, b, bank)
-                second_product(1, b, PIECE)
-            else:
-                acc[1, b] = psum.tile([P, CHUNK], F32, name=f"acc1_{b}", tag=f"bank{bank}")
-                nc.tensor.matmul_mx(
-                    out=acc[1, b][:],
-                    lhsT=w_codes[:, b * P : (b + 1) * P].bitcast(E4M3X4),
-                    lhsT_scale=w_plane[:, b * P : (b + 1) * P],
-                    rhs=r_codes[1][:].bitcast(E4M3X4),
-                    rhs_scale=r_plane[1][:],
-                    start=True,
-                    stop=False,
-                )
-                first_product(1, b)
-            dx1 = keep.tile([P, CHUNK], F32, name=f"dx1{b}")
-            evacuate(1, b, dx1[:])
-            scatter(pages[b], dx1[:], CHUNK, CHUNK)
-            nc.sync.dma_start(out=out[b * P : (b + 1) * P, :], in_=pages[b][:])
+        clear(0)
+        rounded = shared.tile([P, HALF, PACK], BF16, name="rounded_first", align_bytes=64, offset=8 * T)
+        first_tier(nc.vector.tensor_copy, [0], rounded)
+        back_first = dequantise(0, 2)
+        pages[1] = shared.tile([P, T], F32, name="page1", align_bytes=64, offset=8 * T + 512)
+        clear(1)
+        q_codes[1] = shared.tile([P, HALF], U32, name="q_next", align_bytes=64, offset=8 * T)
+        first_tier(nc.scalar.copy, [1])
+        back_second = dequantise(HALF, 3)
+        left_first = keep.tile([P, HALF, PACK], BF16, name="left_first", tag="left_first", align_bytes=64)
+        residual_on_vector(0, back_first, left_first)
+        weighted = weigh(0, 0, 2)
+        left_second = keep.tile([P, HALF, PACK], BF16, name="left_second", align_bytes=64)
+        residual_on_vector(1, back_second, left_second)
+        q_codes[2] = keep.tile([P, PIECE], U32, name="q_second", tag="left_first", align_bytes=64)
+        rounded = shared.tile([P, PIECE, PACK], BF16, name="rounded_second", align_bytes=64, offset=4 * T - 1024)
+        first_tier(nc.scalar.copy, [2, 3], rounded)
+        for b in (2, 3):
+            pages[b] = shared.tile([P, T], F32, name=f"page{b}", align_bytes=64, offset=4 * T * (b - 2))
+            nc.gpsimd.memset(pages[b][:], 0.0)
+        place_weighted(0, 0, weighted)
+        place_weighted(0, HALF, weigh(0, HALF, 3))
+        place(1, 0, [HALF, HALF], 4)
+        place(2, 0, [HALF, HALF], 6)
+        left = shared.tile([P, PIECE, PACK], BF16, name="left2", align_bytes=64, offset=13 * T + 1024)
+        residual_on_tensor([2, 3], (0, 1), (2, 3), (4, 5), left)
+        place(3, 0, [HALF, HALF], 3)
+        place(0, PIECE, [PIECE], 6)
+        q_codes[3] = shared.tile([P, 2 * PIECE], U32, name="q_late", align_bytes=64, offset=13 * T + 2048)
+        first_tier(nc.scalar.copy, [4, 5])
+        place(1, PIECE, [PIECE], 7)
+        place(2, PIECE, [PIECE], 6)
+        residual_on_tensor([4, 5], (0, 1), (2, 3), (4, 5))
+        rounded = shared.tile([P, PIECE, PACK], BF16, name="rounded_last", align_bytes=64, offset=13 * T)
+        first_tier(nc.scalar.copy, [6, 7], rounded)
+        place(3, PIECE, [PIECE], 3)
+        place(0, 2 * PIECE, [PIECE], 7)
+        residual_on_tensor([6, 7], (2, 4), (0, 3), (1, 5))
+        place(1, 2 * PIECE, [PIECE], 3)
+        place(0, 3 * PIECE, [PIECE], 6)
+        place(1, 3 * PIECE, [PIECE], 7)
+        place(2, 2 * PIECE, [2 * PIECE], 0)
+        place(3, 2 * PIECE, [2 * PIECE], 1)

@@ -17,6 +17,8 @@ MULT = mybir.AluOpType.mult
 ADD = mybir.AluOpType.add
 SUB = mybir.AluOpType.subtract
 IS_EQUAL = mybir.AluOpType.is_equal
+ABS = mybir.ActivationFunctionType.Abs
+RELU = mybir.ActivationFunctionType.Relu
 COPY = mybir.ActivationFunctionType.Copy
 
 P = 128
@@ -43,8 +45,8 @@ def tile_list_embg_tgq8_none_kernel(tc, dy, w_words, w_scales, wgo, offs, out):
         w_plane = keep.tile([P, N], U8, name="w_plane", align_bytes=64)
         wgo_sb = keep.tile([P, J], F32, name="wgo_sb")
         dy_rows = dy.rearrange("(p i) j -> p i j", i=PACK)
-        loads = [(0, 1), (1, 2), (2, 4), (4, 6), (6, 8)]
-        loaded = [keep.tile([P, PACK, (hi - lo) * HALF], F32, name=f"raw{lo}") for lo, hi in loads]
+        loads = [(0, 1), (1, 2), (2, 3), (3, 5), (5, 8)]
+        loaded = [keep.tile([P, PACK, (hi - lo) * HALF], F32, name=f"raw{lo}", tag=f"raw{lo}", align_bytes=64) for lo, hi in loads]
         raw = []
         for (lo, hi), tile in zip(loads, loaded):
             raw.extend(tile[:, :, g * HALF : (g + 1) * HALF] for g in range(hi - lo))
@@ -54,7 +56,7 @@ def tile_list_embg_tgq8_none_kernel(tc, dy, w_words, w_scales, wgo, offs, out):
             nc.sync.dma_start(out=loaded[n][:], in_=dy_rows[:, :, lo * HALF : hi * HALF])
 
         nc.gpsimd.memset(w_plane[:].bitcast(I32), 0)
-        for n in range(3):
+        for n in range(4):
             load_dy(n)
         nc.sync.dma_start(out=w_codes[:].bitcast(I32), in_=w_words[0].rearrange("p n i -> p (n i)").bitcast(I32))
         for q in range(4):
@@ -62,14 +64,13 @@ def tile_list_embg_tgq8_none_kernel(tc, dy, w_words, w_scales, wgo, offs, out):
                 out=w_plane[32 * q : 32 * q + 4, :].bitcast(I32), in_=w_scales[0, 4 * q : 4 * q + 4, :].bitcast(I32)
             )
         nc.sync.dma_start(offsets[:], offs)
-        nc.sync.dma_start(out=wgo_sb[:, :PIECE], in_=wgo[:, :PIECE])
-        load_dy(3)
+        nc.sync.dma_start(out=wgo_sb[:, : 3 * HALF], in_=wgo[:, : 3 * HALF])
         load_dy(4)
-        nc.sync.dma_start(out=wgo_sb[:, PIECE:], in_=wgo[:, PIECE:])
+        nc.sync.dma_start(out=wgo_sb[:, 3 * HALF :], in_=wgo[:, 3 * HALF :])
 
         ramp = keep.tile([P, P], F32, name="ramp")
         nc.gpsimd.iota(ramp[:], [[1, P]], base=0, channel_multiplier=-1, allow_small_or_imprecise_dtypes=True)
-        marks = shared.tile([P, K], BF16, name="marks", align_bytes=64, offset=8 * T)
+        marks = shared.tile([P, K], BF16, name="marks", align_bytes=64, offset=9 * T)
         nc.gpsimd.memset(marks[:].bitcast(I32), 0)
         diagonal = marks[:, 0:K:PACK]
         nc.vector.tensor_scalar(out=diagonal, in0=ramp[:], scalar1=0.0, scalar2=None, op0=IS_EQUAL)
@@ -82,21 +83,23 @@ def tile_list_embg_tgq8_none_kernel(tc, dy, w_words, w_scales, wgo, offs, out):
         for t in range(1, PACK):
             nc.vector.tensor_copy(out=eye_codes[t].bitcast(U8)[:, t:K:PACK], in_=eye_first[:].bitcast(U8)[:, 0:K:PACK])
         eye = keep.tile([P, P], F32, name="eye")
-        nc.gpsimd.tensor_scalar(out=eye[:], in0=ramp[:], scalar1=0.0, scalar2=None, op0=IS_EQUAL)
+        distance = keep.tile([P, P], F32, name="distance")
+        nc.scalar.activation(out=distance[:], in_=ramp[:], func=ABS)
+        nc.scalar.activation(out=eye[:], in_=distance[:], func=RELU, scale=-1.0, bias=1.0)
         zeros = keep.tile([P, HALF], F32, name="zeros")
         nc.gpsimd.memset(zeros[:], 0.0)
         pages = [keep.tile([P, T], F32, name="page0", align_bytes=64), None, None, None]
 
-        q_codes = [keep.tile([P, HALF], U32, name="q_first", align_bytes=64), None, None, None]
+        q_codes = [keep.tile([P, HALF], U32, name="q_first", align_bytes=64), None, None, None, None]
         q_plane = keep.tile([P, J], U8, name="q_plane", align_bytes=64)
-        r_codes = [keep.tile([P, n * HALF], U32, name=f"r_codes{h}", align_bytes=64) for h, n in enumerate((1, 1, 2, 4))]
+        r_codes = [keep.tile([P, n * HALF], U32, name=f"r_codes{h}", align_bytes=64) for h, n in enumerate((1, 1, 1, 2, 3))]
         r_plane = keep.tile([P, J], U8, name="r_plane", align_bytes=64)
 
         first = (q_codes, q_plane, E5M2X4)
         second = (r_codes, r_plane, E4M3X4)
 
         def words(codes, j, width):
-            starts = (0, HALF, PIECE, 2 * PIECE)
+            starts = (0, HALF, 2 * HALF, 3 * HALF, 5 * HALF)
             h = max(n for n, start in enumerate(starts) if start <= j)
             lo = j - starts[h]
             return codes[h][:, lo : lo + width]
@@ -150,23 +153,21 @@ def tile_list_embg_tgq8_none_kernel(tc, dy, w_words, w_scales, wgo, offs, out):
         def window(b, j, width):
             return pages[b][:].indirect(offsets[:, j // 16 : (j + width) // 16])
 
-        def weigh(b, j, number):
-            acc = product(b, j, [HALF], number, [first, second])
-            weighted = keep.tile([P, HALF], F32, name=f"weighted{b}_{j}")
-            nc.vector.tensor_tensor(out=weighted[:], in0=acc[:], in1=wgo_sb[:, j : j + HALF], op=MULT)
-            return weighted
+        def weigh(b, j, number, tiers, weighted):
+            acc = product(b, j, [HALF], number, tiers)
+            nc.vector.tensor_tensor(out=weighted, in0=acc[:], in1=wgo_sb[:, j : j + HALF], op=MULT)
 
         def place_weighted(b, j, weighted):
-            nc.vector.tensor_tensor(out=window(b, j, HALF), in0=weighted[:], in1=zeros[:], op=ADD)
+            nc.vector.tensor_tensor(out=window(b, j, HALF), in0=weighted, in1=zeros[:], op=ADD)
 
         def clear(b):
             for lo in range(0, T, 2 * PIECE):
                 nc.vector.memset(pages[b][:, lo : lo + 2 * PIECE].bitcast(I32), 0)
 
-        def place(b, j, widths, number):
+        def place(b, j, widths, number, tag=None):
             width = sum(widths)
             acc = product(b, j, widths, number, [second, first])
-            dx = keep.tile([P, width], F32, name=f"dx{b}_{j}")
+            dx = keep.tile([P, width], F32, name=f"dx{b}_{j}", tag=tag or f"dx{b}_{j}", align_bytes=64)
             nc.scalar.copy(out=dx[:], in_=acc[:])
             nc.vector.tensor_tensor(out=window(b, j, width), in0=dx[:], in1=wgo_sb[:, j : j + width], op=MULT)
             if j + width == J:
@@ -174,10 +175,10 @@ def tile_list_embg_tgq8_none_kernel(tc, dy, w_words, w_scales, wgo, offs, out):
 
         def residual_on_tensor(units, back_banks, diff_banks, turn_banks, left=None):
             if left is None:
-                left = keep.tile([P, PIECE, PACK], BF16, name=f"left{units[0]}", align_bytes=64)
+                left = keep.tile([P, len(units) * HALF, PACK], BF16, name=f"left{units[0]}", align_bytes=64)
             left_words = left[:].rearrange("p j i -> p (j i)").bitcast(F32).rearrange("p (j u) -> p j u", u=2)
             minus = [keep.tile([P, PACK, HALF], F32, name=f"minus{x}") for x in units]
-            pairs = [keep.tile([P, 2, P, 2], BF16, name=f"pairs{x}", align_bytes=64) for x in units]
+            pairs = [keep.tile([P, 2, P, 2], BF16, name=f"pairs{x}", tag=f"pairs{x}", align_bytes=64) for x in units]
             for g, x in enumerate(units):
                 back = dequantise(x * HALF, back_banks[g])
                 nc.scalar.activation(out=minus[g][:], in_=back[:], func=COPY, scale=-1.0)
@@ -201,10 +202,10 @@ def tile_list_embg_tgq8_none_kernel(tc, dy, w_words, w_scales, wgo, offs, out):
 
         def first_tier(copy, units, rounded=None):
             if rounded is None:
-                rounded = keep.tile([P, len(units) * HALF, PACK], BF16, name=f"rounded{units[0]}", align_bytes=64)
+                rounded = keep.tile([P, len(units) * HALF, PACK], BF16, name=f"rounded{units[0]}", align_bytes=64)[:]
             for g, x in enumerate(units):
                 cast(copy, rounded[:, g * HALF : (g + 1) * HALF, :], raw[x])
-            quantise(q_codes, q_plane, E5M2X4, units[0] * HALF, rounded[:])
+            quantise(q_codes, q_plane, E5M2X4, units[0] * HALF, rounded)
 
         def residual_on_vector(x, back, left):
             nc.vector.tensor_tensor(
@@ -216,45 +217,45 @@ def tile_list_embg_tgq8_none_kernel(tc, dy, w_words, w_scales, wgo, offs, out):
             quantise(r_codes, r_plane, E4M3X4, x * HALF, left[:])
 
         clear(0)
-        rounded = shared.tile([P, HALF, PACK], BF16, name="rounded_first", align_bytes=64, offset=8 * T)
-        first_tier(nc.vector.tensor_copy, [0], rounded)
+        rounded = shared.tile([P, HALF, PACK], BF16, name="rounded_first", align_bytes=64, offset=9 * T)
+        first_tier(nc.vector.tensor_copy, [0], rounded[:])
         back_first = dequantise(0, 2)
-        pages[1] = shared.tile([P, T], F32, name="page1", align_bytes=64, offset=8 * T + 512)
+        pages[1] = shared.tile([P, T], F32, name="page1", align_bytes=64, offset=9 * T + 512)
         clear(1)
-        q_codes[1] = shared.tile([P, HALF], U32, name="q_next", align_bytes=64, offset=8 * T)
+        q_codes[1] = shared.tile([P, HALF], U32, name="q_next", align_bytes=64, offset=9 * T)
         first_tier(nc.scalar.copy, [1])
         back_second = dequantise(HALF, 3)
-        left_first = keep.tile([P, HALF, PACK], BF16, name="left_first", tag="left_first", align_bytes=64)
+        left_first = keep.tile([P, HALF, PACK], BF16, name="left_first", align_bytes=64)
         residual_on_vector(0, back_first, left_first)
-        weighted = weigh(0, 0, 2)
+        q_codes[2] = keep.tile([P, HALF], U32, name="q_third", tag="raw0", align_bytes=64)
+        first_tier(nc.scalar.copy, [2])
+        back_third = dequantise(2 * HALF, 6)
         left_second = keep.tile([P, HALF, PACK], BF16, name="left_second", align_bytes=64)
         residual_on_vector(1, back_second, left_second)
-        q_codes[2] = keep.tile([P, PIECE], U32, name="q_second", tag="left_first", align_bytes=64)
-        rounded = shared.tile([P, PIECE, PACK], BF16, name="rounded_second", align_bytes=64, offset=4 * T - 1024)
-        first_tier(nc.scalar.copy, [2, 3], rounded)
+        left_third = shared.tile([P, HALF, PACK], BF16, name="left_third", align_bytes=64, offset=4 * T - 512)
+        residual_on_vector(2, back_third, left_third)
+        q_codes[3] = keep.tile([P, PIECE], U32, name="q_middle", tag="raw1", align_bytes=64)
+        first_tier(nc.scalar.copy, [3, 4])
+        weighted = keep.tile([P, 2, HALF], F32, name="weighted", tag="raw2", align_bytes=64)
+        weigh(0, 0, 2, [first, second], weighted[:, 0, :])
+        weigh(1, 0, 7, [second, first], weighted[:, 1, :])
         for b in (2, 3):
             pages[b] = shared.tile([P, T], F32, name=f"page{b}", align_bytes=64, offset=4 * T * (b - 2))
             nc.gpsimd.memset(pages[b][:], 0.0)
-        place_weighted(0, 0, weighted)
-        place_weighted(0, HALF, weigh(0, HALF, 3))
-        place(1, 0, [HALF, HALF], 4)
-        place(2, 0, [HALF, HALF], 6)
-        left = shared.tile([P, PIECE, PACK], BF16, name="left2", align_bytes=64, offset=13 * T + 1024)
-        residual_on_tensor([2, 3], (0, 1), (2, 3), (4, 5), left)
-        place(3, 0, [HALF, HALF], 3)
-        place(0, PIECE, [PIECE], 6)
-        q_codes[3] = shared.tile([P, 2 * PIECE], U32, name="q_late", align_bytes=64, offset=13 * T + 2048)
-        first_tier(nc.scalar.copy, [4, 5])
-        place(1, PIECE, [PIECE], 7)
-        place(2, PIECE, [PIECE], 6)
-        residual_on_tensor([4, 5], (0, 1), (2, 3), (4, 5))
-        rounded = shared.tile([P, PIECE, PACK], BF16, name="rounded_last", align_bytes=64, offset=13 * T)
-        first_tier(nc.scalar.copy, [6, 7], rounded)
-        place(3, PIECE, [PIECE], 3)
-        place(0, 2 * PIECE, [PIECE], 7)
-        residual_on_tensor([6, 7], (2, 4), (0, 3), (1, 5))
-        place(1, 2 * PIECE, [PIECE], 3)
-        place(0, 3 * PIECE, [PIECE], 6)
-        place(1, 3 * PIECE, [PIECE], 7)
-        place(2, 2 * PIECE, [2 * PIECE], 0)
-        place(3, 2 * PIECE, [2 * PIECE], 1)
+        for b in range(2):
+            place_weighted(b, 0, weighted[:, b, :])
+        place(0, HALF, [HALF, HALF], 3)
+        place(1, HALF, [HALF, HALF], 6, "before_late")
+        place(2, 0, [HALF, HALF, HALF], 7)
+        residual_on_tensor([3, 4], (0, 1), (2, 3), (4, 5))
+        q_codes[4] = keep.tile([P, 3 * HALF], U32, name="q_late", tag="before_late", align_bytes=64)
+        rounded = keep.tile([P, 3 * HALF, PACK], BF16, name="rounded_late", tag="pairs4", align_bytes=64)
+        first_tier(nc.scalar.copy, [5, 6], rounded[:, :PIECE, :])
+        first_tier(nc.scalar.copy, [7], rounded[:, PIECE:, :])
+        place(3, 0, [HALF, HALF, HALF], 3)
+        for b in range(3):
+            place(b, 3 * HALF, [PIECE], 6 + b % 2)
+        residual_on_tensor([5, 6, 7], (4, 5, 4), (0, 1, 2), (3, 5, 3))
+        place(3, 3 * HALF, [PIECE], 5)
+        for b in range(BLOCKS):
+            place(b, 5 * HALF, [PIECE, HALF], (6, 7, 0, 1)[b])

@@ -45,8 +45,8 @@ def tile_list_embg_tgq8_none_kernel(tc, dy, w_words, w_scales, wgo, offs, out):
         w_plane = keep.tile([P, N], U8, name="w_plane", align_bytes=64)
         wgo_sb = keep.tile([P, J], F32, name="wgo_sb")
         dy_rows = dy.rearrange("(p i) j -> p i j", i=PACK)
-        loads = [(0, 1), (1, 2), (2, 3), (3, 5), (5, 8)]
-        loaded = [keep.tile([P, PACK, (hi - lo) * HALF], F32, name=f"raw{lo}", tag=f"raw{lo}", align_bytes=64) for lo, hi in loads]
+        loads = [(0, 2), (2, 3), (3, 5), (5, 8)]
+        loaded = [keep.tile([P, PACK, (hi - lo) * HALF], F32, name=f"raw{lo}") for lo, hi in loads]
         raw = []
         for (lo, hi), tile in zip(loads, loaded):
             raw.extend(tile[:, :, g * HALF : (g + 1) * HALF] for g in range(hi - lo))
@@ -56,7 +56,7 @@ def tile_list_embg_tgq8_none_kernel(tc, dy, w_words, w_scales, wgo, offs, out):
             nc.sync.dma_start(out=loaded[n][:], in_=dy_rows[:, :, lo * HALF : hi * HALF])
 
         nc.gpsimd.memset(w_plane[:].bitcast(I32), 0)
-        for n in range(4):
+        for n in range(3):
             load_dy(n)
         nc.sync.dma_start(out=w_codes[:].bitcast(I32), in_=w_words[0].rearrange("p n i -> p (n i)").bitcast(I32))
         for q in range(4):
@@ -65,12 +65,12 @@ def tile_list_embg_tgq8_none_kernel(tc, dy, w_words, w_scales, wgo, offs, out):
             )
         nc.sync.dma_start(offsets[:], offs)
         nc.sync.dma_start(out=wgo_sb[:, : 3 * HALF], in_=wgo[:, : 3 * HALF])
-        load_dy(4)
+        load_dy(3)
         nc.sync.dma_start(out=wgo_sb[:, 3 * HALF :], in_=wgo[:, 3 * HALF :])
 
         ramp = keep.tile([P, P], F32, name="ramp")
         nc.gpsimd.iota(ramp[:], [[1, P]], base=0, channel_multiplier=-1, allow_small_or_imprecise_dtypes=True)
-        marks = shared.tile([P, K], BF16, name="marks", align_bytes=64, offset=9 * T)
+        marks = shared.tile([P, K], BF16, name="marks", align_bytes=64, offset=12 * T)
         nc.gpsimd.memset(marks[:].bitcast(I32), 0)
         diagonal = marks[:, 0:K:PACK]
         nc.vector.tensor_scalar(out=diagonal, in0=ramp[:], scalar1=0.0, scalar2=None, op0=IS_EQUAL)
@@ -86,13 +86,12 @@ def tile_list_embg_tgq8_none_kernel(tc, dy, w_words, w_scales, wgo, offs, out):
         distance = keep.tile([P, P], F32, name="distance")
         nc.scalar.activation(out=distance[:], in_=ramp[:], func=ABS)
         nc.scalar.activation(out=eye[:], in_=distance[:], func=RELU, scale=-1.0, bias=1.0)
-        zeros = keep.tile([P, HALF], F32, name="zeros")
-        nc.gpsimd.memset(zeros[:], 0.0)
         pages = [keep.tile([P, T], F32, name="page0", align_bytes=64), None, None, None]
 
         q_codes = [keep.tile([P, HALF], U32, name="q_first", align_bytes=64), None, None, None, None]
         q_plane = keep.tile([P, J], U8, name="q_plane", align_bytes=64)
-        r_codes = [keep.tile([P, n * HALF], U32, name=f"r_codes{h}", align_bytes=64) for h, n in enumerate((1, 1, 1, 2, 3))]
+        r_all = keep.tile([P, J], U32, name="r_all", align_bytes=64)
+        r_codes = [r_all[:, lo * HALF : hi * HALF] for lo, hi in ((0, 1), (1, 2), (2, 3), (3, 5), (5, 8))]
         r_plane = keep.tile([P, J], U8, name="r_plane", align_bytes=64)
 
         first = (q_codes, q_plane, E5M2X4)
@@ -153,21 +152,15 @@ def tile_list_embg_tgq8_none_kernel(tc, dy, w_words, w_scales, wgo, offs, out):
         def window(b, j, width):
             return pages[b][:].indirect(offsets[:, j // 16 : (j + width) // 16])
 
-        def weigh(b, j, number, tiers, weighted):
-            acc = product(b, j, [HALF], number, tiers)
-            nc.vector.tensor_tensor(out=weighted, in0=acc[:], in1=wgo_sb[:, j : j + HALF], op=MULT)
-
-        def place_weighted(b, j, weighted):
-            nc.vector.tensor_tensor(out=window(b, j, HALF), in0=weighted, in1=zeros[:], op=ADD)
-
         def clear(b):
             for lo in range(0, T, 2 * PIECE):
                 nc.vector.memset(pages[b][:, lo : lo + 2 * PIECE].bitcast(I32), 0)
 
-        def place(b, j, widths, number, tag=None):
+        def place(b, j, widths, number, tiers, dx=None):
             width = sum(widths)
-            acc = product(b, j, widths, number, [second, first])
-            dx = keep.tile([P, width], F32, name=f"dx{b}_{j}", tag=tag or f"dx{b}_{j}", align_bytes=64)
+            acc = product(b, j, widths, number, tiers)
+            if dx is None:
+                dx = keep.tile([P, width], F32, name=f"dx{b}_{j}")
             nc.scalar.copy(out=dx[:], in_=acc[:])
             nc.vector.tensor_tensor(out=window(b, j, width), in0=dx[:], in1=wgo_sb[:, j : j + width], op=MULT)
             if j + width == J:
@@ -207,55 +200,57 @@ def tile_list_embg_tgq8_none_kernel(tc, dy, w_words, w_scales, wgo, offs, out):
                 cast(copy, rounded[:, g * HALF : (g + 1) * HALF, :], raw[x])
             quantise(q_codes, q_plane, E5M2X4, units[0] * HALF, rounded)
 
-        def residual_on_vector(x, back, left):
+        def subtract(x, back, left):
             nc.vector.tensor_tensor(
-                out=by_fours(left[:], "p (c j) i"),
+                out=by_fours(left, "p (c j) i"),
                 in0=by_fours(raw[x], "p i (c j)"),
                 in1=by_fours(back[:], "p i (c j)"),
                 op=SUB,
             )
-            quantise(r_codes, r_plane, E4M3X4, x * HALF, left[:])
 
         clear(0)
-        rounded = shared.tile([P, HALF, PACK], BF16, name="rounded_first", align_bytes=64, offset=9 * T)
+        rounded = shared.tile([P, HALF, PACK], BF16, name="rounded_first", align_bytes=64, offset=12 * T)
         first_tier(nc.vector.tensor_copy, [0], rounded[:])
-        back_first = dequantise(0, 2)
-        pages[1] = shared.tile([P, T], F32, name="page1", align_bytes=64, offset=9 * T + 512)
-        clear(1)
-        q_codes[1] = shared.tile([P, HALF], U32, name="q_next", align_bytes=64, offset=9 * T)
-        first_tier(nc.scalar.copy, [1])
-        back_second = dequantise(HALF, 3)
-        left_first = keep.tile([P, HALF, PACK], BF16, name="left_first", align_bytes=64)
-        residual_on_vector(0, back_first, left_first)
-        q_codes[2] = keep.tile([P, HALF], U32, name="q_third", tag="raw0", align_bytes=64)
+        back = [dequantise(0, 2)]
+        q_codes[1] = shared.tile([P, HALF], U32, name="q_next", align_bytes=64, offset=12 * T)
+        rounded = keep.tile([P, HALF, PACK], BF16, name="rounded_next", tag="rounded_next", align_bytes=64)
+        first_tier(nc.scalar.copy, [1], rounded[:])
+        back.append(dequantise(HALF, 3))
+        left = keep.tile([P, PIECE, PACK], BF16, name="left_first", tag="left_first", align_bytes=64)
+        subtract(0, back[0], left[:, :HALF, :])
+        q_codes[2] = keep.tile([P, HALF], U32, name="q_third", tag="rounded_next", align_bytes=64)
         first_tier(nc.scalar.copy, [2])
-        back_third = dequantise(2 * HALF, 6)
-        left_second = keep.tile([P, HALF, PACK], BF16, name="left_second", align_bytes=64)
-        residual_on_vector(1, back_second, left_second)
-        left_third = shared.tile([P, HALF, PACK], BF16, name="left_third", align_bytes=64, offset=4 * T - 512)
-        residual_on_vector(2, back_third, left_third)
-        q_codes[3] = keep.tile([P, PIECE], U32, name="q_middle", tag="raw1", align_bytes=64)
-        first_tier(nc.scalar.copy, [3, 4])
-        weighted = keep.tile([P, 2, HALF], F32, name="weighted", tag="raw2", align_bytes=64)
-        weigh(0, 0, 2, [first, second], weighted[:, 0, :])
-        weigh(1, 0, 7, [second, first], weighted[:, 1, :])
+        back.append(dequantise(2 * HALF, 6))
+        subtract(1, back[1], left[:, HALF:, :])
+        nc.vector.quantize_mx(
+            out=r_all[:, :PIECE].bitcast(E4M3X4), scales=r_plane[:, :PIECE], in_=left[:].rearrange("p j i -> p (j i)")
+        )
+        left = shared.tile([P, HALF, PACK], BF16, name="left_third", align_bytes=64, offset=0)
+        subtract(2, back[2], left[:])
+        quantise(r_codes, r_plane, E4M3X4, 2 * HALF, left[:])
+        q_codes[3] = keep.tile([P, PIECE], U32, name="q_middle", tag="left_first", align_bytes=64)
+        rounded = shared.tile([P, PIECE, PACK], BF16, name="rounded_middle", align_bytes=64, offset=1024)
+        first_tier(nc.scalar.copy, [3, 4], rounded[:])
+        pages[1] = shared.tile([P, T], F32, name="page1", align_bytes=64, offset=0)
+        nc.gpsimd.memset(pages[1][:], 0.0)
+        dx = shared.tile([P, PIECE], F32, name="dx_first", align_bytes=64, offset=8 * T - 512)
+        place(0, 0, [HALF, HALF], 3, [first, second], dx)
         for b in (2, 3):
-            pages[b] = shared.tile([P, T], F32, name=f"page{b}", align_bytes=64, offset=4 * T * (b - 2))
+            pages[b] = shared.tile([P, T], F32, name=f"page{b}", align_bytes=64, offset=4 * T * (b - 1))
             nc.gpsimd.memset(pages[b][:], 0.0)
-        for b in range(2):
-            place_weighted(b, 0, weighted[:, b, :])
-        place(0, HALF, [HALF, HALF], 3)
-        place(1, HALF, [HALF, HALF], 6, "before_late")
-        place(2, 0, [HALF, HALF, HALF], 7)
+        place(1, 0, [HALF, HALF, HALF], 6, [second, first])
+        dx = keep.tile([P, 3 * HALF], F32, name="dx_third", tag="before_late", align_bytes=64)
+        place(2, 0, [HALF, HALF, HALF], 7, [second, first], dx)
         residual_on_tensor([3, 4], (0, 1), (2, 3), (4, 5))
         q_codes[4] = keep.tile([P, 3 * HALF], U32, name="q_late", tag="before_late", align_bytes=64)
         rounded = keep.tile([P, 3 * HALF, PACK], BF16, name="rounded_late", tag="pairs4", align_bytes=64)
         first_tier(nc.scalar.copy, [5, 6], rounded[:, :PIECE, :])
         first_tier(nc.scalar.copy, [7], rounded[:, PIECE:, :])
-        place(3, 0, [HALF, HALF, HALF], 3)
-        for b in range(3):
-            place(b, 3 * HALF, [PIECE], 6 + b % 2)
+        place(3, 0, [HALF, HALF, HALF], 3, [second, first])
+        place(0, PIECE, [HALF, PIECE], 6, [second, first])
+        place(1, 3 * HALF, [PIECE], 7, [second, first])
+        place(2, 3 * HALF, [PIECE], 6, [second, first])
         residual_on_tensor([5, 6, 7], (4, 5, 4), (0, 1, 2), (3, 5, 3))
-        place(3, 3 * HALF, [PIECE], 5)
+        place(3, 3 * HALF, [PIECE], 5, [second, first])
         for b in range(BLOCKS):
-            place(b, 5 * HALF, [PIECE, HALF], (6, 7, 0, 1)[b])
+            place(b, 5 * HALF, [PIECE, HALF], (6, 7, 0, 1)[b], [second, first])

@@ -23,10 +23,10 @@ COPY = mybir.ActivationFunctionType.Copy
 
 P = 128
 PACK = 4
-PIECE = 256
-HALF = 128
-BLOCKS = N // P
-PIECES = J // PIECE
+UNIT = 128
+UNITS = J // UNIT
+PAGE = 4 * T
+CLEAR = 512
 
 
 def by_fours(ap, order):
@@ -46,14 +46,14 @@ def tile_list_embg_tgq8_none_kernel(tc, dy, w_words, w_scales, wgo, offs, out):
         wgo_sb = keep.tile([P, J], F32, name="wgo_sb")
         dy_rows = dy.rearrange("(p i) j -> p i j", i=PACK)
         loads = [(0, 2), (2, 3), (3, 5), (5, 8)]
-        loaded = [keep.tile([P, PACK, (hi - lo) * HALF], F32, name=f"raw{lo}") for lo, hi in loads]
+        loaded = [keep.tile([P, PACK, (hi - lo) * UNIT], F32, name=f"raw{lo}") for lo, hi in loads]
         raw = []
         for (lo, hi), tile in zip(loads, loaded):
-            raw.extend(tile[:, :, g * HALF : (g + 1) * HALF] for g in range(hi - lo))
+            raw.extend(tile[:, :, g * UNIT : (g + 1) * UNIT] for g in range(hi - lo))
 
         def load_dy(n):
             lo, hi = loads[n]
-            nc.sync.dma_start(out=loaded[n][:], in_=dy_rows[:, :, lo * HALF : hi * HALF])
+            nc.sync.dma_start(out=loaded[n][:], in_=dy_rows[:, :, lo * UNIT : hi * UNIT])
 
         nc.gpsimd.memset(w_plane[:].bitcast(I32), 0)
         for n in range(3):
@@ -64,13 +64,16 @@ def tile_list_embg_tgq8_none_kernel(tc, dy, w_words, w_scales, wgo, offs, out):
                 out=w_plane[32 * q : 32 * q + 4, :].bitcast(I32), in_=w_scales[0, 4 * q : 4 * q + 4, :].bitcast(I32)
             )
         nc.sync.dma_start(offsets[:], offs)
-        nc.sync.dma_start(out=wgo_sb[:, : 3 * HALF], in_=wgo[:, : 3 * HALF])
+        nc.sync.dma_start(out=wgo_sb[:, : 3 * UNIT], in_=wgo[:, : 3 * UNIT])
         load_dy(3)
-        nc.sync.dma_start(out=wgo_sb[:, 3 * HALF :], in_=wgo[:, 3 * HALF :])
+        nc.sync.dma_start(out=wgo_sb[:, 3 * UNIT :], in_=wgo[:, 3 * UNIT :])
+
+        def placed(shape, dtype, name, offset):
+            return shared.tile(shape, dtype, name=name, align_bytes=64, offset=offset)
 
         ramp = keep.tile([P, P], F32, name="ramp")
         nc.gpsimd.iota(ramp[:], [[1, P]], base=0, channel_multiplier=-1, allow_small_or_imprecise_dtypes=True)
-        marks = shared.tile([P, K], BF16, name="marks", align_bytes=64, offset=12 * T)
+        marks = placed([P, K], BF16, "marks", 2 * PAGE + 64)
         nc.gpsimd.memset(marks[:].bitcast(I32), 0)
         diagonal = marks[:, 0:K:PACK]
         nc.vector.tensor_scalar(out=diagonal, in0=ramp[:], scalar1=0.0, scalar2=None, op0=IS_EQUAL)
@@ -86,22 +89,27 @@ def tile_list_embg_tgq8_none_kernel(tc, dy, w_words, w_scales, wgo, offs, out):
         distance = keep.tile([P, P], F32, name="distance")
         nc.scalar.activation(out=distance[:], in_=ramp[:], func=ABS)
         nc.scalar.activation(out=eye[:], in_=distance[:], func=RELU, scale=-1.0, bias=1.0)
-        pages = [keep.tile([P, T], F32, name="page0", align_bytes=64), None, None, None]
 
-        q_codes = [keep.tile([P, HALF], U32, name="q_first", align_bytes=64), None, None, None, None]
+        pages = {}
+        q_codes = {}
         q_plane = keep.tile([P, J], U8, name="q_plane", align_bytes=64)
-        r_all = keep.tile([P, J], U32, name="r_all", align_bytes=64)
-        r_codes = [r_all[:, lo * HALF : hi * HALF] for lo, hi in ((0, 1), (1, 2), (2, 3), (3, 5), (5, 8))]
+        r_early = keep.tile([P, 3 * UNIT], U32, name="r_early", align_bytes=64)
         r_plane = keep.tile([P, J], U8, name="r_plane", align_bytes=64)
-
+        r_codes = {x: (r_early, x) for x in range(3)}
         first = (q_codes, q_plane, E5M2X4)
         second = (r_codes, r_plane, E4M3X4)
 
-        def words(codes, j, width):
-            starts = (0, HALF, 2 * HALF, 3 * HALF, 5 * HALF)
-            h = max(n for n, start in enumerate(starts) if start <= j)
-            lo = j - starts[h]
-            return codes[h][:, lo : lo + width]
+        def words(codes, x, count):
+            tile, place_in_tile = codes[x]
+            return tile[:, place_in_tile * UNIT : (place_in_tile + count) * UNIT]
+
+        def runs(codes, lo, hi):
+            found = []
+            while hi > lo:
+                count = 2 if hi - lo >= 2 and codes[hi - 2][0] is codes[hi - 1][0] else 1
+                found.append((hi - count, count))
+                hi = hi - count
+            return found
 
         def bank(number, shape, name):
             return psum.tile(shape, F32, name=name, tag=f"bank{number}")
@@ -109,96 +117,33 @@ def tile_list_embg_tgq8_none_kernel(tc, dy, w_words, w_scales, wgo, offs, out):
         def cast(copy, dst, src):
             copy(out=by_fours(dst, "p (c j) i"), in_=by_fours(src, "p i (c j)"))
 
-        def quantise(codes, plane, fmt, j, values):
-            width = values.shape[1]
+        def quantise(tier, x, values):
+            codes, plane, fmt = tier
+            count = values.shape[1] // UNIT
             nc.vector.quantize_mx(
-                out=words(codes, j, width).bitcast(fmt),
-                scales=plane[:, j : j + width],
+                out=words(codes, x, count).bitcast(fmt),
+                scales=plane[:, x * UNIT : (x + count) * UNIT],
                 in_=values.rearrange("p j i -> p (j i)"),
             )
 
-        def dequantise(j, number):
-            back = bank(number, [P, PACK, HALF], f"back{j}")
+        def first_tier(copy, units, rounded):
+            for g, x in enumerate(units):
+                cast(copy, rounded[:, g * UNIT : (g + 1) * UNIT, :], raw[x])
+            quantise(first, units[0], rounded[:])
+
+        def dequantise(x, number):
+            back = bank(number, [P, PACK, UNIT], f"back{x}")
             for t in range(PACK):
                 nc.tensor.matmul_mx(
                     out=back[:, t, :],
                     lhsT=eye_codes[t].bitcast(E4M3X4),
                     lhsT_scale=eye_plane[:],
-                    rhs=words(q_codes, j, HALF).bitcast(E5M2X4),
-                    rhs_scale=q_plane[:, j : j + HALF],
+                    rhs=words(q_codes, x, 1).bitcast(E5M2X4),
+                    rhs_scale=q_plane[:, x * UNIT : (x + 1) * UNIT],
                     start=True,
                     stop=True,
                 )
             return back
-
-        def product(b, j, widths, number, tiers):
-            acc = bank(number, [P, sum(widths)], f"acc{b}_{j}")
-            passes = []
-            for codes, plane, fmt in tiers:
-                for n, cols in enumerate(widths):
-                    passes.append((codes, plane, fmt, sum(widths[:n]), cols))
-            for n, (codes, plane, fmt, lo, cols) in enumerate(passes):
-                nc.tensor.matmul_mx(
-                    out=acc[:, lo : lo + cols],
-                    lhsT=w_codes[:, b * P : (b + 1) * P].bitcast(E4M3X4),
-                    lhsT_scale=w_plane[:, b * P : (b + 1) * P],
-                    rhs=words(codes, j + lo, cols).bitcast(fmt),
-                    rhs_scale=plane[:, j + lo : j + lo + cols],
-                    start=(n == 0),
-                    stop=(n == len(passes) - 1),
-                )
-            return acc
-
-        def window(b, j, width):
-            return pages[b][:].indirect(offsets[:, j // 16 : (j + width) // 16])
-
-        def clear(b):
-            for lo in range(0, T, 2 * PIECE):
-                nc.vector.memset(pages[b][:, lo : lo + 2 * PIECE].bitcast(I32), 0)
-
-        def place(b, j, widths, number, tiers, dx=None):
-            width = sum(widths)
-            acc = product(b, j, widths, number, tiers)
-            if dx is None:
-                dx = keep.tile([P, width], F32, name=f"dx{b}_{j}")
-            nc.scalar.copy(out=dx[:], in_=acc[:])
-            nc.vector.tensor_tensor(out=window(b, j, width), in0=dx[:], in1=wgo_sb[:, j : j + width], op=MULT)
-            if j + width == J:
-                nc.sync.dma_start(out=out[b * P : (b + 1) * P, :], in_=pages[b][:])
-
-        def residual_on_tensor(units, back_banks, diff_banks, turn_banks, left=None):
-            if left is None:
-                left = keep.tile([P, len(units) * HALF, PACK], BF16, name=f"left{units[0]}", align_bytes=64)
-            left_words = left[:].rearrange("p j i -> p (j i)").bitcast(F32).rearrange("p (j u) -> p j u", u=2)
-            minus = [keep.tile([P, PACK, HALF], F32, name=f"minus{x}") for x in units]
-            pairs = [keep.tile([P, 2, P, 2], BF16, name=f"pairs{x}", tag=f"pairs{x}", align_bytes=64) for x in units]
-            for g, x in enumerate(units):
-                back = dequantise(x * HALF, back_banks[g])
-                nc.scalar.activation(out=minus[g][:], in_=back[:], func=COPY, scale=-1.0)
-            for g, x in enumerate(units):
-                diff = bank(diff_banks[g], [P, PACK, P], f"diff{x}")
-                terms = [raw[x][:, t, :] for t in range(PACK)] + [minus[g][:, t, :] for t in range(PACK)]
-                for n, term in enumerate(terms):
-                    nc.tensor.matmul(
-                        diff[:, n % PACK, :], term, eye[:], start=(n == 0), stop=(n == len(terms) - 1), is_transpose=True
-                    )
-                nc.scalar.copy(out=pairs[g][:], in_=diff[:].rearrange("j (u e) p -> j u p e", e=2))
-            for g, x in enumerate(units):
-                pair_words = pairs[g][:].rearrange("j u p e -> j (u p e)").bitcast(F32)
-                turned = bank(turn_banks[g], [P, 2, P], f"turned{x}")
-                for u in range(2):
-                    nc.tensor.transpose(turned[:, u, :], pair_words[:, u * P : (u + 1) * P], eye[:])
-                nc.scalar.copy(
-                    out=left_words[:, g * HALF : (g + 1) * HALF, :], in_=turned[:].rearrange("p u j -> p j u")
-                )
-            quantise(r_codes, r_plane, E4M3X4, units[0] * HALF, left[:])
-
-        def first_tier(copy, units, rounded=None):
-            if rounded is None:
-                rounded = keep.tile([P, len(units) * HALF, PACK], BF16, name=f"rounded{units[0]}", align_bytes=64)[:]
-            for g, x in enumerate(units):
-                cast(copy, rounded[:, g * HALF : (g + 1) * HALF, :], raw[x])
-            quantise(q_codes, q_plane, E5M2X4, units[0] * HALF, rounded)
 
         def subtract(x, back, left):
             nc.vector.tensor_tensor(
@@ -208,49 +153,141 @@ def tile_list_embg_tgq8_none_kernel(tc, dy, w_words, w_scales, wgo, offs, out):
                 op=SUB,
             )
 
-        clear(0)
-        rounded = shared.tile([P, HALF, PACK], BF16, name="rounded_first", align_bytes=64, offset=12 * T)
-        first_tier(nc.vector.tensor_copy, [0], rounded[:])
-        back = [dequantise(0, 2)]
-        q_codes[1] = shared.tile([P, HALF], U32, name="q_next", align_bytes=64, offset=12 * T)
-        rounded = keep.tile([P, HALF, PACK], BF16, name="rounded_next", tag="rounded_next", align_bytes=64)
-        first_tier(nc.scalar.copy, [1], rounded[:])
-        back.append(dequantise(HALF, 3))
-        left = keep.tile([P, PIECE, PACK], BF16, name="left_first", tag="left_first", align_bytes=64)
-        subtract(0, back[0], left[:, :HALF, :])
-        q_codes[2] = keep.tile([P, HALF], U32, name="q_third", tag="rounded_next", align_bytes=64)
-        first_tier(nc.scalar.copy, [2])
-        back.append(dequantise(2 * HALF, 6))
-        subtract(1, back[1], left[:, HALF:, :])
-        nc.vector.quantize_mx(
-            out=r_all[:, :PIECE].bitcast(E4M3X4), scales=r_plane[:, :PIECE], in_=left[:].rearrange("p j i -> p (j i)")
-        )
-        left = shared.tile([P, HALF, PACK], BF16, name="left_third", align_bytes=64, offset=0)
-        subtract(2, back[2], left[:])
-        quantise(r_codes, r_plane, E4M3X4, 2 * HALF, left[:])
-        q_codes[3] = keep.tile([P, PIECE], U32, name="q_middle", tag="left_first", align_bytes=64)
-        rounded = shared.tile([P, PIECE, PACK], BF16, name="rounded_middle", align_bytes=64, offset=1024)
-        first_tier(nc.scalar.copy, [3, 4], rounded[:])
-        pages[1] = shared.tile([P, T], F32, name="page1", align_bytes=64, offset=0)
+        def clear(b, view):
+            for lo in range(0, T, CLEAR):
+                nc.vector.memset(pages[b][:, lo : lo + CLEAR].bitcast(view), 0)
+
+
+        def sums(b, lo, hi, number, late_first):
+            acc = bank(number, [P, (hi - lo) * UNIT], f"acc{b}_{lo}")
+            if late_first:
+                passes = [(tier, x, n) for tier in (second, first) for x, n in runs(tier[0], lo, hi)]
+            else:
+                passes = [(first, x, n) for x, n in reversed(runs(q_codes, lo, hi))]
+                passes = passes + [(second, x, n) for x, n in reversed(runs(r_codes, lo, hi))]
+            return acc, passes
+
+        def place(b, lo, hi, number, late_first=False, dx=None, passes=None):
+            acc, found = sums(b, lo, hi, number, late_first)
+            if passes is None:
+                passes = found
+            for n, ((codes, plane, fmt), x, count) in enumerate(passes):
+                nc.tensor.matmul_mx(
+                    out=acc[:, (x - lo) * UNIT : (x - lo + count) * UNIT],
+                    lhsT=w_codes[:, b * P : (b + 1) * P].bitcast(E4M3X4),
+                    lhsT_scale=w_plane[:, b * P : (b + 1) * P],
+                    rhs=words(codes, x, count).bitcast(fmt),
+                    rhs_scale=plane[:, x * UNIT : (x + count) * UNIT],
+                    start=(n == 0),
+                    stop=(n == len(passes) - 1),
+                )
+            if dx is None:
+                dx = keep.tile([P, (hi - lo) * UNIT], F32, name=f"dx{b}_{lo}")
+            nc.scalar.copy(out=dx[:], in_=acc[:])
+            window = pages[b][:].indirect(offsets[:, lo * UNIT // 16 : hi * UNIT // 16])
+            nc.vector.tensor_tensor(out=window, in0=dx[:], in1=wgo_sb[:, lo * UNIT : hi * UNIT], op=MULT)
+            if hi == UNITS:
+                nc.sync.dma_start(out=out[b * P : (b + 1) * P, :], in_=pages[b][:])
+
+        def negate(x, number, minus=None):
+            back = dequantise(x, number)
+            if minus is None:
+                minus = keep.tile([P, PACK, UNIT], F32, name=f"minus{x}", tag=f"minus{x}", align_bytes=64)
+            nc.scalar.activation(out=minus[:], in_=back[:], func=COPY, scale=-1.0)
+            return minus
+
+        def difference(x, minus, number):
+            diff = bank(number, [P, PACK, P], f"diff{x}")
+            terms = [raw[x][:, t, :] for t in range(PACK)] + [minus[:, t, :] for t in range(PACK)]
+            for n, term in enumerate(terms):
+                nc.tensor.matmul(
+                    diff[:, n % PACK, :], term, eye[:], start=(n == 0), stop=(n == len(terms) - 1), is_transpose=True
+                )
+            pairs = keep.tile([P, 2, P, 2], BF16, name=f"pairs{x}", align_bytes=64)
+            nc.scalar.copy(out=pairs[:], in_=diff[:].rearrange("j (u e) p -> j u p e", e=2))
+            return pairs
+
+        def turn_back(x, pairs, number):
+            pair_words = pairs[:].rearrange("j u p e -> j (u p e)").bitcast(F32)
+            turned = bank(number, [P, 2, P], f"turned{x}")
+            for u in range(2):
+                nc.tensor.transpose(turned[:, u, :], pair_words[:, u * P : (u + 1) * P], eye[:])
+            left = keep.tile([P, UNIT, PACK], BF16, name=f"left{x}", align_bytes=64)
+            left_words = left[:].rearrange("p j i -> p (j i)").bitcast(F32).rearrange("p (j u) -> p j u", u=2)
+            nc.scalar.copy(out=left_words, in_=turned[:].rearrange("p u j -> p j u"))
+            quantise(second, x, left[:])
+
+        def late_cast(x, tag):
+            rounded = keep.tile([P, UNIT, PACK], BF16, name=f"rounded{x}", tag=tag, align_bytes=64)
+            first_tier(nc.scalar.copy, [x], rounded)
+
+        pages[0] = keep.tile([P, T], F32, name="page0", align_bytes=64)
+        clear(0, I32)
+        q_codes[0] = (keep.tile([P, UNIT], U32, name="q0", align_bytes=64), 0)
+        q_codes[1] = (keep.tile([P, UNIT], U32, name="q1", align_bytes=64), 0)
+        rounded0 = placed([P, UNIT, PACK], BF16, "rounded0", 2 * PAGE)
+        rounded1 = placed([P, UNIT, PACK], BF16, "rounded1", 2 * PAGE + 1024)
+        cast(nc.vector.tensor_copy, rounded0[:], raw[0])
+        cast(nc.vector.tensor_copy, rounded1[:], raw[1])
+        quantise(first, 0, rounded0[:])
+        quantise(first, 1, rounded1[:])
+        back0 = dequantise(0, 0)
+        back1 = dequantise(1, 1)
+        q_codes[2] = (placed([P, UNIT], U32, "q2", 2 * PAGE), 0)
+        first_tier(nc.scalar.copy, [2], keep.tile([P, UNIT, PACK], BF16, name="rounded2", align_bytes=64))
+        back2 = dequantise(2, 2)
+        left01 = placed([P, 2 * UNIT, PACK], BF16, "left01", 3 * PAGE + 1024)
+        subtract(0, back0, left01[:, :UNIT, :])
+        subtract(1, back1, left01[:, UNIT:, :])
+        quantise(second, 0, left01[:])
+        left2 = placed([P, UNIT, PACK], BF16, "left2", 0)
+        subtract(2, back2, left2[:])
+        q_middle = placed([P, 2 * UNIT], U32, "q_middle", 3 * PAGE + 1024)
+        for x in (3, 4):
+            q_codes[x] = (q_middle, x - 3)
+        first_tier(nc.scalar.copy, [3, 4], placed([P, 2 * UNIT, PACK], BF16, "rounded34", 1024))
+        quantise(second, 2, left2[:])
+        dx = placed([P, 2 * UNIT], F32, "dx_first", 6 * PAGE - 512)
+        place(0, 0, 2, 1, dx=dx, passes=[(first, 0, 1), (first, 1, 1), (second, 0, 2)])
+        pages[1] = placed([P, T], F32, "page1", 0)
         nc.gpsimd.memset(pages[1][:], 0.0)
-        dx = shared.tile([P, PIECE], F32, name="dx_first", align_bytes=64, offset=8 * T - 512)
-        place(0, 0, [HALF, HALF], 3, [first, second], dx)
         for b in (2, 3):
-            pages[b] = shared.tile([P, T], F32, name=f"page{b}", align_bytes=64, offset=4 * T * (b - 1))
+            pages[b] = placed([P, T], F32, f"page{b}", (b + 3) * PAGE)
             nc.gpsimd.memset(pages[b][:], 0.0)
-        place(1, 0, [HALF, HALF, HALF], 6, [second, first])
-        dx = keep.tile([P, 3 * HALF], F32, name="dx_third", tag="before_late", align_bytes=64)
-        place(2, 0, [HALF, HALF, HALF], 7, [second, first], dx)
-        residual_on_tensor([3, 4], (0, 1), (2, 3), (4, 5))
-        q_codes[4] = keep.tile([P, 3 * HALF], U32, name="q_late", tag="before_late", align_bytes=64)
-        rounded = keep.tile([P, 3 * HALF, PACK], BF16, name="rounded_late", tag="pairs4", align_bytes=64)
-        first_tier(nc.scalar.copy, [5, 6], rounded[:, :PIECE, :])
-        first_tier(nc.scalar.copy, [7], rounded[:, PIECE:, :])
-        place(3, 0, [HALF, HALF, HALF], 3, [second, first])
-        place(0, PIECE, [HALF, PIECE], 6, [second, first])
-        place(1, 3 * HALF, [PIECE], 7, [second, first])
-        place(2, 3 * HALF, [PIECE], 6, [second, first])
-        residual_on_tensor([5, 6, 7], (4, 5, 4), (0, 1, 2), (3, 5, 3))
-        place(3, 3 * HALF, [PIECE], 5, [second, first])
-        for b in range(BLOCKS):
-            place(b, 5 * HALF, [PIECE, HALF], (6, 7, 0, 1)[b], [second, first])
+
+        minus3 = negate(3, 3)
+        place(1, 0, 3, 0)
+        minus4 = negate(4, 4, placed([P, PACK, UNIT], F32, "minus4", 4 * PAGE))
+        place(2, 0, 3, 2, dx=placed([P, 3 * UNIT], F32, "dx_third", PAGE + 1024))
+        q_late = placed([P, 3 * UNIT], U32, "q_late", PAGE)
+        r_late = placed([P, 5 * UNIT], U32, "r_late", PAGE + 1536)
+        for x in range(3, UNITS):
+            r_codes[x] = (r_late, x - 3)
+        for x in range(5, UNITS):
+            q_codes[x] = (q_late, x - 5)
+        pairs3 = difference(3, minus3, 1)
+        late_cast(5, "minus3")
+        turn_back(3, pairs3, 5)
+        pairs4 = difference(4, minus4, 0)
+        first_tier(nc.scalar.copy, [6], placed([P, UNIT, PACK], BF16, "rounded6", 4 * PAGE))
+        place(3, 0, 3, 5)
+        turn_back(4, pairs4, 6)
+        first_tier(nc.scalar.copy, [7], placed([P, UNIT, PACK], BF16, "rounded7", 4 * PAGE + 1024))
+        minus5 = negate(5, 0)
+        place(0, 2, 4, 6)
+        minus6 = negate(6, 3)
+        pairs5 = difference(5, minus5, 1)
+        turn_back(5, pairs5, 5)
+        place(2, 3, 5, 1)
+        pairs6 = difference(6, minus6, 0)
+        place(3, 3, 5, 5)
+        minus7 = negate(7, 3)
+        turn_back(6, pairs6, 7)
+        pairs7 = difference(7, minus7, 1)
+        place(1, 3, 6, 0)
+        turn_back(7, pairs7, 6)
+        place(0, 4, 6, 6)
+        place(1, 6, 8, 1)
+        place(0, 6, 8, 3, late_first=True)
+        place(2, 5, 8, 4, late_first=True)
+        place(3, 5, 8, 7, late_first=True)

@@ -26,7 +26,7 @@ PACK = 4
 UNIT = 128
 UNITS = J // UNIT
 PAGE = 4 * T
-CLEAR = 512
+CLEAR = 256
 
 
 def by_fours(ap, order):
@@ -93,9 +93,9 @@ def tile_list_embg_tgq8_none_kernel(tc, dy, w_words, w_scales, wgo, offs, out):
         pages = {}
         q_codes = {}
         q_plane = keep.tile([P, J], U8, name="q_plane", align_bytes=64)
-        r_early = keep.tile([P, 3 * UNIT], U32, name="r_early", align_bytes=64)
+        r_all = keep.tile([P, J], U32, name="r_all", align_bytes=64)
         r_plane = keep.tile([P, J], U8, name="r_plane", align_bytes=64)
-        r_codes = {x: (r_early, x) for x in range(3)}
+        r_codes = {x: (r_all, x) for x in range(UNITS)}
         first = (q_codes, q_plane, E5M2X4)
         second = (r_codes, r_plane, E4M3X4)
 
@@ -153,9 +153,9 @@ def tile_list_embg_tgq8_none_kernel(tc, dy, w_words, w_scales, wgo, offs, out):
                 op=SUB,
             )
 
-        def clear(b, view):
-            for lo in range(0, T, CLEAR):
-                nc.vector.memset(pages[b][:, lo : lo + CLEAR].bitcast(view), 0)
+        def clear(b, start, stop, step):
+            for lo in range(start, stop, step):
+                nc.vector.memset(pages[b][:, lo : lo + step].bitcast(I32), 0)
 
 
         def sums(b, lo, hi, number, late_first):
@@ -222,7 +222,7 @@ def tile_list_embg_tgq8_none_kernel(tc, dy, w_words, w_scales, wgo, offs, out):
             first_tier(nc.scalar.copy, [x], rounded)
 
         pages[0] = keep.tile([P, T], F32, name="page0", align_bytes=64)
-        clear(0, I32)
+        clear(0, 0, T, 2 * CLEAR)
         q_codes[0] = (keep.tile([P, UNIT], U32, name="q0", align_bytes=64), 0)
         q_codes[1] = (keep.tile([P, UNIT], U32, name="q1", align_bytes=64), 0)
         rounded0 = placed([P, UNIT, PACK], BF16, "rounded0", 2 * PAGE)
@@ -233,38 +233,33 @@ def tile_list_embg_tgq8_none_kernel(tc, dy, w_words, w_scales, wgo, offs, out):
         quantise(first, 1, rounded1[:])
         back0 = dequantise(0, 0)
         back1 = dequantise(1, 1)
-        q_codes[2] = (placed([P, UNIT], U32, "q2", 2 * PAGE), 0)
+        q_codes[2] = (placed([P, UNIT], U32, "q2", 2 * PAGE + 512), 0)
         first_tier(nc.scalar.copy, [2], keep.tile([P, UNIT, PACK], BF16, name="rounded2", align_bytes=64))
         back2 = dequantise(2, 2)
+        pages[1] = placed([P, T], F32, "page1", PAGE + 64)
+        clear(1, 0, T // 2, CLEAR)
         left01 = placed([P, 2 * UNIT, PACK], BF16, "left01", 3 * PAGE + 1024)
         subtract(0, back0, left01[:, :UNIT, :])
         subtract(1, back1, left01[:, UNIT:, :])
         quantise(second, 0, left01[:])
         left2 = placed([P, UNIT, PACK], BF16, "left2", 0)
         subtract(2, back2, left2[:])
-        q_middle = placed([P, 2 * UNIT], U32, "q_middle", 3 * PAGE + 1024)
-        for x in (3, 4):
-            q_codes[x] = (q_middle, x - 3)
+        q_late = placed([P, 5 * UNIT], U32, "q_late", 3 * PAGE + 1024)
+        for x in range(3, UNITS):
+            q_codes[x] = (q_late, x - 3)
         first_tier(nc.scalar.copy, [3, 4], placed([P, 2 * UNIT, PACK], BF16, "rounded34", 1024))
         quantise(second, 2, left2[:])
-        dx = placed([P, 2 * UNIT], F32, "dx_first", 6 * PAGE - 512)
+        clear(1, T // 2, T, CLEAR)
+        dx = placed([P, 2 * UNIT], F32, "dx_first", 5 * PAGE)
         place(0, 0, 2, 1, dx=dx, passes=[(first, 0, 1), (first, 1, 1), (second, 0, 2)])
-        pages[1] = placed([P, T], F32, "page1", 0)
-        nc.gpsimd.memset(pages[1][:], 0.0)
-        for b in (2, 3):
-            pages[b] = placed([P, T], F32, f"page{b}", (b + 3) * PAGE)
+        for b, offset in ((2, 0), (3, 5 * PAGE)):
+            pages[b] = placed([P, T], F32, f"page{b}", offset)
             nc.gpsimd.memset(pages[b][:], 0.0)
 
         minus3 = negate(3, 3)
         place(1, 0, 3, 0)
         minus4 = negate(4, 4, placed([P, PACK, UNIT], F32, "minus4", 4 * PAGE))
-        place(2, 0, 3, 2, dx=placed([P, 3 * UNIT], F32, "dx_third", PAGE + 1024))
-        q_late = placed([P, 3 * UNIT], U32, "q_late", PAGE)
-        r_late = placed([P, 5 * UNIT], U32, "r_late", PAGE + 1536)
-        for x in range(3, UNITS):
-            r_codes[x] = (r_late, x - 3)
-        for x in range(5, UNITS):
-            q_codes[x] = (q_late, x - 5)
+        place(2, 0, 3, 2)
         pairs3 = difference(3, minus3, 1)
         late_cast(5, "minus3")
         turn_back(3, pairs3, 5)

@@ -207,19 +207,13 @@ def tile_list_embg_tgq8_none_kernel(tc, dy, w_words, w_scales, wgo, offs, out):
             nc.scalar.copy(out=pairs[:], in_=diff[:].rearrange("j (u e) p -> j u p e", e=2))
             return pairs
 
-        def turn_back(x, pairs, number):
+        def turn_back(x, pairs, number, left):
             pair_words = pairs[:].rearrange("j u p e -> j (u p e)").bitcast(F32)
             turned = bank(number, [P, 2, P], f"turned{x}")
             for u in range(2):
                 nc.tensor.transpose(turned[:, u, :], pair_words[:, u * P : (u + 1) * P], eye[:])
-            left = keep.tile([P, UNIT, PACK], BF16, name=f"left{x}", align_bytes=64)
-            left_words = left[:].rearrange("p j i -> p (j i)").bitcast(F32).rearrange("p (j u) -> p j u", u=2)
+            left_words = left.rearrange("p j i -> p (j i)").bitcast(F32).rearrange("p (j u) -> p j u", u=2)
             nc.scalar.copy(out=left_words, in_=turned[:].rearrange("p u j -> p j u"))
-            quantise(second, x, left[:])
-
-        def late_cast(x, tag):
-            rounded = keep.tile([P, UNIT, PACK], BF16, name=f"rounded{x}", tag=tag, align_bytes=64)
-            first_tier(nc.scalar.copy, [x], rounded)
 
         pages[0] = keep.tile([P, T], F32, name="page0", align_bytes=64)
         clear(0, 0, T, 2 * CLEAR)
@@ -256,33 +250,38 @@ def tile_list_embg_tgq8_none_kernel(tc, dy, w_words, w_scales, wgo, offs, out):
             pages[b] = placed([P, T], F32, f"page{b}", offset)
             nc.gpsimd.memset(pages[b][:], 0.0)
 
-        minus3 = negate(3, 3)
+        minus3 = negate(3, 3, placed([P, PACK, UNIT], F32, "minus3", 4 * PAGE))
         place(1, 0, 3, 0)
-        minus4 = negate(4, 4, placed([P, PACK, UNIT], F32, "minus4", 4 * PAGE))
+        minus4 = negate(4, 4, placed([P, PACK, UNIT], F32, "minus4", 4 * PAGE + 2048))
         place(2, 0, 3, 2)
+        left34 = keep.tile([P, 2 * UNIT, PACK], BF16, name="left34", align_bytes=64)
         pairs3 = difference(3, minus3, 1)
-        late_cast(5, "minus3")
-        turn_back(3, pairs3, 5)
+        rounded56 = placed([P, 2 * UNIT, PACK], BF16, "rounded56", 4 * PAGE)
+        cast(nc.scalar.copy, rounded56[:, :UNIT, :], raw[5])
         pairs4 = difference(4, minus4, 0)
-        first_tier(nc.scalar.copy, [6], placed([P, UNIT, PACK], BF16, "rounded6", 4 * PAGE))
-        place(3, 0, 3, 5)
-        turn_back(4, pairs4, 6)
-        first_tier(nc.scalar.copy, [7], placed([P, UNIT, PACK], BF16, "rounded7", 4 * PAGE + 1024))
-        minus5 = negate(5, 0)
-        place(0, 2, 4, 6)
-        minus6 = negate(6, 3)
+        turn_back(3, pairs3, 5, left34[:, :UNIT, :])
+        cast(nc.scalar.copy, rounded56[:, UNIT:, :], raw[6])
+        quantise(first, 5, rounded56[:])
+        turn_back(4, pairs4, 6, left34[:, UNIT:, :])
+        quantise(second, 3, left34[:])
+        place(3, 0, 3, 0)
+        first_tier(nc.scalar.copy, [7], placed([P, UNIT, PACK], BF16, "rounded7", 4 * PAGE + 2048))
+        place(0, 2, 5, 5)
+        minus5 = negate(5, 6)
+        minus6 = negate(6, 0)
+        place(1, 3, 5, 2)
+        left567 = keep.tile([P, 3 * UNIT, PACK], BF16, name="left567", align_bytes=64)
         pairs5 = difference(5, minus5, 1)
-        turn_back(5, pairs5, 5)
-        place(2, 3, 5, 1)
-        pairs6 = difference(6, minus6, 0)
-        place(3, 3, 5, 5)
-        minus7 = negate(7, 3)
-        turn_back(6, pairs6, 7)
-        pairs7 = difference(7, minus7, 1)
-        place(1, 3, 6, 0)
-        turn_back(7, pairs7, 6)
-        place(0, 4, 6, 6)
-        place(1, 6, 8, 1)
-        place(0, 6, 8, 3, late_first=True)
-        place(2, 5, 8, 4, late_first=True)
-        place(3, 5, 8, 7, late_first=True)
+        minus7 = negate(7, 5)
+        place(2, 3, 5, 6)
+        pairs6 = difference(6, minus6, 3)
+        turn_back(5, pairs5, 4, left567[:, :UNIT, :])
+        pairs7 = difference(7, minus7, 0)
+        turn_back(6, pairs6, 7, left567[:, UNIT : 2 * UNIT, :])
+        turn_back(7, pairs7, 4, left567[:, 2 * UNIT :, :])
+        quantise(second, 5, left567[:])
+        place(3, 3, 5, 0)
+        place(0, 5, 8, 7)
+        place(1, 5, 8, 1, late_first=True)
+        place(2, 5, 8, 3, late_first=True)
+        place(3, 5, 8, 5, late_first=True)

@@ -238,12 +238,12 @@ def tile_list_embg_tgq8_none_kernel(tc, dy, w_words, w_scales, wgo, offs, out):
         quantise(second, 0, left01[:])
         left2 = placed([P, UNIT, PACK], BF16, "left2", 0)
         subtract(2, back2, left2[:])
+        quantise(second, 2, left2[:])
+        clear(1, T // 2, T, CLEAR)
         q_late = placed([P, 5 * UNIT], U32, "q_late", 3 * PAGE + 1024)
         for x in range(3, UNITS):
             q_codes[x] = (q_late, x - 3)
         first_tier(nc.scalar.copy, [3, 4], placed([P, 2 * UNIT, PACK], BF16, "rounded34", 1024))
-        quantise(second, 2, left2[:])
-        clear(1, T // 2, T, CLEAR)
         dx = placed([P, 2 * UNIT], F32, "dx_first", 5 * PAGE)
         place(0, 0, 2, 1, dx=dx, passes=[(first, 0, 1), (first, 1, 1), (second, 0, 2)])
         for b, offset in ((2, 0), (3, 5 * PAGE)):

@@ -266,7 +266,7 @@ def tile_list_embg_tgq8_none_kernel(tc, dy, w_words, w_scales, wgo, offs, out):
         quantise(second, 3, left34[:])
         place(3, 0, 3, 0)
         first_tier(nc.scalar.copy, [7], placed([P, UNIT, PACK], BF16, "rounded7", 4 * PAGE + 2048))
-        place(0, 2, 5, 5)
+        place(0, 2, 4, 5)
         minus5 = negate(5, 6)
         minus6 = negate(6, 0)
         place(1, 3, 5, 2)
@@ -281,7 +281,7 @@ def tile_list_embg_tgq8_none_kernel(tc, dy, w_words, w_scales, wgo, offs, out):
         turn_back(7, pairs7, 4, left567[:, 2 * UNIT :, :])
         quantise(second, 5, left567[:])
         place(3, 3, 5, 0)
-        place(0, 5, 8, 7)
-        place(1, 5, 8, 1, late_first=True)
-        place(2, 5, 8, 3, late_first=True)
-        place(3, 5, 8, 5, late_first=True)
+        place(1, 5, 8, 7)
+        place(2, 5, 8, 1, late_first=True)
+        place(3, 5, 8, 3, late_first=True)
+        place(0, 4, 8, 5, late_first=True)

@@ -17,8 +17,6 @@ MULT = mybir.AluOpType.mult
 ADD = mybir.AluOpType.add
 SUB = mybir.AluOpType.subtract
 IS_EQUAL = mybir.AluOpType.is_equal
-ABS = mybir.ActivationFunctionType.Abs
-RELU = mybir.ActivationFunctionType.Relu
 COPY = mybir.ActivationFunctionType.Copy
 
 P = 128
@@ -71,26 +69,30 @@ def tile_list_embg_tgq8_none_kernel(tc, dy, w_words, w_scales, wgo, offs, out):
         def placed(shape, dtype, name, offset):
             return shared.tile(shape, dtype, name=name, align_bytes=64, offset=offset)
 
-        ramp = keep.tile([P, P], F32, name="ramp")
+        pages = {}
+
+        def clear(b, start, stop, step):
+            for lo in range(start, stop, step):
+                nc.vector.memset(pages[b][:, lo : lo + step].bitcast(I32), 0)
+
+        ramp = placed([P, P], F32, "ramp", 6 * PAGE)
         nc.gpsimd.iota(ramp[:], [[1, P]], base=0, channel_multiplier=-1, allow_small_or_imprecise_dtypes=True)
         marks = placed([P, K], BF16, "marks", 2 * PAGE + 64)
         nc.gpsimd.memset(marks[:].bitcast(I32), 0)
         diagonal = marks[:, 0:K:PACK]
         nc.vector.tensor_scalar(out=diagonal, in0=ramp[:], scalar1=0.0, scalar2=None, op0=IS_EQUAL)
+        eye = keep.tile([P, P], F32, name="eye")
+        nc.vector.tensor_scalar(out=eye[:], in0=ramp[:], scalar1=0.0, scalar2=None, op0=IS_EQUAL)
         eye_first = keep.tile([P, P], U32, name="eye_first", align_bytes=64)
         eye_rest = keep.tile([P, (PACK - 1) * P], U32, name="eye_rest", align_bytes=64)
         eye_plane = keep.tile([P, P], U8, name="eye_plane", align_bytes=64)
         nc.vector.memset(eye_rest[:], 0)
         nc.vector.quantize_mx(out=eye_first[:].bitcast(E4M3X4), scales=eye_plane[:], in_=marks[:])
+        pages[1] = placed([P, T], F32, "page1", 6 * PAGE)
+        clear(1, 0, 2 * CLEAR, CLEAR)
         eye_codes = [eye_first[:]] + [eye_rest[:, t * P : (t + 1) * P] for t in range(PACK - 1)]
         for t in range(1, PACK):
             nc.vector.tensor_copy(out=eye_codes[t].bitcast(U8)[:, t:K:PACK], in_=eye_first[:].bitcast(U8)[:, 0:K:PACK])
-        eye = keep.tile([P, P], F32, name="eye")
-        distance = keep.tile([P, P], F32, name="distance")
-        nc.scalar.activation(out=distance[:], in_=ramp[:], func=ABS)
-        nc.scalar.activation(out=eye[:], in_=distance[:], func=RELU, scale=-1.0, bias=1.0)
-
-        pages = {}
         q_codes = {}
         q_plane = keep.tile([P, J], U8, name="q_plane", align_bytes=64)
         r_all = keep.tile([P, J], U32, name="r_all", align_bytes=64)
@@ -153,10 +155,6 @@ def tile_list_embg_tgq8_none_kernel(tc, dy, w_words, w_scales, wgo, offs, out):
                 op=SUB,
             )
 
-        def clear(b, start, stop, step):
-            for lo in range(start, stop, step):
-                nc.vector.memset(pages[b][:, lo : lo + step].bitcast(I32), 0)
-
 
         def sums(b, lo, hi, number, late_first):
             acc = bank(number, [P, (hi - lo) * UNIT], f"acc{b}_{lo}")
@@ -167,7 +165,7 @@ def tile_list_embg_tgq8_none_kernel(tc, dy, w_words, w_scales, wgo, offs, out):
                 passes = passes + [(second, x, n) for x, n in reversed(runs(r_codes, lo, hi))]
             return acc, passes
 
-        def place(b, lo, hi, number, late_first=False, dx=None, passes=None):
+        def copied_sums(b, lo, hi, number, late_first, dx, passes):
             acc, found = sums(b, lo, hi, number, late_first)
             if passes is None:
                 passes = found
@@ -181,13 +179,19 @@ def tile_list_embg_tgq8_none_kernel(tc, dy, w_words, w_scales, wgo, offs, out):
                     start=(n == 0),
                     stop=(n == len(passes) - 1),
                 )
-            if dx is None:
-                dx = keep.tile([P, (hi - lo) * UNIT], F32, name=f"dx{b}_{lo}")
-            nc.scalar.copy(out=dx[:], in_=acc[:])
+            nc.scalar.copy(out=dx, in_=acc[:])
+
+        def scatter(b, lo, hi, dx):
             window = pages[b][:].indirect(offsets[:, lo * UNIT // 16 : hi * UNIT // 16])
             nc.vector.tensor_tensor(out=window, in0=dx[:], in1=wgo_sb[:, lo * UNIT : hi * UNIT], op=MULT)
             if hi == UNITS:
                 nc.sync.dma_start(out=out[b * P : (b + 1) * P, :], in_=pages[b][:])
+
+        def place(b, lo, hi, number, late_first=False, dx=None, passes=None):
+            if dx is None:
+                dx = keep.tile([P, (hi - lo) * UNIT], F32, name=f"dx{b}_{lo}")
+            copied_sums(b, lo, hi, number, late_first, dx[:], passes)
+            scatter(b, lo, hi, dx)
 
         def negate(x, number, minus=None):
             back = dequantise(x, number)
@@ -230,22 +234,25 @@ def tile_list_embg_tgq8_none_kernel(tc, dy, w_words, w_scales, wgo, offs, out):
         q_codes[2] = (placed([P, UNIT], U32, "q2", 2 * PAGE + 512), 0)
         first_tier(nc.scalar.copy, [2], keep.tile([P, UNIT, PACK], BF16, name="rounded2", align_bytes=64))
         back2 = dequantise(2, 2)
-        pages[1] = placed([P, T], F32, "page1", PAGE + 64)
-        clear(1, 0, T // 2, CLEAR)
-        left01 = placed([P, 2 * UNIT, PACK], BF16, "left01", 3 * PAGE + 1024)
-        subtract(0, back0, left01[:, :UNIT, :])
-        subtract(1, back1, left01[:, UNIT:, :])
-        quantise(second, 0, left01[:])
+        clear(1, 2 * CLEAR, 5 * CLEAR, CLEAR)
+        left0 = keep.tile([P, UNIT, PACK], BF16, name="left0", align_bytes=64)
+        left1 = placed([P, UNIT, PACK], BF16, "left1", 3 * PAGE + 1024)
         left2 = placed([P, UNIT, PACK], BF16, "left2", 0)
+        subtract(0, back0, left0[:])
+        subtract(1, back1, left1[:])
+        quantise(second, 0, left0[:])
         subtract(2, back2, left2[:])
+        quantise(second, 1, left1[:])
         quantise(second, 2, left2[:])
-        clear(1, T // 2, T, CLEAR)
+        clear(1, 5 * CLEAR, T, CLEAR)
         q_late = placed([P, 5 * UNIT], U32, "q_late", 3 * PAGE + 1024)
         for x in range(3, UNITS):
             q_codes[x] = (q_late, x - 3)
         first_tier(nc.scalar.copy, [3, 4], placed([P, 2 * UNIT, PACK], BF16, "rounded34", 1024))
         dx = placed([P, 2 * UNIT], F32, "dx_first", 5 * PAGE)
-        place(0, 0, 2, 1, dx=dx, passes=[(first, 0, 1), (first, 1, 1), (second, 0, 2)])
+        copied_sums(0, 0, 1, 7, True, dx[:, :UNIT], None)
+        copied_sums(0, 1, 2, 1, False, dx[:, UNIT:], None)
+        scatter(0, 0, 2, dx)
         for b, offset in ((2, 0), (3, 5 * PAGE)):
             pages[b] = placed([P, T], F32, f"page{b}", offset)
             nc.gpsimd.memset(pages[b][:], 0.0)

@@ -43,8 +43,13 @@ def tile_list_embg_tgq8_none_kernel(tc, dy, w_words, w_scales, wgo, offs, out):
         w_plane = keep.tile([P, N], U8, name="w_plane", align_bytes=64)
         wgo_sb = keep.tile([P, J], F32, name="wgo_sb")
         dy_rows = dy.rearrange("(p i) j -> p i j", i=PACK)
-        loads = [(0, 2), (2, 3), (3, 5), (5, 8)]
-        loaded = [keep.tile([P, PACK, (hi - lo) * UNIT], F32, name=f"raw{lo}") for lo, hi in loads]
+        loads = [(0, 1), (1, 2), (2, 3), (3, 5), (5, 8)]
+        loaded = [
+            shared.tile([P, PACK, UNIT], F32, name="raw2", align_bytes=64, offset=3 * PAGE + 1024)
+            if lo == 2
+            else keep.tile([P, PACK, (hi - lo) * UNIT], F32, name=f"raw{lo}")
+            for lo, hi in loads
+        ]
         raw = []
         for (lo, hi), tile in zip(loads, loaded):
             raw.extend(tile[:, :, g * UNIT : (g + 1) * UNIT] for g in range(hi - lo))
@@ -53,8 +58,8 @@ def tile_list_embg_tgq8_none_kernel(tc, dy, w_words, w_scales, wgo, offs, out):
             lo, hi = loads[n]
             nc.sync.dma_start(out=loaded[n][:], in_=dy_rows[:, :, lo * UNIT : hi * UNIT])
 
-        nc.gpsimd.memset(w_plane[:].bitcast(I32), 0)
-        for n in range(3):
+        nc.vector.memset(w_plane[:].bitcast(I32), 0)
+        for n in range(4):
             load_dy(n)
         nc.sync.dma_start(out=w_codes[:].bitcast(I32), in_=w_words[0].rearrange("p n i -> p (n i)").bitcast(I32))
         for q in range(4):
@@ -63,7 +68,7 @@ def tile_list_embg_tgq8_none_kernel(tc, dy, w_words, w_scales, wgo, offs, out):
             )
         nc.sync.dma_start(offsets[:], offs)
         nc.sync.dma_start(out=wgo_sb[:, : 3 * UNIT], in_=wgo[:, : 3 * UNIT])
-        load_dy(3)
+        load_dy(4)
         nc.sync.dma_start(out=wgo_sb[:, 3 * UNIT :], in_=wgo[:, 3 * UNIT :])
 
         def placed(shape, dtype, name, offset):
@@ -75,10 +80,10 @@ def tile_list_embg_tgq8_none_kernel(tc, dy, w_words, w_scales, wgo, offs, out):
             for lo in range(start, stop, step):
                 nc.vector.memset(pages[b][:, lo : lo + step].bitcast(I32), 0)
 
-        ramp = placed([P, P], F32, "ramp", 6 * PAGE)
+        ramp = placed([P, P], F32, "ramp", 7 * PAGE - 256)
         nc.gpsimd.iota(ramp[:], [[1, P]], base=0, channel_multiplier=-1, allow_small_or_imprecise_dtypes=True)
         marks = placed([P, K], BF16, "marks", 2 * PAGE + 64)
-        nc.gpsimd.memset(marks[:].bitcast(I32), 0)
+        nc.vector.memset(marks[:].bitcast(I32), 0)
         diagonal = marks[:, 0:K:PACK]
         nc.vector.tensor_scalar(out=diagonal, in0=ramp[:], scalar1=0.0, scalar2=None, op0=IS_EQUAL)
         eye = keep.tile([P, P], F32, name="eye")
@@ -88,8 +93,9 @@ def tile_list_embg_tgq8_none_kernel(tc, dy, w_words, w_scales, wgo, offs, out):
         eye_plane = keep.tile([P, P], U8, name="eye_plane", align_bytes=64)
         nc.vector.memset(eye_rest[:], 0)
         nc.vector.quantize_mx(out=eye_first[:].bitcast(E4M3X4), scales=eye_plane[:], in_=marks[:])
-        pages[1] = placed([P, T], F32, "page1", 6 * PAGE)
-        clear(1, 0, 2 * CLEAR, CLEAR)
+        pages[0] = placed([P, T], F32, "page0", 6 * PAGE)
+        pages[1] = placed([P, T], F32, "page1", 7 * PAGE)
+        clear(0, 0, CLEAR, CLEAR)
         eye_codes = [eye_first[:]] + [eye_rest[:, t * P : (t + 1) * P] for t in range(PACK - 1)]
         for t in range(1, PACK):
             nc.vector.tensor_copy(out=eye_codes[t].bitcast(U8)[:, t:K:PACK], in_=eye_first[:].bitcast(U8)[:, 0:K:PACK])
@@ -219,38 +225,45 @@ def tile_list_embg_tgq8_none_kernel(tc, dy, w_words, w_scales, wgo, offs, out):
             left_words = left.rearrange("p j i -> p (j i)").bitcast(F32).rearrange("p (j u) -> p j u", u=2)
             nc.scalar.copy(out=left_words, in_=turned[:].rearrange("p u j -> p j u"))
 
-        pages[0] = keep.tile([P, T], F32, name="page0", align_bytes=64)
-        clear(0, 0, T, 2 * CLEAR)
+        clear(0, CLEAR, 6 * CLEAR, CLEAR)
         q_codes[0] = (keep.tile([P, UNIT], U32, name="q0", align_bytes=64), 0)
-        q_codes[1] = (keep.tile([P, UNIT], U32, name="q1", align_bytes=64), 0)
         rounded0 = placed([P, UNIT, PACK], BF16, "rounded0", 2 * PAGE)
-        rounded1 = placed([P, UNIT, PACK], BF16, "rounded1", 2 * PAGE + 1024)
         cast(nc.vector.tensor_copy, rounded0[:], raw[0])
-        cast(nc.vector.tensor_copy, rounded1[:], raw[1])
+        clear(0, 6 * CLEAR, T, CLEAR)
         quantise(first, 0, rounded0[:])
-        quantise(first, 1, rounded1[:])
         back0 = dequantise(0, 0)
+        rounded1 = placed([P, UNIT, PACK], BF16, "rounded1", 2 * PAGE + 2048)
+        rounded2 = keep.tile([P, UNIT, PACK], BF16, name="rounded2", align_bytes=64)
+        rounded34 = keep.tile([P, 2 * UNIT, PACK], BF16, name="rounded34", align_bytes=64)
+        cast(nc.scalar.copy, rounded1[:], raw[1])
+        cast(nc.scalar.copy, rounded2[:], raw[2])
+        cast(nc.scalar.copy, rounded34[:, :UNIT, :], raw[3])
+        cast(nc.scalar.copy, rounded34[:, UNIT:, :], raw[4])
+        clear(1, 0, 5 * CLEAR, CLEAR)
+        q_codes[1] = (placed([P, UNIT], U32, "q1", 2 * PAGE), 0)
+        quantise(first, 1, rounded1[:])
         back1 = dequantise(1, 1)
-        q_codes[2] = (placed([P, UNIT], U32, "q2", 2 * PAGE + 512), 0)
-        first_tier(nc.scalar.copy, [2], keep.tile([P, UNIT, PACK], BF16, name="rounded2", align_bytes=64))
-        back2 = dequantise(2, 2)
-        clear(1, 2 * CLEAR, 5 * CLEAR, CLEAR)
+        clear(1, 5 * CLEAR, 6 * CLEAR, CLEAR)
         left0 = keep.tile([P, UNIT, PACK], BF16, name="left0", align_bytes=64)
-        left1 = placed([P, UNIT, PACK], BF16, "left1", 3 * PAGE + 1024)
+        left1 = keep.tile([P, UNIT, PACK], BF16, name="left1", align_bytes=64)
         left2 = placed([P, UNIT, PACK], BF16, "left2", 0)
         subtract(0, back0, left0[:])
+        q_codes[2] = (placed([P, UNIT], U32, "q2", 2 * PAGE + 2048), 0)
+        quantise(first, 2, rounded2[:])
+        back2 = dequantise(2, 2)
         subtract(1, back1, left1[:])
         quantise(second, 0, left0[:])
-        subtract(2, back2, left2[:])
+        clear(1, 6 * CLEAR, 7 * CLEAR, CLEAR)
         quantise(second, 1, left1[:])
+        subtract(2, back2, left2[:])
+        clear(1, 7 * CLEAR, T, CLEAR)
         quantise(second, 2, left2[:])
-        clear(1, 5 * CLEAR, T, CLEAR)
         q_late = placed([P, 5 * UNIT], U32, "q_late", 3 * PAGE + 1024)
         for x in range(3, UNITS):
             q_codes[x] = (q_late, x - 3)
-        first_tier(nc.scalar.copy, [3, 4], placed([P, 2 * UNIT, PACK], BF16, "rounded34", 1024))
+        quantise(first, 3, rounded34[:])
         dx = placed([P, 2 * UNIT], F32, "dx_first", 5 * PAGE)
-        copied_sums(0, 0, 1, 7, True, dx[:, :UNIT], None)
+        copied_sums(0, 0, 1, 0, False, dx[:, :UNIT], None)
         copied_sums(0, 1, 2, 1, False, dx[:, UNIT:], None)
         scatter(0, 0, 2, dx)
         for b, offset in ((2, 0), (3, 5 * PAGE)):
@@ -258,37 +271,37 @@ def tile_list_embg_tgq8_none_kernel(tc, dy, w_words, w_scales, wgo, offs, out):
             nc.gpsimd.memset(pages[b][:], 0.0)
 
         minus3 = negate(3, 3, placed([P, PACK, UNIT], F32, "minus3", 4 * PAGE))
-        place(1, 0, 3, 0)
+        place(1, 0, 3, 7, passes=[(second, 0, 2), (first, 0, 1), (first, 1, 1), (first, 2, 1), (second, 2, 1)])
         minus4 = negate(4, 4, placed([P, PACK, UNIT], F32, "minus4", 4 * PAGE + 2048))
-        place(2, 0, 3, 2)
+        place(2, 0, 3, 2, late_first=True)
         left34 = keep.tile([P, 2 * UNIT, PACK], BF16, name="left34", align_bytes=64)
-        pairs3 = difference(3, minus3, 1)
+        pairs3 = difference(3, minus3, 0)
         rounded56 = placed([P, 2 * UNIT, PACK], BF16, "rounded56", 4 * PAGE)
         cast(nc.scalar.copy, rounded56[:, :UNIT, :], raw[5])
-        pairs4 = difference(4, minus4, 0)
+        pairs4 = difference(4, minus4, 1)
         turn_back(3, pairs3, 5, left34[:, :UNIT, :])
         cast(nc.scalar.copy, rounded56[:, UNIT:, :], raw[6])
         quantise(first, 5, rounded56[:])
         turn_back(4, pairs4, 6, left34[:, UNIT:, :])
         quantise(second, 3, left34[:])
-        place(3, 0, 3, 0)
+        place(3, 0, 3, 1)
         first_tier(nc.scalar.copy, [7], placed([P, UNIT, PACK], BF16, "rounded7", 4 * PAGE + 2048))
         place(0, 2, 4, 5)
         minus5 = negate(5, 6)
-        minus6 = negate(6, 0)
+        minus6 = negate(6, 1)
         place(1, 3, 5, 2)
         left567 = keep.tile([P, 3 * UNIT, PACK], BF16, name="left567", align_bytes=64)
-        pairs5 = difference(5, minus5, 1)
+        pairs5 = difference(5, minus5, 0)
         minus7 = negate(7, 5)
         place(2, 3, 5, 6)
-        pairs6 = difference(6, minus6, 3)
+        pairs6 = difference(6, minus6, 2)
         turn_back(5, pairs5, 4, left567[:, :UNIT, :])
-        pairs7 = difference(7, minus7, 0)
+        pairs7 = difference(7, minus7, 1)
         turn_back(6, pairs6, 7, left567[:, UNIT : 2 * UNIT, :])
         turn_back(7, pairs7, 4, left567[:, 2 * UNIT :, :])
         quantise(second, 5, left567[:])
-        place(3, 3, 5, 0)
+        place(3, 3, 5, 1)
         place(1, 5, 8, 7)
-        place(2, 5, 8, 1, late_first=True)
+        place(2, 5, 8, 0, late_first=True)
         place(3, 5, 8, 3, late_first=True)
         place(0, 4, 8, 5, late_first=True)

@@ -43,7 +43,7 @@ def tile_list_embg_tgq8_none_kernel(tc, dy, w_words, w_scales, wgo, offs, out):
         w_plane = keep.tile([P, N], U8, name="w_plane", align_bytes=64)
         wgo_sb = keep.tile([P, J], F32, name="wgo_sb")
         dy_rows = dy.rearrange("(p i) j -> p i j", i=PACK)
-        loads = [(0, 1), (1, 2), (2, 3), (3, 5), (5, 8)]
+        loads = [(0, 2), (2, 3), (3, 5), (5, 8)]
         loaded = [
             shared.tile([P, PACK, UNIT], F32, name="raw2", align_bytes=64, offset=3 * PAGE + 1024)
             if lo == 2
@@ -59,16 +59,17 @@ def tile_list_embg_tgq8_none_kernel(tc, dy, w_words, w_scales, wgo, offs, out):
             nc.sync.dma_start(out=loaded[n][:], in_=dy_rows[:, :, lo * UNIT : hi * UNIT])
 
         nc.vector.memset(w_plane[:].bitcast(I32), 0)
-        for n in range(4):
-            load_dy(n)
+        load_dy(0)
+        load_dy(1)
         nc.sync.dma_start(out=w_codes[:].bitcast(I32), in_=w_words[0].rearrange("p n i -> p (n i)").bitcast(I32))
+        load_dy(2)
         for q in range(4):
             nc.scalar.dma_start(
                 out=w_plane[32 * q : 32 * q + 4, :].bitcast(I32), in_=w_scales[0, 4 * q : 4 * q + 4, :].bitcast(I32)
             )
         nc.sync.dma_start(offsets[:], offs)
         nc.sync.dma_start(out=wgo_sb[:, : 3 * UNIT], in_=wgo[:, : 3 * UNIT])
-        load_dy(4)
+        load_dy(3)
         nc.sync.dma_start(out=wgo_sb[:, 3 * UNIT :], in_=wgo[:, 3 * UNIT :])
 
         def placed(shape, dtype, name, offset):
@@ -225,11 +226,12 @@ def tile_list_embg_tgq8_none_kernel(tc, dy, w_words, w_scales, wgo, offs, out):
             left_words = left.rearrange("p j i -> p (j i)").bitcast(F32).rearrange("p (j u) -> p j u", u=2)
             nc.scalar.copy(out=left_words, in_=turned[:].rearrange("p u j -> p j u"))
 
-        clear(0, CLEAR, 6 * CLEAR, CLEAR)
+        clear(0, CLEAR, T, CLEAR)
+        clear(1, 0, CLEAR, CLEAR)
         q_codes[0] = (keep.tile([P, UNIT], U32, name="q0", align_bytes=64), 0)
         rounded0 = placed([P, UNIT, PACK], BF16, "rounded0", 2 * PAGE)
         cast(nc.vector.tensor_copy, rounded0[:], raw[0])
-        clear(0, 6 * CLEAR, T, CLEAR)
+        clear(1, CLEAR, 2 * CLEAR, CLEAR)
         quantise(first, 0, rounded0[:])
         back0 = dequantise(0, 0)
         rounded1 = placed([P, UNIT, PACK], BF16, "rounded1", 2 * PAGE + 2048)
@@ -239,11 +241,11 @@ def tile_list_embg_tgq8_none_kernel(tc, dy, w_words, w_scales, wgo, offs, out):
         cast(nc.scalar.copy, rounded2[:], raw[2])
         cast(nc.scalar.copy, rounded34[:, :UNIT, :], raw[3])
         cast(nc.scalar.copy, rounded34[:, UNIT:, :], raw[4])
-        clear(1, 0, 5 * CLEAR, CLEAR)
+        clear(1, 2 * CLEAR, 3 * CLEAR, CLEAR)
         q_codes[1] = (placed([P, UNIT], U32, "q1", 2 * PAGE), 0)
         quantise(first, 1, rounded1[:])
         back1 = dequantise(1, 1)
-        clear(1, 5 * CLEAR, 6 * CLEAR, CLEAR)
+        clear(1, 3 * CLEAR, 6 * CLEAR, CLEAR)
         left0 = keep.tile([P, UNIT, PACK], BF16, name="left0", align_bytes=64)
         left1 = keep.tile([P, UNIT, PACK], BF16, name="left1", align_bytes=64)
         left2 = placed([P, UNIT, PACK], BF16, "left2", 0)

@@ -62,11 +62,11 @@ def tile_list_embg_tgq8_none_kernel(tc, dy, w_words, w_scales, wgo, offs, out):
         load_dy(0)
         load_dy(1)
         nc.sync.dma_start(out=w_codes[:].bitcast(I32), in_=w_words[0].rearrange("p n i -> p (n i)").bitcast(I32))
-        load_dy(2)
         for q in range(4):
-            nc.scalar.dma_start(
+            nc.sync.dma_start(
                 out=w_plane[32 * q : 32 * q + 4, :].bitcast(I32), in_=w_scales[0, 4 * q : 4 * q + 4, :].bitcast(I32)
             )
+        load_dy(2)
         nc.sync.dma_start(offsets[:], offs)
         nc.sync.dma_start(out=wgo_sb[:, : 3 * UNIT], in_=wgo[:, : 3 * UNIT])
         load_dy(3)

from contextlib import ExitStack

import concourse.mybir as mybir

K, N, T, J = 512, 512, 2048, 1024
FLOPS = 1610612736

F32 = mybir.dt.float32
BF16 = mybir.dt.bfloat16
I32 = mybir.dt.int32
U32 = mybir.dt.uint32
U16 = mybir.dt.uint16
U8 = mybir.dt.uint8
E4M3X4 = mybir.dt.float8_e4m3fn_x4
E5M2X4 = mybir.dt.float8_e5m2_x4
MULT = mybir.AluOpType.mult
ADD = mybir.AluOpType.add
SUB = mybir.AluOpType.subtract
IS_EQUAL = mybir.AluOpType.is_equal
COPY = mybir.ActivationFunctionType.Copy

P = 128
PACK = 4
UNIT = 128
UNITS = J // UNIT
PAGE = 4 * T
CLEAR = 256


def by_fours(ap, order):
    return ap.rearrange(order + " -> p c i j", j=4)


def tile_list_embg_tgq8_none_kernel(tc, dy, w_words, w_scales, wgo, offs, out):
    nc = tc.nc
    with ExitStack() as ctx:
        keep = ctx.enter_context(tc.tile_pool(name="keep", bufs=1))
        shared = ctx.enter_context(tc.tile_pool(name="shared", bufs=1))
        psum = ctx.enter_context(tc.psum_pool(name="psum", bufs=1))

        offsets = keep.tile([P, J // 16], U16, name="offsets")
        w_codes = keep.tile([P, N], U32, name="w_codes", align_bytes=64)
        w_plane = keep.tile([P, N], U8, name="w_plane", align_bytes=64)
        wgo_sb = keep.tile([P, J], F32, name="wgo_sb")
        dy_rows = dy.rearrange("(p i) j -> p i j", i=PACK)
        loads = [(0, 2), (2, 3), (3, 5), (5, 8)]
        loaded = [
            shared.tile([P, PACK, UNIT], F32, name="raw2", align_bytes=64, offset=3 * PAGE + 1024)
            if lo == 2
            else keep.tile([P, PACK, (hi - lo) * UNIT], F32, name=f"raw{lo}")
            for lo, hi in loads
        ]
        raw = []
        for (lo, hi), tile in zip(loads, loaded):
            raw.extend(tile[:, :, g * UNIT : (g + 1) * UNIT] for g in range(hi - lo))

        def load_dy(n):
            lo, hi = loads[n]
            nc.sync.dma_start(out=loaded[n][:], in_=dy_rows[:, :, lo * UNIT : hi * UNIT])

        nc.vector.memset(w_plane[:].bitcast(I32), 0)
        load_dy(0)
        load_dy(1)
        nc.sync.dma_start(out=w_codes[:].bitcast(I32), in_=w_words[0].rearrange("p n i -> p (n i)").bitcast(I32))
        for q in range(4):
            nc.sync.dma_start(
                out=w_plane[32 * q : 32 * q + 4, :].bitcast(I32), in_=w_scales[0, 4 * q : 4 * q + 4, :].bitcast(I32)
            )
        load_dy(2)
        nc.sync.dma_start(offsets[:], offs)
        nc.sync.dma_start(out=wgo_sb[:, : 3 * UNIT], in_=wgo[:, : 3 * UNIT])
        load_dy(3)
        nc.sync.dma_start(out=wgo_sb[:, 3 * UNIT :], in_=wgo[:, 3 * UNIT :])

        def placed(shape, dtype, name, offset):
            return shared.tile(shape, dtype, name=name, align_bytes=64, offset=offset)

        pages = {}

        def clear(b, start, stop, step):
            for lo in range(start, stop, step):
                nc.vector.memset(pages[b][:, lo : lo + step].bitcast(I32), 0)

        ramp = placed([P, P], F32, "ramp", 7 * PAGE - 256)
        nc.gpsimd.iota(ramp[:], [[1, P]], base=0, channel_multiplier=-1, allow_small_or_imprecise_dtypes=True)
        marks = placed([P, K], BF16, "marks", 2 * PAGE + 64)
        nc.vector.memset(marks[:].bitcast(I32), 0)
        diagonal = marks[:, 0:K:PACK]
        nc.vector.tensor_scalar(out=diagonal, in0=ramp[:], scalar1=0.0, scalar2=None, op0=IS_EQUAL)
        eye = keep.tile([P, P], F32, name="eye")
        nc.vector.tensor_scalar(out=eye[:], in0=ramp[:], scalar1=0.0, scalar2=None, op0=IS_EQUAL)
        eye_first = keep.tile([P, P], U32, name="eye_first", align_bytes=64)
        eye_rest = keep.tile([P, (PACK - 1) * P], U32, name="eye_rest", align_bytes=64)
        eye_plane = keep.tile([P, P], U8, name="eye_plane", align_bytes=64)
        nc.vector.memset(eye_rest[:], 0)
        nc.vector.quantize_mx(out=eye_first[:].bitcast(E4M3X4), scales=eye_plane[:], in_=marks[:])
        pages[0] = placed([P, T], F32, "page0", 6 * PAGE)
        pages[1] = placed([P, T], F32, "page1", 7 * PAGE)
        clear(0, 0, CLEAR, CLEAR)
        eye_codes = [eye_first[:]] + [eye_rest[:, t * P : (t + 1) * P] for t in range(PACK - 1)]
        for t in range(1, PACK):
            nc.vector.tensor_copy(out=eye_codes[t].bitcast(U8)[:, t:K:PACK], in_=eye_first[:].bitcast(U8)[:, 0:K:PACK])
        q_codes = {}
        q_plane = keep.tile([P, J], U8, name="q_plane", align_bytes=64)
        r_all = keep.tile([P, J], U32, name="r_all", align_bytes=64)
        r_plane = keep.tile([P, J], U8, name="r_plane", align_bytes=64)
        r_codes = {x: (r_all, x) for x in range(UNITS)}
        first = (q_codes, q_plane, E5M2X4)
        second = (r_codes, r_plane, E4M3X4)

        def words(codes, x, count):
            tile, place_in_tile = codes[x]
            return tile[:, place_in_tile * UNIT : (place_in_tile + count) * UNIT]

        def runs(codes, lo, hi):
            found = []
            while hi > lo:
                count = 2 if hi - lo >= 2 and codes[hi - 2][0] is codes[hi - 1][0] else 1
                found.append((hi - count, count))
                hi = hi - count
            return found

        def bank(number, shape, name):
            return psum.tile(shape, F32, name=name, tag=f"bank{number}")

        def cast(copy, dst, src):
            copy(out=by_fours(dst, "p (c j) i"), in_=by_fours(src, "p i (c j)"))

        def quantise(tier, x, values):
            codes, plane, fmt = tier
            count = values.shape[1] // UNIT
            nc.vector.quantize_mx(
                out=words(codes, x, count).bitcast(fmt),
                scales=plane[:, x * UNIT : (x + count) * UNIT],
                in_=values.rearrange("p j i -> p (j i)"),
            )

        def first_tier(copy, units, rounded):
            for g, x in enumerate(units):
                cast(copy, rounded[:, g * UNIT : (g + 1) * UNIT, :], raw[x])
            quantise(first, units[0], rounded[:])

        def dequantise(x, number):
            back = bank(number, [P, PACK, UNIT], f"back{x}")
            for t in range(PACK):
                nc.tensor.matmul_mx(
                    out=back[:, t, :],
                    lhsT=eye_codes[t].bitcast(E4M3X4),
                    lhsT_scale=eye_plane[:],
                    rhs=words(q_codes, x, 1).bitcast(E5M2X4),
                    rhs_scale=q_plane[:, x * UNIT : (x + 1) * UNIT],
                    start=True,
                    stop=True,
                )
            return back

        def subtract(x, back, left):
            nc.vector.tensor_tensor(
                out=by_fours(left, "p (c j) i"),
                in0=by_fours(raw[x], "p i (c j)"),
                in1=by_fours(back[:], "p i (c j)"),
                op=SUB,
            )


        def sums(b, lo, hi, number, late_first):
            acc = bank(number, [P, (hi - lo) * UNIT], f"acc{b}_{lo}")
            if late_first:
                passes = [(tier, x, n) for tier in (second, first) for x, n in runs(tier[0], lo, hi)]
            else:
                passes = [(first, x, n) for x, n in reversed(runs(q_codes, lo, hi))]
                passes = passes + [(second, x, n) for x, n in reversed(runs(r_codes, lo, hi))]
            return acc, passes

        def copied_sums(b, lo, hi, number, late_first, dx, passes):
            acc, found = sums(b, lo, hi, number, late_first)
            if passes is None:
                passes = found
            for n, ((codes, plane, fmt), x, count) in enumerate(passes):
                nc.tensor.matmul_mx(
                    out=acc[:, (x - lo) * UNIT : (x - lo + count) * UNIT],
                    lhsT=w_codes[:, b * P : (b + 1) * P].bitcast(E4M3X4),
                    lhsT_scale=w_plane[:, b * P : (b + 1) * P],
                    rhs=words(codes, x, count).bitcast(fmt),
                    rhs_scale=plane[:, x * UNIT : (x + count) * UNIT],
                    start=(n == 0),
                    stop=(n == len(passes) - 1),
                )
            nc.scalar.copy(out=dx, in_=acc[:])

        def scatter(b, lo, hi, dx):
            window = pages[b][:].indirect(offsets[:, lo * UNIT // 16 : hi * UNIT // 16])
            nc.vector.tensor_tensor(out=window, in0=dx[:], in1=wgo_sb[:, lo * UNIT : hi * UNIT], op=MULT)
            if hi == UNITS:
                nc.sync.dma_start(out=out[b * P : (b + 1) * P, :], in_=pages[b][:])

        def place(b, lo, hi, number, late_first=False, dx=None, passes=None):
            if dx is None:
                dx = keep.tile([P, (hi - lo) * UNIT], F32, name=f"dx{b}_{lo}")
            copied_sums(b, lo, hi, number, late_first, dx[:], passes)
            scatter(b, lo, hi, dx)

        def negate(x, number, minus=None):
            back = dequantise(x, number)
            if minus is None:
                minus = keep.tile([P, PACK, UNIT], F32, name=f"minus{x}", tag=f"minus{x}", align_bytes=64)
            nc.scalar.activation(out=minus[:], in_=back[:], func=COPY, scale=-1.0)
            return minus

        def difference(x, minus, number):
            diff = bank(number, [P, PACK, P], f"diff{x}")
            terms = [raw[x][:, t, :] for t in range(PACK)] + [minus[:, t, :] for t in range(PACK)]
            for n, term in enumerate(terms):
                nc.tensor.matmul(
                    diff[:, n % PACK, :], term, eye[:], start=(n == 0), stop=(n == len(terms) - 1), is_transpose=True
                )
            pairs = keep.tile([P, 2, P, 2], BF16, name=f"pairs{x}", align_bytes=64)
            nc.scalar.copy(out=pairs[:], in_=diff[:].rearrange("j (u e) p -> j u p e", e=2))
            return pairs

        def turn_back(x, pairs, number, left):
            pair_words = pairs[:].rearrange("j u p e -> j (u p e)").bitcast(F32)
            turned = bank(number, [P, 2, P], f"turned{x}")
            for u in range(2):
                nc.tensor.transpose(turned[:, u, :], pair_words[:, u * P : (u + 1) * P], eye[:])
            left_words = left.rearrange("p j i -> p (j i)").bitcast(F32).rearrange("p (j u) -> p j u", u=2)
            nc.scalar.copy(out=left_words, in_=turned[:].rearrange("p u j -> p j u"))

        clear(0, CLEAR, T, CLEAR)
        clear(1, 0, CLEAR, CLEAR)
        q_codes[0] = (keep.tile([P, UNIT], U32, name="q0", align_bytes=64), 0)
        rounded0 = placed([P, UNIT, PACK], BF16, "rounded0", 2 * PAGE)
        cast(nc.vector.tensor_copy, rounded0[:], raw[0])
        clear(1, CLEAR, 2 * CLEAR, CLEAR)
        quantise(first, 0, rounded0[:])
        back0 = dequantise(0, 0)
        rounded1 = placed([P, UNIT, PACK], BF16, "rounded1", 2 * PAGE + 2048)
        rounded2 = keep.tile([P, UNIT, PACK], BF16, name="rounded2", align_bytes=64)
        rounded34 = keep.tile([P, 2 * UNIT, PACK], BF16, name="rounded34", align_bytes=64)
        cast(nc.scalar.copy, rounded1[:], raw[1])
        cast(nc.scalar.copy, rounded2[:], raw[2])
        cast(nc.scalar.copy, rounded34[:, :UNIT, :], raw[3])
        cast(nc.scalar.copy, rounded34[:, UNIT:, :], raw[4])
        clear(1, 2 * CLEAR, 3 * CLEAR, CLEAR)
        q_codes[1] = (placed([P, UNIT], U32, "q1", 2 * PAGE), 0)
        quantise(first, 1, rounded1[:])
        back1 = dequantise(1, 1)
        clear(1, 3 * CLEAR, 6 * CLEAR, CLEAR)
        left0 = keep.tile([P, UNIT, PACK], BF16, name="left0", align_bytes=64)
        left1 = keep.tile([P, UNIT, PACK], BF16, name="left1", align_bytes=64)
        left2 = placed([P, UNIT, PACK], BF16, "left2", 0)
        subtract(0, back0, left0[:])
        q_codes[2] = (placed([P, UNIT], U32, "q2", 2 * PAGE + 2048), 0)
        quantise(first, 2, rounded2[:])
        back2 = dequantise(2, 2)
        subtract(1, back1, left1[:])
        quantise(second, 0, left0[:])
        clear(1, 6 * CLEAR, 7 * CLEAR, CLEAR)
        quantise(second, 1, left1[:])
        subtract(2, back2, left2[:])
        clear(1, 7 * CLEAR, T, CLEAR)
        quantise(second, 2, left2[:])
        q_late = placed([P, 5 * UNIT], U32, "q_late", 3 * PAGE + 1024)
        for x in range(3, UNITS):
            q_codes[x] = (q_late, x - 3)
        quantise(first, 3, rounded34[:])
        dx = placed([P, 2 * UNIT], F32, "dx_first", 5 * PAGE)
        copied_sums(0, 0, 1, 0, False, dx[:, :UNIT], None)
        copied_sums(0, 1, 2, 1, False, dx[:, UNIT:], None)
        scatter(0, 0, 2, dx)
        for b, offset in ((2, 0), (3, 5 * PAGE)):
            pages[b] = placed([P, T], F32, f"page{b}", offset)
            nc.gpsimd.memset(pages[b][:], 0.0)

        minus3 = negate(3, 3, placed([P, PACK, UNIT], F32, "minus3", 4 * PAGE))
        place(1, 0, 3, 7, passes=[(second, 0, 2), (first, 0, 1), (first, 1, 1), (first, 2, 1), (second, 2, 1)])
        minus4 = negate(4, 4, placed([P, PACK, UNIT], F32, "minus4", 4 * PAGE + 2048))
        place(2, 0, 3, 2, late_first=True)
        left34 = keep.tile([P, 2 * UNIT, PACK], BF16, name="left34", align_bytes=64)
        pairs3 = difference(3, minus3, 0)
        rounded56 = placed([P, 2 * UNIT, PACK], BF16, "rounded56", 4 * PAGE)
        cast(nc.scalar.copy, rounded56[:, :UNIT, :], raw[5])
        pairs4 = difference(4, minus4, 1)
        turn_back(3, pairs3, 5, left34[:, :UNIT, :])
        cast(nc.scalar.copy, rounded56[:, UNIT:, :], raw[6])
        quantise(first, 5, rounded56[:])
        turn_back(4, pairs4, 6, left34[:, UNIT:, :])
        quantise(second, 3, left34[:])
        place(3, 0, 3, 1)
        first_tier(nc.scalar.copy, [7], placed([P, UNIT, PACK], BF16, "rounded7", 4 * PAGE + 2048))
        place(0, 2, 4, 5)
        minus5 = negate(5, 6)
        minus6 = negate(6, 1)
        place(1, 3, 5, 2)
        left567 = keep.tile([P, 3 * UNIT, PACK], BF16, name="left567", align_bytes=64)
        pairs5 = difference(5, minus5, 0)
        minus7 = negate(7, 5)
        place(2, 3, 5, 6)
        pairs6 = difference(6, minus6, 2)
        turn_back(5, pairs5, 4, left567[:, :UNIT, :])
        pairs7 = difference(7, minus7, 1)
        turn_back(6, pairs6, 7, left567[:, UNIT : 2 * UNIT, :])
        turn_back(7, pairs7, 4, left567[:, 2 * UNIT :, :])
        quantise(second, 5, left567[:])
        place(3, 3, 5, 1)
        place(1, 5, 8, 7)
        place(2, 5, 8, 0, late_first=True)
        place(3, 5, 8, 3, late_first=True)
        place(0, 4, 8, 5, late_first=True)
